import numpy as np
import ml_dtypes


def mxq(x, axis, fmt="e4m3"):
    dtype, down = {"e4m3": (ml_dtypes.float8_e4m3fn, 7), "e5m2": (ml_dtypes.float8_e5m2, 14)}[fmt]
    v = np.moveaxis(np.asarray(x, np.float32).astype(ml_dtypes.bfloat16).astype(np.float64), axis, -1)
    blocks = v.reshape(v.shape[:-1] + (-1, 32))
    amax = np.abs(blocks).max(-1, keepdims=True)
    byte = np.maximum(np.where(amax > 0, np.frexp(amax)[1] - 1 + 127, 0) - down, 1)
    scale = np.exp2(byte - 127.0)
    codes = (blocks / scale).astype(np.float32).astype(dtype).astype(np.float64)
    return np.moveaxis((codes * scale).reshape(v.shape), -1, axis)


WIDE = False


def mx_kscale(k):
    if not WIDE:
        return np.ones(k)
    levels = np.array([18, -18])
    if k % 512:
        return np.exp2(np.random.permutation(np.resize(levels, k // 32))).repeat(32)
    a = np.empty((k // 512, 16))
    for p in range(k // 512):
        a[p, :8] = np.random.permutation(np.resize(levels, 8))
        for g in range(8):
            far = levels[np.abs(levels - a[p, g]) >= 10]
            a[p, g + 8] = far[np.random.randint(len(far))]
    return np.exp2(a.ravel()).repeat(32)


def f64(x):
    return np.asarray(x).astype(np.float64)


def striped(idx):
    return np.tile(np.asarray(idx).reshape(-1, 16).T, (8, 1)).astype(np.uint16)


def unstriped(offs):
    return offs[:16].T.reshape(-1).astype(np.int64)


def setup_inputs():
    n = np.random.standard_normal
    uni = np.random.uniform
    idx = np.random.permutation(2048)[:512]
    soft1 = np.exp(0.4 * n((512, 512)))
    soft2 = np.exp(0.4 * n((512, 512)))
    f_d = mx_kscale(512)
    f_r = mx_kscale(512)
    return {
        "x1": (0.35 * n((512, 512)) * f_d[:, None] * f_r[None, :]).astype(np.float32),
        "x2": (0.35 * n((512, 512)) * f_d[:, None] * f_r[None, :]).astype(np.float32),
        "wT": (n((512, 2048)) / np.sqrt(512) / f_d[:, None]).astype(np.float32),
        "y1": (soft1 / soft1.sum(-1, keepdims=True)).astype(np.float32),
        "u1": (uni(0.75, 1.3, (512, 1)) / f_r[:, None]).astype(np.float32),
        "w1": (uni(0.75, 1.3, (512, 1)) / np.sqrt(512)).astype(np.float32),
        "y2": (soft2 / soft2.sum(-1, keepdims=True)).astype(np.float32),
        "u2": (uni(0.75, 1.3, (512, 1)) / f_r[:, None]).astype(np.float32),
        "w2": (uni(0.75, 1.3, (512, 1)) / np.sqrt(512)).astype(np.float32),
        "ts": np.tile(uni(0.75, 1.3, 2048), (128, 1)).astype(np.float32),
        "offs": striped(idx),
    }


def reference(x1, x2, wT, y1, u1, w1, y2, u2, w2, ts, offs):
    idx = unstriped(offs)
    wT_i = f64(wT)[:, idx]
    ts_i = f64(ts)[:1][:, idx]
    q_wT_i = mxq(wT_i, 0, "e4m3")
    a1 = mxq(f64(x1), 0, "e4m3").T @ q_wT_i
    z1 = f64(u1) * ts_i * a1
    m1 = (z1).max(-1, keepdims=True)
    e1 = np.exp(z1 - m1)
    t1 = (e1).sum(-1, keepdims=True)
    g1 = f64(w1) * f64(u1) * ts_i * (e1 / t1 - f64(y1))
    a2 = mxq(f64(x2), 0, "e4m3").T @ q_wT_i
    z2 = f64(u2) * ts_i * a2
    m2 = (z2).max(-1, keepdims=True)
    e2 = np.exp(z2 - m2)
    t2 = (e2).sum(-1, keepdims=True)
    g2 = f64(w2) * f64(u2) * ts_i * (e2 / t2 - f64(y2))
    d1 = mxq(f64(x1), 1, "e4m3") @ mxq(g1, 0, "e5m2")
    d2 = mxq(f64(x2), 1, "e4m3") @ mxq(g2, 0, "e5m2")
    dw = d1 + d2
    out = np.zeros((512, 2048))
    out[:, idx] = dw
    return out

@@ -1,0 +1,211 @@
+from contextlib import ExitStack
+
+import concourse.mybir as mybir
+from concourse.masks import make_identity
+
+F32 = mybir.dt.float32
+BF16 = mybir.dt.bfloat16
+U32 = mybir.dt.uint32
+U16 = mybir.dt.uint16
+U8 = mybir.dt.uint8
+E4M3 = mybir.dt.float8_e4m3fn_x4
+E5M2 = mybir.dt.float8_e5m2_x4
+ALU = mybir.AluOpType
+ACT = mybir.ActivationFunctionType
+AX = mybir.AxisListType
+
+P = 128
+PACK = 4
+D = 512
+R = 512
+S = 512
+T = 2048
+FLOPS = 4 * 2 * 512 * 512 * 512
+TURNED = (False, True)
+WINDOWS = 3
+
+
+def tile_attend_gheads_sm_kernel(tc, x1, x2, wT, y1, u1, w1, y2, u2, w2, ts, offs, out):
+    nc = tc.nc
+    xs, ys, us, ws = (x1, x2), (y1, y2), (u1, u2), (w1, w2)
+    heads = (0, 1)
+    with ExitStack() as ctx:
+        keep = ctx.enter_context(tc.tile_pool(name="keep", bufs=1))
+        psum = ctx.enter_context(tc.psum_pool(name="psum", bufs=1))
+
+        def bank(b, name):
+            return psum.tile([P, 512], F32, name=name, tag="bank%d" % b)
+
+        offsets = keep.tile([P, S // 16], U16, name="offsets")
+        x_raw = [keep.tile([P, PACK, R], F32, name="x_raw%d" % h) for h in heads]
+        w_plane = [keep.tile([P, T], F32, name="w_plane%d" % j) for j in range(PACK)]
+        y_raw = [keep.tile([P, PACK, S], F32, name="y_raw%d" % h) for h in heads]
+        w_view = wT.rearrange("(p j) n -> j p n", j=PACK)
+        ts_win = keep.tile([P, T], F32, name="ts_win")
+        nc.vector.memset(ts_win[:].bitcast(U32), 0)
+        nc.sync.dma_start(x_raw[0][:], xs[0].rearrange("(p j) r -> p j r", j=PACK))
+        nc.sync.dma_start(offsets[:], offs)
+        nc.sync.dma_start(ts_win[0:1, :], ts[0:1, :])
+        for j in range(PACK):
+            nc.sync.dma_start(w_plane[j][:], w_view[j])
+        nc.sync.dma_start(x_raw[1][:], xs[1].rearrange("(p j) r -> p j r", j=PACK))
+        for h in heads:
+            nc.sync.dma_start(y_raw[h][:], ys[h].rearrange("(p t) i -> p t i", t=PACK))
+
+        ident = keep.tile([P, P], F32, name="ident")
+        make_identity(nc, ident[:])
+        u_col = [keep.tile([P, PACK], F32, name="u_col%d" % h) for h in heads]
+        w_col = [keep.tile([P, PACK], F32, name="w_col%d" % h) for h in heads]
+        neg_u = [keep.tile([P, PACK], F32, name="neg_u%d" % h) for h in heads]
+        wu = [keep.tile([P, PACK], F32, name="wu%d" % h) for h in heads]
+        for h in heads:
+            nc.scalar.dma_start(u_col[h][:], us[h].rearrange("(p t) o -> p (t o)", t=PACK))
+            nc.scalar.dma_start(w_col[h][:], ws[h].rearrange("(p t) o -> p (t o)", t=PACK))
+        for h in heads:
+            nc.gpsimd.tensor_scalar(neg_u[h][:], u_col[h][:], -1.0, 0.0, ALU.mult, ALU.add)
+            nc.gpsimd.tensor_tensor(wu[h][:], u_col[h][:], w_col[h][:], ALU.mult)
+
+        warm = keep.tile([P, 1], F32, name="warm")
+        nc.scalar.activation(warm[:], ident[:, 0:1], ACT.Exp)
+        windows = [keep.tile([P, T], F32, name="window%d" % k) for k in range(WINDOWS)]
+        for k in range(WINDOWS):
+            nc.vector.memset(windows[k][:].bitcast(U32), 0)
+
+        def codes(name):
+            c = keep.tile([P, 512], U32, name=name + "_c", align_bytes=64)
+            s = keep.tile([P, 512], U8, name=name + "_s", align_bytes=64)
+            return c, s
+
+        def quantise(q, src, fmt, lo=0, hi=512):
+            nc.vector.quantize_mx(out=q[0][:, lo:hi].bitcast(fmt), scales=q[1][:, lo:hi], in_=src[:, PACK * lo : PACK * hi])
+
+        def mm(acc, lhs, lo, lfmt, rhs, rfmt, start, stop):
+            nc.tensor.matmul_mx(out=acc, lhsT=lhs[0][:, lo : lo + P].bitcast(lfmt), lhsT_scale=lhs[1][:, lo : lo + P],
+                                rhs=rhs[0][:].bitcast(rfmt), rhs_scale=rhs[1][:], start=start, stop=stop)
+
+        x_d = [keep.tile([P, R * PACK], BF16, name="x_d%d" % h, align_bytes=64) for h in heads]
+        x_r = [keep.tile([P, D * PACK], BF16, name="x_r%d" % h, align_bytes=64) for h in heads]
+        qx_d = [codes("qx_d%d" % h) for h in heads]
+        qx_r = [codes("qx_r%d" % h) for h in heads]
+        qg = [codes("qg%d" % h) for h in heads]
+        qw = codes("qw")
+
+        def deal_x(h, copy):
+            copy(x_d[h][:].rearrange("p (t s j) -> p s t j", t=PACK, j=PACK), x_raw[h][:].rearrange("p j (s t) -> p s t j", t=PACK))
+
+        def turn_x(h, banks):
+            words = x_d[h][:].bitcast(F32)
+            for u in range(2):
+                bk = bank(banks[u], "xw%d%d" % (h, u))
+                for t in range(PACK):
+                    nc.tensor.transpose(bk[:, t * P : (t + 1) * P], words[:, 256 * t + u : 256 * (t + 1) : 2], ident[:])
+                nc.scalar.copy(
+                    x_r[h][:, u * 1024 : (u + 1) * 1024].rearrange("s (e p t) -> s e p t", e=2, t=PACK),
+                    bk[:].bitcast(BF16).rearrange("s (t p e) -> s e p t", t=PACK, e=2),
+                )
+
+        ts_row = keep.tile([P, S], F32, name="ts_row")
+        nc.vector.tensor_copy(ts_row[:], ts_win[:].indirect(offsets[:]))
+        deal_x(0, nc.scalar.copy)
+        bk = bank(0, "ts_turned")
+        for c in range(4):
+            nc.tensor.transpose(bk[:, c * P : (c + 1) * P], ts_row[:, c * P : (c + 1) * P], ident[:])
+        ts_col = keep.tile([P, 4], F32, name="ts_col")
+        nc.scalar.copy(ts_col[:], bk[:, 0:512:P])
+        bk = bank(1, "ts_spread")
+        for c in range(4):
+            nc.tensor.transpose(bk[:, c * P : (c + 1) * P], ts_col[:, c : c + 1].to_broadcast([P, P]), ident[:])
+        ts_all = keep.tile([P, S], F32, name="ts_all")
+        nc.scalar.copy(ts_all[:], bk[:])
+
+        w_d = keep.tile([P, S, PACK], BF16, name="w_d", align_bytes=64)
+        w_flat = w_d[:].rearrange("p i j -> p (i j)")
+        nc.vector.tensor_copy(w_d[:, :, 0], w_plane[0][:].indirect(offsets[:]))
+        quantise(qx_d[0], x_d[0], E4M3)
+        turn_x(0, (2, 3))
+        factor = [keep.tile([P, PACK, S], F32, name="factor%d" % h) for h in heads]
+        for h in heads:
+            for t in range(PACK):
+                nc.scalar.activation(factor[h][:, t, :], ts_all[:], ACT.Copy, scale=wu[h][:, t : t + 1])
+        nc.vector.tensor_copy(w_d[:, :, 1], w_plane[1][:].indirect(offsets[:]))
+        quantise(qx_r[0], x_r[0], E4M3)
+        nc.vector.tensor_copy(w_d[:, :, 2], w_plane[2][:].indirect(offsets[:]))
+        for half in range(2):
+            nc.vector.tensor_copy(w_d[:, half * 256 : (half + 1) * 256, 3], w_plane[3][:].indirect(offsets[:, half * 16 : (half + 1) * 16]))
+            quantise(qw, w_flat, E4M3, half * 256, (half + 1) * 256)
+
+        work = [keep.tile([P, PACK, S], F32, name="work%d" % h) for h in heads]
+        neg_m = [keep.tile([P, PACK], F32, name="neg_m%d" % h) for h in heads]
+        total = [keep.tile([P, PACK], F32, name="total%d" % h) for h in heads]
+        inv = [keep.tile([P, PACK], F32, name="inv%d" % h) for h in heads]
+        g = [keep.tile([P, S * PACK], BF16, name="g%d" % h, align_bytes=64) for h in heads]
+        turned = keep.tile([P, 4, R], F32, name="turned")
+
+        def expo(h, t):
+            nc.scalar.activation(work[h][:, t, :], work[h][:, t, :], ACT.Exp, bias=neg_m[h][:, t : t + 1], scale=-1.0,
+                                 accum_out=total[h][:, t : t + 1])
+
+        def scores_direct(h, banks):
+            acc = []
+            for t in range(PACK):
+                bk = bank(banks[t], "a%d%d" % (h, t))
+                mm(bk[:], qx_d[h], t * P, E4M3, qw, E4M3, True, True)
+                acc.append(bk)
+            for t in range(PACK + 1):
+                if t < PACK:
+                    nc.vector.scalar_tensor_tensor(work[h][:, t, :], acc[t][:], neg_u[h][:, t : t + 1], ts_all[:], ALU.mult, ALU.mult)
+                if t > 0:
+                    nc.vector.tensor_reduce(neg_m[h][:, t - 1 : t], work[h][:, t - 1, :], AX.X, ALU.min)
+                    expo(h, t - 1)
+
+        def scores_turned(h, banks_a, banks_s):
+            for c in range(4):
+                bk = bank(banks_a[c], "aT%d%d" % (h, c))
+                mm(bk[:], qw, c * P, E4M3, qx_d[h], E4M3, True, True)
+                nc.scalar.activation(turned[:, c, :], bk[:], ACT.Copy, scale=ts_col[:, c : c + 1])
+            sb = [bank(banks_s[t], "s%d%d" % (h, t)) for t in range(PACK)]
+            order = [(c, t) for c in range(4) for t in range(PACK)] if banks_a != banks_s else [(c, t) for t in range(PACK) for c in range(4)]
+            for c, t in order:
+                nc.tensor.transpose(sb[t][:, c * P : (c + 1) * P], turned[:, c, t * P : (t + 1) * P], ident[:])
+            return sb
+
+        def max_turned(h, sb):
+            for t in range(PACK):
+                nc.vector.tensor_scalar(work[h][:, t, :], sb[t][:], neg_u[h][:, t : t + 1], None, ALU.mult, ALU.min,
+                                        accum_out=neg_m[h][:, t : t + 1])
+                expo(h, t)
+
+        def gradient(h):
+            nc.vector.reciprocal(inv[h][:], total[h][:])
+            for t in range(PACK):
+                nc.vector.scalar_tensor_tensor(work[h][:, t, :], work[h][:, t, :], inv[h][:, t : t + 1], y_raw[h][:, t, :], ALU.mult, ALU.subtract)
+            nc.vector.tensor_tensor(
+                g[h][:].rearrange("p (c i t) -> p c t i", i=4, t=PACK),
+                work[h][:].rearrange("p t (c i) -> p c t i", i=4),
+                factor[h][:].rearrange("p t (c i) -> p c t i", i=4),
+                ALU.mult,
+            )
+
+        deal_x(1, nc.scalar.copy)
+        scores_direct(0, (0, 1, 2, 3))
+        quantise(qx_d[1], x_d[1], E4M3)
+        sb = scores_turned(1, (4, 5, 6, 7), (4, 5, 6, 7))
+        turn_x(1, (0, 1))
+        gradient(0)
+        max_turned(1, sb)
+        quantise(qg[0], g[0], E5M2)
+        quantise(qx_r[1], x_r[1], E4M3)
+        acc = [bank(j, "dw%d" % j) for j in range(PACK)]
+        for j in range(PACK):
+            mm(acc[j][:], qx_r[0], j * P, E4M3, qg[0], E5M2, True, False)
+        gradient(1)
+        quantise(qg[1], g[1], E5M2)
+
+        dw = [keep.tile([P, S], F32, name="dw%d" % j) for j in range(PACK)]
+        out_view = out.rearrange("(p j) n -> j p n", j=PACK)
+        for j in range(PACK):
+            mm(acc[j][:], qx_r[1], j * P, E4M3, qg[1], E5M2, False, True)
+            nc.scalar.copy(dw[j][:], acc[j][:])
+            win = windows[j % WINDOWS]
+            nc.vector.tensor_copy(win[:].indirect(offsets[:]), dw[j][:])
+            nc.sync.dma_start(out_view[j], win[:])

@@ -37,7 +37,7 @@ def tile_attend_gheads_sm_kernel(tc, x1, x2, wT, y1, u1, w1, y2, u2, w2, ts, off
             return psum.tile([P, 512], F32, name=name, tag="bank%d" % b)
 
         offsets = keep.tile([P, S // 16], U16, name="offsets")
-        x_raw = [keep.tile([P, PACK, R], F32, name="x_raw%d" % h) for h in heads]
+        x_raw = [keep.tile([P, PACK, R], F32, name="x_raw%d" % h, align_bytes=64) for h in heads]
         w_plane = [keep.tile([P, T], F32, name="w_plane%d" % j) for j in range(PACK)]
         y_raw = [keep.tile([P, PACK, S], F32, name="y_raw%d" % h) for h in heads]
         w_view = wT.rearrange("(p j) n -> j p n", j=PACK)
@@ -67,9 +67,8 @@ def tile_attend_gheads_sm_kernel(tc, x1, x2, wT, y1, u1, w1, y2, u2, w2, ts, off
 
         warm = keep.tile([P, 1], F32, name="warm")
         nc.scalar.activation(warm[:], ident[:, 0:1], ACT.Exp)
-        windows = [keep.tile([P, T], F32, name="window%d" % k) for k in range(WINDOWS)]
-        for k in range(WINDOWS):
-            nc.vector.memset(windows[k][:].bitcast(U32), 0)
+        window2 = keep.tile([P, T], F32, name="window2")
+        nc.vector.memset(window2[:], 0.0)
 
         def codes(name):
             c = keep.tile([P, 512], U32, name=name + "_c", align_bytes=64)
@@ -123,37 +122,40 @@ def tile_attend_gheads_sm_kernel(tc, x1, x2, wT, y1, u1, w1, y2, u2, w2, ts, off
         nc.vector.tensor_copy(w_d[:, :, 0], w_plane[0][:].indirect(offsets[:]))
         quantise(qx_d[0], x_d[0], E4M3)
         turn_x(0, (2, 3))
-        factor = [keep.tile([P, PACK, S], F32, name="factor%d" % h) for h in heads]
-        for h in heads:
-            for t in range(PACK):
-                nc.scalar.activation(factor[h][:, t, :], ts_all[:], ACT.Copy, scale=wu[h][:, t : t + 1])
         nc.vector.tensor_copy(w_d[:, :, 1], w_plane[1][:].indirect(offsets[:]))
         quantise(qx_r[0], x_r[0], E4M3)
         nc.vector.tensor_copy(w_d[:, :, 2], w_plane[2][:].indirect(offsets[:]))
+        acc1 = []
         for half in range(2):
             nc.vector.tensor_copy(w_d[:, half * 256 : (half + 1) * 256, 3], w_plane[3][:].indirect(offsets[:, half * 16 : (half + 1) * 16]))
             quantise(qw, w_flat, E4M3, half * 256, (half + 1) * 256)
+            for t in range(PACK):
+                if t % 2 == 0:
+                    acc1.append(bank(2 * half + t // 2, "a1_%d%d" % (half, t)))
+                nc.tensor.matmul_mx(out=acc1[-1][:, (t % 2) * 256 : (t % 2 + 1) * 256], lhsT=qx_d[0][0][:, t * P : (t + 1) * P].bitcast(E4M3),
+                                    lhsT_scale=qx_d[0][1][:, t * P : (t + 1) * P], rhs=qw[0][:, half * 256 : (half + 1) * 256].bitcast(E4M3),
+                                    rhs_scale=qw[1][:, half * 256 : (half + 1) * 256], start=True, stop=True)
 
         work = [keep.tile([P, PACK, S], F32, name="work%d" % h) for h in heads]
         neg_m = [keep.tile([P, PACK], F32, name="neg_m%d" % h) for h in heads]
         total = [keep.tile([P, PACK], F32, name="total%d" % h) for h in heads]
         inv = [keep.tile([P, PACK], F32, name="inv%d" % h) for h in heads]
         g = [keep.tile([P, S * PACK], BF16, name="g%d" % h, align_bytes=64) for h in heads]
+        planes = [None, keep.tile([P, PACK, S], BF16, name="planes1", align_bytes=64)]
+        g_t = [keep.tile([P, R], BF16, name="g_t%d" % c, align_bytes=64) for c in range(4)]
+        cinv = keep.tile([P, PACK], F32, name="cinv")
         turned = keep.tile([P, 4, R], F32, name="turned")
 
         def expo(h, t):
             nc.scalar.activation(work[h][:, t, :], work[h][:, t, :], ACT.Exp, bias=neg_m[h][:, t : t + 1], scale=-1.0,
                                  accum_out=total[h][:, t : t + 1])
 
-        def scores_direct(h, banks):
-            acc = []
+        def scores_direct(h, acc):
             for t in range(PACK):
-                bk = bank(banks[t], "a%d%d" % (h, t))
-                mm(bk[:], qx_d[h], t * P, E4M3, qw, E4M3, True, True)
-                acc.append(bk)
+                nc.vector.scalar_tensor_tensor(work[h][:, t, 0:256], acc[t // 2][:, (t % 2) * 256 : (t % 2 + 1) * 256], neg_u[h][:, t : t + 1], ts_all[:, 0:256], ALU.mult, ALU.mult)
             for t in range(PACK + 1):
                 if t < PACK:
-                    nc.vector.scalar_tensor_tensor(work[h][:, t, :], acc[t][:], neg_u[h][:, t : t + 1], ts_all[:], ALU.mult, ALU.mult)
+                    nc.vector.scalar_tensor_tensor(work[h][:, t, 256:512], acc[2 + t // 2][:, (t % 2) * 256 : (t % 2 + 1) * 256], neg_u[h][:, t : t + 1], ts_all[:, 256:512], ALU.mult, ALU.mult)
                 if t > 0:
                     nc.vector.tensor_reduce(neg_m[h][:, t - 1 : t], work[h][:, t - 1, :], AX.X, ALU.min)
                     expo(h, t - 1)
@@ -175,35 +177,85 @@ def tile_attend_gheads_sm_kernel(tc, x1, x2, wT, y1, u1, w1, y2, u2, w2, ts, off
                                         accum_out=neg_m[h][:, t : t + 1])
                 expo(h, t)
 
-        def gradient(h):
-            nc.vector.reciprocal(inv[h][:], total[h][:])
-            for t in range(PACK):
-                nc.vector.scalar_tensor_tensor(work[h][:, t, :], work[h][:, t, :], inv[h][:, t : t + 1], y_raw[h][:, t, :], ALU.mult, ALU.subtract)
-            nc.vector.tensor_tensor(
-                g[h][:].rearrange("p (c i t) -> p c t i", i=4, t=PACK),
-                work[h][:].rearrange("p t (c i) -> p c t i", i=4),
-                factor[h][:].rearrange("p t (c i) -> p c t i", i=4),
-                ALU.mult,
-            )
+        def recip(h, lo, hi):
+            nc.vector.reciprocal(inv[h][:, lo:hi], total[h][:, lo:hi])
 
+        def fold(lo, hi):
+            nc.vector.tensor_tensor(cinv[:, lo:hi], inv[0][:, lo:hi], wu[0][:, lo:hi], ALU.mult)
+
+        def diff(h, t, col):
+            nc.vector.scalar_tensor_tensor(work[h][:, t, :], work[h][:, t, :], col[:, t : t + 1], y_raw[h][:, t, :], ALU.mult, ALU.subtract)
+
+        def turn_g():
+            hb = [bank(c, "hT%d" % c) for c in range(4)]
+            for t in range(PACK):
+                for c in range(4):
+                    nc.tensor.transpose(hb[c][:, t * P : (t + 1) * P], work[0][:, t, c * P : (c + 1) * P], ident[:])
+            for c in range(4):
+                nc.scalar.activation(g_t[c][:].rearrange("i (s t) -> i s t", t=PACK), hb[c][:].rearrange("i (t s) -> i s t", t=PACK),
+                                     ACT.Copy, scale=ts_col[:, c : c + 1])
+            for pair in range(2):
+                bk = bank(4 + pair, "gw%d" % pair)
+                for k in range(2):
+                    words = g_t[2 * pair + k][:].bitcast(F32)
+                    for u in range(2):
+                        nc.tensor.transpose(bk[:, (2 * k + u) * P : (2 * k + u + 1) * P], words[:, u:256:2], ident[:])
+                nc.scalar.copy(g[0][:, pair * 1024 : (pair + 1) * 1024].bitcast(F32).rearrange("s (k i u) -> s k i u", k=2, u=2),
+                               bk[:].rearrange("s (k u i) -> s k i u", k=2, u=2))
+
+        def weave(h, lo, hi, copy):
+            copy(g[h][:, PACK * lo : PACK * hi].rearrange("p (c i t) -> p c t i", i=4, t=PACK),
+                 planes[h][:, :, lo:hi].rearrange("p t (c i) -> p c t i", i=4))
+
+        def zero(name, tag):
+            win = keep.tile([P, T], F32, name=name, tag=tag, align_bytes=64)
+            for k in range(4):
+                nc.gpsimd.memset(win[:, k * 512 : (k + 1) * 512], 0.0)
+            return win
+
+        window0 = zero("window0", "w_d")
+        for t in range(PACK):
+            nc.gpsimd.tensor_scalar(y_raw[0][:, t, :], y_raw[0][:, t, :], wu[0][:, t : t + 1], 0.0, ALU.mult, ALU.add)
         deal_x(1, nc.scalar.copy)
-        scores_direct(0, (0, 1, 2, 3))
+        window1 = zero("window1", "x_raw1")
+        windows = [window0, window1, window2]
+        scores_direct(0, acc1)
+        recip(0, 0, 2)
         quantise(qx_d[1], x_d[1], E4M3)
+        fold(0, 2)
         sb = scores_turned(1, (4, 5, 6, 7), (4, 5, 6, 7))
         turn_x(1, (0, 1))
-        gradient(0)
+        recip(0, 2, 3)
+        diff(0, 0, cinv)
+        fold(2, 3)
+        recip(0, 3, 4)
+        diff(0, 1, cinv)
+        fold(3, 4)
+        diff(0, 2, cinv)
+        diff(0, 3, cinv)
         max_turned(1, sb)
+        turn_g()
+        recip(1, 0, 2)
+        quantise(qx_r[1], x_r[1], E4M3, 0, 128)
+        diff(1, 0, inv[1])
+        recip(1, 2, 4)
+        for t in range(1, PACK):
+            diff(1, t, inv[1])
+        for t in range(PACK):
+            nc.vector.scalar_tensor_tensor(planes[1][:, t, :], work[1][:, t, :], wu[1][:, t : t + 1], ts_all[:], ALU.mult, ALU.mult)
         quantise(qg[0], g[0], E5M2)
-        quantise(qx_r[1], x_r[1], E4M3)
+        weave(1, 0, 256, nc.vector.tensor_copy)
+        weave(1, 256, 512, nc.scalar.copy)
+        quantise(qg[1], g[1], E5M2, 0, 256)
+        quantise(qg[1], g[1], E5M2, 256, 512)
+        quantise(qx_r[1], x_r[1], E4M3, 128, 256)
+        quantise(qx_r[1], x_r[1], E4M3, 256, 512)
         acc = [bank(j, "dw%d" % j) for j in range(PACK)]
-        for j in range(PACK):
-            mm(acc[j][:], qx_r[0], j * P, E4M3, qg[0], E5M2, True, False)
-        gradient(1)
-        quantise(qg[1], g[1], E5M2)
 
         dw = [keep.tile([P, S], F32, name="dw%d" % j) for j in range(PACK)]
         out_view = out.rearrange("(p j) n -> j p n", j=PACK)
         for j in range(PACK):
+            mm(acc[j][:], qx_r[0], j * P, E4M3, qg[0], E5M2, True, False)
             mm(acc[j][:], qx_r[1], j * P, E4M3, qg[1], E5M2, False, True)
             nc.scalar.copy(dw[j][:], acc[j][:])
             win = windows[j % WINDOWS]

@@ -48,22 +48,23 @@ def tile_attend_gheads_sm_kernel(tc, x1, x2, wT, y1, u1, w1, y2, u2, w2, ts, off
         nc.sync.dma_start(ts_win[0:1, :], ts[0:1, :])
         for j in range(PACK):
             nc.sync.dma_start(w_plane[j][:], w_view[j])
+        u_col = [keep.tile([P, PACK], F32, name="u_col%d" % h) for h in heads]
+        w_col = [keep.tile([P, PACK], F32, name="w_col%d" % h) for h in heads]
+        nc.sync.dma_start(u_col[0][:], us[0].rearrange("(p t) o -> p (t o)", t=PACK))
+        nc.sync.dma_start(w_col[0][:], ws[0].rearrange("(p t) o -> p (t o)", t=PACK))
+        nc.scalar.dma_start(u_col[1][:], us[1].rearrange("(p t) o -> p (t o)", t=PACK))
+        nc.scalar.dma_start(w_col[1][:], ws[1].rearrange("(p t) o -> p (t o)", t=PACK))
         nc.sync.dma_start(x_raw[1][:], xs[1].rearrange("(p j) r -> p j r", j=PACK))
         for h in heads:
             nc.sync.dma_start(y_raw[h][:], ys[h].rearrange("(p t) i -> p t i", t=PACK))
 
         ident = keep.tile([P, P], F32, name="ident")
         make_identity(nc, ident[:])
-        u_col = [keep.tile([P, PACK], F32, name="u_col%d" % h) for h in heads]
-        w_col = [keep.tile([P, PACK], F32, name="w_col%d" % h) for h in heads]
-        neg_u = [keep.tile([P, PACK], F32, name="neg_u%d" % h) for h in heads]
+        neg_u = keep.tile([P, PACK], F32, name="neg_u")
         wu = [keep.tile([P, PACK], F32, name="wu%d" % h) for h in heads]
-        for h in heads:
-            nc.scalar.dma_start(u_col[h][:], us[h].rearrange("(p t) o -> p (t o)", t=PACK))
-            nc.scalar.dma_start(w_col[h][:], ws[h].rearrange("(p t) o -> p (t o)", t=PACK))
-        for h in heads:
-            nc.gpsimd.tensor_scalar(neg_u[h][:], u_col[h][:], -1.0, 0.0, ALU.mult, ALU.add)
-            nc.gpsimd.tensor_tensor(wu[h][:], u_col[h][:], w_col[h][:], ALU.mult)
+        nc.gpsimd.tensor_scalar(neg_u[:], u_col[1][:], -1.0, 0.0, ALU.mult, ALU.add)
+        nc.gpsimd.tensor_tensor(wu[1][:], u_col[1][:], w_col[1][:], ALU.mult)
+        nc.gpsimd.tensor_tensor(wu[0][:], u_col[0][:], w_col[0][:], ALU.mult)
 
         warm = keep.tile([P, 1], F32, name="warm")
         nc.scalar.activation(warm[:], ident[:, 0:1], ACT.Exp)
@@ -92,9 +93,9 @@ def tile_attend_gheads_sm_kernel(tc, x1, x2, wT, y1, u1, w1, y2, u2, w2, ts, off
         def deal_x(h, copy):
             copy(x_d[h][:].rearrange("p (t s j) -> p s t j", t=PACK, j=PACK), x_raw[h][:].rearrange("p j (s t) -> p s t j", t=PACK))
 
-        def turn_x(h, banks):
+        def turn_x(h, banks, halves=(0, 1)):
             words = x_d[h][:].bitcast(F32)
-            for u in range(2):
+            for u in halves:
                 bk = bank(banks[u], "xw%d%d" % (h, u))
                 for t in range(PACK):
                     nc.tensor.transpose(bk[:, t * P : (t + 1) * P], words[:, 256 * t + u : 256 * (t + 1) : 2], ident[:])
@@ -122,6 +123,9 @@ def tile_attend_gheads_sm_kernel(tc, x1, x2, wT, y1, u1, w1, y2, u2, w2, ts, off
         nc.vector.tensor_copy(w_d[:, :, 0], w_plane[0][:].indirect(offsets[:]))
         quantise(qx_d[0], x_d[0], E4M3)
         turn_x(0, (2, 3))
+        factor = keep.tile([P, PACK, S], F32, name="factor")
+        for t in range(PACK):
+            nc.scalar.activation(factor[:, t, :], ts_all[:], ACT.Copy, scale=wu[1][:, t : t + 1])
         nc.vector.tensor_copy(w_d[:, :, 1], w_plane[1][:].indirect(offsets[:]))
         quantise(qx_r[0], x_r[0], E4M3)
         nc.vector.tensor_copy(w_d[:, :, 2], w_plane[2][:].indirect(offsets[:]))
@@ -141,23 +145,22 @@ def tile_attend_gheads_sm_kernel(tc, x1, x2, wT, y1, u1, w1, y2, u2, w2, ts, off
         total = [keep.tile([P, PACK], F32, name="total%d" % h) for h in heads]
         inv = [keep.tile([P, PACK], F32, name="inv%d" % h) for h in heads]
         g = [keep.tile([P, S * PACK], BF16, name="g%d" % h, align_bytes=64) for h in heads]
-        planes = [None, keep.tile([P, PACK, S], BF16, name="planes1", align_bytes=64)]
         g_t = [keep.tile([P, R], BF16, name="g_t%d" % c, align_bytes=64) for c in range(4)]
         cinv = keep.tile([P, PACK], F32, name="cinv")
         turned = keep.tile([P, 4, R], F32, name="turned")
 
         def expo(h, t):
-            nc.scalar.activation(work[h][:, t, :], work[h][:, t, :], ACT.Exp, bias=neg_m[h][:, t : t + 1], scale=-1.0,
+            nc.scalar.activation(work[h][:, t, :], work[h][:, t, :], ACT.Exp, bias=neg_m[h][:, t : t + 1], scale=(1.0, -1.0)[h],
                                  accum_out=total[h][:, t : t + 1])
 
         def scores_direct(h, acc):
             for t in range(PACK):
-                nc.vector.scalar_tensor_tensor(work[h][:, t, 0:256], acc[t // 2][:, (t % 2) * 256 : (t % 2 + 1) * 256], neg_u[h][:, t : t + 1], ts_all[:, 0:256], ALU.mult, ALU.mult)
+                nc.vector.scalar_tensor_tensor(work[h][:, t, 0:256], acc[t // 2][:, (t % 2) * 256 : (t % 2 + 1) * 256], u_col[h][:, t : t + 1], ts_all[:, 0:256], ALU.mult, ALU.mult)
             for t in range(PACK + 1):
                 if t < PACK:
-                    nc.vector.scalar_tensor_tensor(work[h][:, t, 256:512], acc[2 + t // 2][:, (t % 2) * 256 : (t % 2 + 1) * 256], neg_u[h][:, t : t + 1], ts_all[:, 256:512], ALU.mult, ALU.mult)
+                    nc.vector.scalar_tensor_tensor(work[h][:, t, 256:512], acc[2 + t // 2][:, (t % 2) * 256 : (t % 2 + 1) * 256], u_col[h][:, t : t + 1], ts_all[:, 256:512], ALU.mult, ALU.mult)
                 if t > 0:
-                    nc.vector.tensor_reduce(neg_m[h][:, t - 1 : t], work[h][:, t - 1, :], AX.X, ALU.min)
+                    nc.vector.tensor_reduce(neg_m[h][:, t - 1 : t], work[h][:, t - 1, :], AX.X, ALU.max, negate=True)
                     expo(h, t - 1)
 
         def scores_turned(h, banks_a, banks_s):
@@ -173,7 +176,7 @@ def tile_attend_gheads_sm_kernel(tc, x1, x2, wT, y1, u1, w1, y2, u2, w2, ts, off
 
         def max_turned(h, sb):
             for t in range(PACK):
-                nc.vector.tensor_scalar(work[h][:, t, :], sb[t][:], neg_u[h][:, t : t + 1], None, ALU.mult, ALU.min,
+                nc.vector.tensor_scalar(work[h][:, t, :], sb[t][:], neg_u[:, t : t + 1], None, ALU.mult, ALU.min,
                                         accum_out=neg_m[h][:, t : t + 1])
                 expo(h, t)
 
@@ -183,14 +186,14 @@ def tile_attend_gheads_sm_kernel(tc, x1, x2, wT, y1, u1, w1, y2, u2, w2, ts, off
         def fold(lo, hi):
             nc.vector.tensor_tensor(cinv[:, lo:hi], inv[0][:, lo:hi], wu[0][:, lo:hi], ALU.mult)
 
-        def diff(h, t, col):
-            nc.vector.scalar_tensor_tensor(work[h][:, t, :], work[h][:, t, :], col[:, t : t + 1], y_raw[h][:, t, :], ALU.mult, ALU.subtract)
+        def diff(h, t, col, op=ALU.subtract):
+            nc.vector.scalar_tensor_tensor(work[h][:, t, :], work[h][:, t, :], col[:, t : t + 1], y_raw[h][:, t, :], ALU.mult, op)
+
+        def turn_add(src, t, start, stop):
+            for c in range(4):
+                nc.tensor.matmul(hb[c][:, t * P : (t + 1) * P], src[:, t, c * P : (c + 1) * P], ident[:], start=start, stop=stop, is_transpose=True)
 
         def turn_g():
-            hb = [bank(c, "hT%d" % c) for c in range(4)]
-            for t in range(PACK):
-                for c in range(4):
-                    nc.tensor.transpose(hb[c][:, t * P : (t + 1) * P], work[0][:, t, c * P : (c + 1) * P], ident[:])
             for c in range(4):
                 nc.scalar.activation(g_t[c][:].rearrange("i (s t) -> i s t", t=PACK), hb[c][:].rearrange("i (t s) -> i s t", t=PACK),
                                      ACT.Copy, scale=ts_col[:, c : c + 1])
@@ -203,9 +206,13 @@ def tile_attend_gheads_sm_kernel(tc, x1, x2, wT, y1, u1, w1, y2, u2, w2, ts, off
                 nc.scalar.copy(g[0][:, pair * 1024 : (pair + 1) * 1024].bitcast(F32).rearrange("s (k i u) -> s k i u", k=2, u=2),
                                bk[:].rearrange("s (k u i) -> s k i u", k=2, u=2))
 
-        def weave(h, lo, hi, copy):
-            copy(g[h][:, PACK * lo : PACK * hi].rearrange("p (c i t) -> p c t i", i=4, t=PACK),
-                 planes[h][:, :, lo:hi].rearrange("p t (c i) -> p c t i", i=4))
+        def weave(lo, hi):
+            nc.vector.tensor_tensor(
+                g[1][:, PACK * lo : PACK * hi].rearrange("p (c i t) -> p c t i", i=4, t=PACK),
+                work[1][:, :, lo:hi].rearrange("p t (c i) -> p c t i", i=4),
+                factor[:, :, lo:hi].rearrange("p t (c i) -> p c t i", i=4),
+                ALU.mult,
+            )
 
         def zero(name, tag):
             win = keep.tile([P, T], F32, name=name, tag=tag, align_bytes=64)
@@ -224,7 +231,6 @@ def tile_attend_gheads_sm_kernel(tc, x1, x2, wT, y1, u1, w1, y2, u2, w2, ts, off
         quantise(qx_d[1], x_d[1], E4M3)
         fold(0, 2)
         sb = scores_turned(1, (4, 5, 6, 7), (4, 5, 6, 7))
-        turn_x(1, (0, 1))
         recip(0, 2, 3)
         diff(0, 0, cinv)
         fold(2, 3)
@@ -233,31 +239,37 @@ def tile_attend_gheads_sm_kernel(tc, x1, x2, wT, y1, u1, w1, y2, u2, w2, ts, off
         fold(3, 4)
         diff(0, 2, cinv)
         diff(0, 3, cinv)
+        hb = [bank(c, "hT%d" % c) for c in range(4)]
+        for t in range(PACK):
+            turn_add(work[0], t, True, True)
         max_turned(1, sb)
         turn_g()
+        turn_x(1, (4, 5))
         recip(1, 0, 2)
-        quantise(qx_r[1], x_r[1], E4M3, 0, 128)
         diff(1, 0, inv[1])
-        recip(1, 2, 4)
-        for t in range(1, PACK):
-            diff(1, t, inv[1])
-        for t in range(PACK):
-            nc.vector.scalar_tensor_tensor(planes[1][:, t, :], work[1][:, t, :], wu[1][:, t : t + 1], ts_all[:], ALU.mult, ALU.mult)
+        recip(1, 2, 3)
+        diff(1, 1, inv[1])
+        recip(1, 3, 4)
+        diff(1, 2, inv[1])
+        diff(1, 3, inv[1])
+        weave(0, 256)
         quantise(qg[0], g[0], E5M2)
-        weave(1, 0, 256, nc.vector.tensor_copy)
-        weave(1, 256, 512, nc.scalar.copy)
+        acc = [bank(j, "dw%d" % j) for j in range(PACK)]
+        for j in range(PACK):
+            mm(acc[j][:], qx_r[0], j * P, E4M3, qg[0], E5M2, True, False)
+        weave(256, 512)
         quantise(qg[1], g[1], E5M2, 0, 256)
+        quantise(qx_r[1], x_r[1], E4M3, 0, 128)
         quantise(qg[1], g[1], E5M2, 256, 512)
         quantise(qx_r[1], x_r[1], E4M3, 128, 256)
-        quantise(qx_r[1], x_r[1], E4M3, 256, 512)
-        acc = [bank(j, "dw%d" % j) for j in range(PACK)]
 
         dw = [keep.tile([P, S], F32, name="dw%d" % j) for j in range(PACK)]
         out_view = out.rearrange("(p j) n -> j p n", j=PACK)
         for j in range(PACK):
-            mm(acc[j][:], qx_r[0], j * P, E4M3, qg[0], E5M2, True, False)
             mm(acc[j][:], qx_r[1], j * P, E4M3, qg[1], E5M2, False, True)
             nc.scalar.copy(dw[j][:], acc[j][:])
             win = windows[j % WINDOWS]
             nc.vector.tensor_copy(win[:].indirect(offsets[:]), dw[j][:])
             nc.sync.dma_start(out_view[j], win[:])
+            if j == 0:
+                quantise(qx_r[1], x_r[1], E4M3, 256, 512)

@@ -21,7 +21,6 @@ R = 512
 S = 512
 T = 2048
 FLOPS = 4 * 2 * 512 * 512 * 512
-TURNED = (False, True)
 WINDOWS = 3
 
 
@@ -68,8 +67,11 @@ def tile_attend_gheads_sm_kernel(tc, x1, x2, wT, y1, u1, w1, y2, u2, w2, ts, off
 
         warm = keep.tile([P, 1], F32, name="warm")
         nc.scalar.activation(warm[:], ident[:, 0:1], ACT.Exp)
-        window2 = keep.tile([P, T], F32, name="window2")
-        nc.vector.memset(window2[:], 0.0)
+        windows = [keep.tile([P, T], F32, name="window%d" % k) for k in range(WINDOWS)]
+        nc.vector.memset(windows[2][:].bitcast(U32), 0)
+        for k in range(2):
+            for q in range(4):
+                nc.gpsimd.memset(windows[k][:, q * 512 : (q + 1) * 512], 0.0)
 
         def codes(name):
             c = keep.tile([P, 512], U32, name=name + "_c", align_bytes=64)
@@ -214,18 +216,10 @@ def tile_attend_gheads_sm_kernel(tc, x1, x2, wT, y1, u1, w1, y2, u2, w2, ts, off
                 ALU.mult,
             )
 
-        def zero(name, tag):
-            win = keep.tile([P, T], F32, name=name, tag=tag, align_bytes=64)
-            for k in range(4):
-                nc.gpsimd.memset(win[:, k * 512 : (k + 1) * 512], 0.0)
-            return win
-
-        window0 = zero("window0", "w_d")
-        for t in range(PACK):
+        for t in range(PACK - 1):
             nc.gpsimd.tensor_scalar(y_raw[0][:, t, :], y_raw[0][:, t, :], wu[0][:, t : t + 1], 0.0, ALU.mult, ALU.add)
         deal_x(1, nc.scalar.copy)
-        window1 = zero("window1", "x_raw1")
-        windows = [window0, window1, window2]
+        nc.scalar.activation(y_raw[0][:, 3, :], y_raw[0][:, 3, :], ACT.Copy, scale=wu[0][:, 3:4])
         scores_direct(0, acc1)
         recip(0, 0, 2)
         quantise(qx_d[1], x_d[1], E4M3)
@@ -268,8 +262,8 @@ def tile_attend_gheads_sm_kernel(tc, x1, x2, wT, y1, u1, w1, y2, u2, w2, ts, off
         for j in range(PACK):
             mm(acc[j][:], qx_r[1], j * P, E4M3, qg[1], E5M2, False, True)
             nc.scalar.copy(dw[j][:], acc[j][:])
+            if j == 0:
+                quantise(qx_r[1], x_r[1], E4M3, 256, 512)
             win = windows[j % WINDOWS]
             nc.vector.tensor_copy(win[:].indirect(offsets[:]), dw[j][:])
             nc.sync.dma_start(out_view[j], win[:])
-            if j == 0:
-                quantise(qx_r[1], x_r[1], E4M3, 256, 512)

@@ -49,10 +49,9 @@ def tile_attend_gheads_sm_kernel(tc, x1, x2, wT, y1, u1, w1, y2, u2, w2, ts, off
             nc.sync.dma_start(w_plane[j][:], w_view[j])
         u_col = [keep.tile([P, PACK], F32, name="u_col%d" % h) for h in heads]
         w_col = [keep.tile([P, PACK], F32, name="w_col%d" % h) for h in heads]
-        nc.sync.dma_start(u_col[0][:], us[0].rearrange("(p t) o -> p (t o)", t=PACK))
-        nc.sync.dma_start(w_col[0][:], ws[0].rearrange("(p t) o -> p (t o)", t=PACK))
-        nc.scalar.dma_start(u_col[1][:], us[1].rearrange("(p t) o -> p (t o)", t=PACK))
-        nc.scalar.dma_start(w_col[1][:], ws[1].rearrange("(p t) o -> p (t o)", t=PACK))
+        for h in (1, 0):
+            nc.scalar.dma_start(u_col[h][:], us[h].rearrange("(p t) o -> p (t o)", t=PACK))
+            nc.scalar.dma_start(w_col[h][:], ws[h].rearrange("(p t) o -> p (t o)", t=PACK))
         nc.sync.dma_start(x_raw[1][:], xs[1].rearrange("(p j) r -> p j r", j=PACK))
         for h in heads:
             nc.sync.dma_start(y_raw[h][:], ys[h].rearrange("(p t) i -> p t i", t=PACK))
@@ -86,7 +85,7 @@ def tile_attend_gheads_sm_kernel(tc, x1, x2, wT, y1, u1, w1, y2, u2, w2, ts, off
                                 rhs=rhs[0][:].bitcast(rfmt), rhs_scale=rhs[1][:], start=start, stop=stop)
 
         x_d = [keep.tile([P, R * PACK], BF16, name="x_d%d" % h, align_bytes=64) for h in heads]
-        x_r = [keep.tile([P, D * PACK], BF16, name="x_r%d" % h, align_bytes=64) for h in heads]
+        x_r = [[keep.tile([P, 1024], BF16, name="x_r0%d" % u, align_bytes=64) for u in range(2)], [None, keep.tile([P, 1024], BF16, name="x_r11", align_bytes=64)]]
         qx_d = [codes("qx_d%d" % h) for h in heads]
         qx_r = [codes("qx_r%d" % h) for h in heads]
         qg = [codes("qg%d" % h) for h in heads]
@@ -95,16 +94,20 @@ def tile_attend_gheads_sm_kernel(tc, x1, x2, wT, y1, u1, w1, y2, u2, w2, ts, off
         def deal_x(h, copy):
             copy(x_d[h][:].rearrange("p (t s j) -> p s t j", t=PACK, j=PACK), x_raw[h][:].rearrange("p j (s t) -> p s t j", t=PACK))
 
-        def turn_x(h, banks, halves=(0, 1)):
+        def turn_x(h, u, b):
             words = x_d[h][:].bitcast(F32)
-            for u in halves:
-                bk = bank(banks[u], "xw%d%d" % (h, u))
-                for t in range(PACK):
-                    nc.tensor.transpose(bk[:, t * P : (t + 1) * P], words[:, 256 * t + u : 256 * (t + 1) : 2], ident[:])
-                nc.scalar.copy(
-                    x_r[h][:, u * 1024 : (u + 1) * 1024].rearrange("s (e p t) -> s e p t", e=2, t=PACK),
-                    bk[:].bitcast(BF16).rearrange("s (t p e) -> s e p t", t=PACK, e=2),
-                )
+            bk = bank(b, "xw%d%d" % (h, u))
+            for t in range(PACK):
+                nc.tensor.transpose(bk[:, t * P : (t + 1) * P], words[:, 256 * t + u : 256 * (t + 1) : 2], ident[:])
+            return bk
+
+        def weave_x(h, u, bk):
+            nc.scalar.copy(x_r[h][u][:].rearrange("s (e p t) -> s e p t", e=2, t=PACK), bk[:].bitcast(BF16).rearrange("s (t p e) -> s e p t", t=PACK, e=2))
+
+        def quantise_x(h, lo, hi):
+            u = lo // 256
+            nc.vector.quantize_mx(out=qx_r[h][0][:, lo:hi].bitcast(E4M3), scales=qx_r[h][1][:, lo:hi],
+                                  in_=x_r[h][u][:, PACK * (lo - 256 * u) : PACK * (hi - 256 * u)])
 
         ts_row = keep.tile([P, S], F32, name="ts_row")
         nc.vector.tensor_copy(ts_row[:], ts_win[:].indirect(offsets[:]))
@@ -114,6 +117,8 @@ def tile_attend_gheads_sm_kernel(tc, x1, x2, wT, y1, u1, w1, y2, u2, w2, ts, off
             nc.tensor.transpose(bk[:, c * P : (c + 1) * P], ts_row[:, c * P : (c + 1) * P], ident[:])
         ts_col = keep.tile([P, 4], F32, name="ts_col")
         nc.scalar.copy(ts_col[:], bk[:, 0:512:P])
+        ts_col2 = keep.tile([P, 4], F32, name="ts_col2", align_bytes=64)
+        nc.scalar.copy(ts_col2[:], bk[:, 0:512:P])
         bk = bank(1, "ts_spread")
         for c in range(4):
             nc.tensor.transpose(bk[:, c * P : (c + 1) * P], ts_col[:, c : c + 1].to_broadcast([P, P]), ident[:])
@@ -124,12 +129,14 @@ def tile_attend_gheads_sm_kernel(tc, x1, x2, wT, y1, u1, w1, y2, u2, w2, ts, off
         w_flat = w_d[:].rearrange("p i j -> p (i j)")
         nc.vector.tensor_copy(w_d[:, :, 0], w_plane[0][:].indirect(offsets[:]))
         quantise(qx_d[0], x_d[0], E4M3)
-        turn_x(0, (2, 3))
+        for u in range(2):
+            weave_x(0, u, turn_x(0, u, 2 + u))
         factor = keep.tile([P, PACK, S], F32, name="factor")
         for t in range(PACK):
             nc.scalar.activation(factor[:, t, :], ts_all[:], ACT.Copy, scale=wu[1][:, t : t + 1])
         nc.vector.tensor_copy(w_d[:, :, 1], w_plane[1][:].indirect(offsets[:]))
-        quantise(qx_r[0], x_r[0], E4M3)
+        quantise_x(0, 0, 256)
+        quantise_x(0, 256, 512)
         nc.vector.tensor_copy(w_d[:, :, 2], w_plane[2][:].indirect(offsets[:]))
         acc1 = []
         for half in range(2):
@@ -169,7 +176,7 @@ def tile_attend_gheads_sm_kernel(tc, x1, x2, wT, y1, u1, w1, y2, u2, w2, ts, off
             for c in range(4):
                 bk = bank(banks_a[c], "aT%d%d" % (h, c))
                 mm(bk[:], qw, c * P, E4M3, qx_d[h], E4M3, True, True)
-                nc.scalar.activation(turned[:, c, :], bk[:], ACT.Copy, scale=ts_col[:, c : c + 1])
+                nc.scalar.activation(turned[:, c, :], bk[:], ACT.Copy, scale=ts_col2[:, c : c + 1])
             sb = [bank(banks_s[t], "s%d%d" % (h, t)) for t in range(PACK)]
             order = [(c, t) for c in range(4) for t in range(PACK)] if banks_a != banks_s else [(c, t) for t in range(PACK) for c in range(4)]
             for c, t in order:
@@ -210,9 +217,9 @@ def tile_attend_gheads_sm_kernel(tc, x1, x2, wT, y1, u1, w1, y2, u2, w2, ts, off
 
         def weave(lo, hi):
             nc.vector.tensor_tensor(
-                g[1][:, PACK * lo : PACK * hi].rearrange("p (c i t) -> p c t i", i=4, t=PACK),
-                work[1][:, :, lo:hi].rearrange("p t (c i) -> p c t i", i=4),
-                factor[:, :, lo:hi].rearrange("p t (c i) -> p c t i", i=4),
+                g[1][:, PACK * lo : PACK * hi].rearrange("p (c i t) -> p c t i", i=2, t=PACK),
+                work[1][:, :, lo:hi].rearrange("p t (c i) -> p c t i", i=2),
+                factor[:, :, lo:hi].rearrange("p t (c i) -> p c t i", i=2),
                 ALU.mult,
             )
 
@@ -225,6 +232,9 @@ def tile_attend_gheads_sm_kernel(tc, x1, x2, wT, y1, u1, w1, y2, u2, w2, ts, off
         quantise(qx_d[1], x_d[1], E4M3)
         fold(0, 2)
         sb = scores_turned(1, (4, 5, 6, 7), (4, 5, 6, 7))
+        xw = turn_x(1, 0, 0)
+        x_r[1][0] = keep.tile([P, 1024], BF16, name="x_r10", tag="ts_col2", align_bytes=64)
+        weave_x(1, 0, xw)
         recip(0, 2, 3)
         diff(0, 0, cinv)
         fold(2, 3)
@@ -238,7 +248,7 @@ def tile_attend_gheads_sm_kernel(tc, x1, x2, wT, y1, u1, w1, y2, u2, w2, ts, off
             turn_add(work[0], t, True, True)
         max_turned(1, sb)
         turn_g()
-        turn_x(1, (4, 5))
+        weave_x(1, 1, turn_x(1, 1, 4))
         recip(1, 0, 2)
         diff(1, 0, inv[1])
         recip(1, 2, 3)
@@ -246,24 +256,23 @@ def tile_attend_gheads_sm_kernel(tc, x1, x2, wT, y1, u1, w1, y2, u2, w2, ts, off
         recip(1, 3, 4)
         diff(1, 2, inv[1])
         diff(1, 3, inv[1])
+        quantise_x(1, 0, 128)
         weave(0, 256)
-        quantise(qg[0], g[0], E5M2)
-        acc = [bank(j, "dw%d" % j) for j in range(PACK)]
-        for j in range(PACK):
-            mm(acc[j][:], qx_r[0], j * P, E4M3, qg[0], E5M2, True, False)
         weave(256, 512)
         quantise(qg[1], g[1], E5M2, 0, 256)
-        quantise(qx_r[1], x_r[1], E4M3, 0, 128)
         quantise(qg[1], g[1], E5M2, 256, 512)
-        quantise(qx_r[1], x_r[1], E4M3, 128, 256)
+        quantise(qg[0], g[0], E5M2)
+        quantise_x(1, 128, 256)
 
         dw = [keep.tile([P, S], F32, name="dw%d" % j) for j in range(PACK)]
         out_view = out.rearrange("(p j) n -> j p n", j=PACK)
         for j in range(PACK):
-            mm(acc[j][:], qx_r[1], j * P, E4M3, qg[1], E5M2, False, True)
-            nc.scalar.copy(dw[j][:], acc[j][:])
+            acc = bank(j, "dw%d" % j)
+            mm(acc[:], qx_r[1], j * P, E4M3, qg[1], E5M2, True, False)
+            mm(acc[:], qx_r[0], j * P, E4M3, qg[0], E5M2, False, True)
+            nc.scalar.copy(dw[j][:], acc[:])
             if j == 0:
-                quantise(qx_r[1], x_r[1], E4M3, 256, 512)
+                quantise_x(1, 256, 512)
             win = windows[j % WINDOWS]
             nc.vector.tensor_copy(win[:].indirect(offsets[:]), dw[j][:])
             nc.sync.dma_start(out_view[j], win[:])

@@ -37,7 +37,7 @@ def tile_attend_gheads_sm_kernel(tc, x1, x2, wT, y1, u1, w1, y2, u2, w2, ts, off
 
         offsets = keep.tile([P, S // 16], U16, name="offsets")
         x_raw = [keep.tile([P, PACK, R], F32, name="x_raw%d" % h, align_bytes=64) for h in heads]
-        w_plane = [keep.tile([P, T], F32, name="w_plane%d" % j) for j in range(PACK)]
+        w_plane = [keep.tile([P, T], F32, name="w_plane%d" % j, align_bytes=64) for j in range(PACK)]
         y_raw = [keep.tile([P, PACK, S], F32, name="y_raw%d" % h) for h in heads]
         w_view = wT.rearrange("(p j) n -> j p n", j=PACK)
         ts_win = keep.tile([P, T], F32, name="ts_win")
@@ -66,14 +66,11 @@ def tile_attend_gheads_sm_kernel(tc, x1, x2, wT, y1, u1, w1, y2, u2, w2, ts, off
 
         warm = keep.tile([P, 1], F32, name="warm")
         nc.scalar.activation(warm[:], ident[:, 0:1], ACT.Exp)
-        windows = [keep.tile([P, T], F32, name="window%d" % k) for k in range(WINDOWS)]
-        nc.vector.memset(windows[2][:].bitcast(U32), 0)
-        for k in range(2):
-            for q in range(4):
-                nc.gpsimd.memset(windows[k][:, q * 512 : (q + 1) * 512], 0.0)
+        window2 = keep.tile([P, T], F32, name="window2")
+        nc.vector.memset(window2[:].bitcast(U32), 0)
 
-        def codes(name):
-            c = keep.tile([P, 512], U32, name=name + "_c", align_bytes=64)
+        def codes(name, tag=None):
+            c = keep.tile([P, 512], U32, name=name + "_c", tag=tag or name + "_c", align_bytes=64)
             s = keep.tile([P, 512], U8, name=name + "_s", align_bytes=64)
             return c, s
 
@@ -87,7 +84,7 @@ def tile_attend_gheads_sm_kernel(tc, x1, x2, wT, y1, u1, w1, y2, u2, w2, ts, off
         x_d = [keep.tile([P, R * PACK], BF16, name="x_d%d" % h, align_bytes=64) for h in heads]
         x_r = [[keep.tile([P, 1024], BF16, name="x_r0%d" % u, align_bytes=64) for u in range(2)], [None, keep.tile([P, 1024], BF16, name="x_r11", align_bytes=64)]]
         qx_d = [codes("qx_d%d" % h) for h in heads]
-        qx_r = [codes("qx_r%d" % h) for h in heads]
+        qx_r = [None, codes("qx_r1")]
         qg = [codes("qg%d" % h) for h in heads]
         qw = codes("qw")
 
@@ -135,8 +132,6 @@ def tile_attend_gheads_sm_kernel(tc, x1, x2, wT, y1, u1, w1, y2, u2, w2, ts, off
         for t in range(PACK):
             nc.scalar.activation(factor[:, t, :], ts_all[:], ACT.Copy, scale=wu[1][:, t : t + 1])
         nc.vector.tensor_copy(w_d[:, :, 1], w_plane[1][:].indirect(offsets[:]))
-        quantise_x(0, 0, 256)
-        quantise_x(0, 256, 512)
         nc.vector.tensor_copy(w_d[:, :, 2], w_plane[2][:].indirect(offsets[:]))
         acc1 = []
         for half in range(2):
@@ -223,10 +218,19 @@ def tile_attend_gheads_sm_kernel(tc, x1, x2, wT, y1, u1, w1, y2, u2, w2, ts, off
                 ALU.mult,
             )
 
+        def zero(name, tag):
+            win = keep.tile([P, T], F32, name=name, tag=tag, align_bytes=64)
+            for k in range(4):
+                nc.gpsimd.memset(win[:, k * 512 : (k + 1) * 512], 0.0)
+            return win
+
+        window0 = zero("window0", "w_d")
         for t in range(PACK - 1):
             nc.gpsimd.tensor_scalar(y_raw[0][:, t, :], y_raw[0][:, t, :], wu[0][:, t : t + 1], 0.0, ALU.mult, ALU.add)
         deal_x(1, nc.scalar.copy)
         nc.scalar.activation(y_raw[0][:, 3, :], y_raw[0][:, 3, :], ACT.Copy, scale=wu[0][:, 3:4])
+        window1 = zero("window1", "x_raw1")
+        windows = [window0, window1, window2]
         scores_direct(0, acc1)
         recip(0, 0, 2)
         quantise(qx_d[1], x_d[1], E4M3)
@@ -243,6 +247,9 @@ def tile_attend_gheads_sm_kernel(tc, x1, x2, wT, y1, u1, w1, y2, u2, w2, ts, off
         fold(3, 4)
         diff(0, 2, cinv)
         diff(0, 3, cinv)
+        qx_r[0] = codes("qx_r0", "w_plane3")
+        quantise_x(0, 0, 256)
+        quantise_x(0, 256, 512)
         hb = [bank(c, "hT%d" % c) for c in range(4)]
         for t in range(PACK):
             turn_add(work[0], t, True, True)

@@ -38,14 +38,15 @@ def tile_attend_gheads_sm_kernel(tc, x1, x2, wT, y1, u1, w1, y2, u2, w2, ts, off
         offsets = keep.tile([P, S // 16], U16, name="offsets")
         x_raw = [keep.tile([P, PACK, R], F32, name="x_raw%d" % h, align_bytes=64) for h in heads]
         w_plane = [keep.tile([P, T], F32, name="w_plane%d" % j, align_bytes=64) for j in range(PACK)]
-        y_raw = [keep.tile([P, PACK, S], F32, name="y_raw%d" % h) for h in heads]
+        y_raw = [keep.tile([P, PACK, S], F32, name="y_raw%d" % h, align_bytes=64) for h in heads]
         w_view = wT.rearrange("(p j) n -> j p n", j=PACK)
         ts_win = keep.tile([P, T], F32, name="ts_win")
         nc.vector.memset(ts_win[:].bitcast(U32), 0)
-        nc.sync.dma_start(x_raw[0][:], xs[0].rearrange("(p j) r -> p j r", j=PACK))
+        nc.sync.dma_start(w_plane[0][:], w_view[0])
         nc.sync.dma_start(offsets[:], offs)
         nc.sync.dma_start(ts_win[0:1, :], ts[0:1, :])
-        for j in range(PACK):
+        nc.sync.dma_start(x_raw[0][:], xs[0].rearrange("(p j) r -> p j r", j=PACK))
+        for j in range(1, PACK):
             nc.sync.dma_start(w_plane[j][:], w_view[j])
         u_col = [keep.tile([P, PACK], F32, name="u_col%d" % h) for h in heads]
         w_col = [keep.tile([P, PACK], F32, name="w_col%d" % h) for h in heads]
@@ -63,11 +64,15 @@ def tile_attend_gheads_sm_kernel(tc, x1, x2, wT, y1, u1, w1, y2, u2, w2, ts, off
         nc.gpsimd.tensor_scalar(neg_u[:], u_col[1][:], -1.0, 0.0, ALU.mult, ALU.add)
         nc.gpsimd.tensor_tensor(wu[1][:], u_col[1][:], w_col[1][:], ALU.mult)
         nc.gpsimd.tensor_tensor(wu[0][:], u_col[0][:], w_col[0][:], ALU.mult)
+        neg_wu = keep.tile([P, PACK], F32, name="neg_wu")
+        nc.gpsimd.tensor_scalar(neg_wu[:], wu[0][:], -1.0, 0.0, ALU.mult, ALU.add)
 
         warm = keep.tile([P, 1], F32, name="warm")
         nc.scalar.activation(warm[:], ident[:, 0:1], ACT.Exp)
         window2 = keep.tile([P, T], F32, name="window2")
         nc.vector.memset(window2[:].bitcast(U32), 0)
+        window1 = keep.tile([P, T], F32, name="window1")
+        nc.vector.memset(window1[:].bitcast(U32), 0)
 
         def codes(name, tag=None):
             c = keep.tile([P, 512], U32, name=name + "_c", tag=tag or name + "_c", align_bytes=64)
@@ -82,14 +87,15 @@ def tile_attend_gheads_sm_kernel(tc, x1, x2, wT, y1, u1, w1, y2, u2, w2, ts, off
                                 rhs=rhs[0][:].bitcast(rfmt), rhs_scale=rhs[1][:], start=start, stop=stop)
 
         x_d = [keep.tile([P, R * PACK], BF16, name="x_d%d" % h, align_bytes=64) for h in heads]
-        x_r = [[keep.tile([P, 1024], BF16, name="x_r0%d" % u, align_bytes=64) for u in range(2)], [None, keep.tile([P, 1024], BF16, name="x_r11", align_bytes=64)]]
+        x_r = [[keep.tile([P, 1024], BF16, name="x_r0%d" % u, align_bytes=64) for u in range(2)], [keep.tile([P, 1024], BF16, name="x_r1%d" % u, align_bytes=64) for u in range(2)]]
         qx_d = [codes("qx_d%d" % h) for h in heads]
         qx_r = [None, codes("qx_r1")]
         qg = [codes("qg%d" % h) for h in heads]
         qw = codes("qw")
 
-        def deal_x(h, copy):
-            copy(x_d[h][:].rearrange("p (t s j) -> p s t j", t=PACK, j=PACK), x_raw[h][:].rearrange("p j (s t) -> p s t j", t=PACK))
+        def deal_x(h, copy, lo=0, hi=PACK):
+            copy(x_d[h][:].rearrange("p (t s j) -> p s t j", t=PACK, j=PACK)[:, :, lo:hi, :],
+                 x_raw[h][:].rearrange("p j (s t) -> p s t j", t=PACK)[:, :, lo:hi, :])
 
         def turn_x(h, u, b):
             words = x_d[h][:].bitcast(F32)
@@ -108,7 +114,6 @@ def tile_attend_gheads_sm_kernel(tc, x1, x2, wT, y1, u1, w1, y2, u2, w2, ts, off
 
         ts_row = keep.tile([P, S], F32, name="ts_row")
         nc.vector.tensor_copy(ts_row[:], ts_win[:].indirect(offsets[:]))
-        deal_x(0, nc.scalar.copy)
         bk = bank(0, "ts_turned")
         for c in range(4):
             nc.tensor.transpose(bk[:, c * P : (c + 1) * P], ts_row[:, c * P : (c + 1) * P], ident[:])
@@ -125,6 +130,7 @@ def tile_attend_gheads_sm_kernel(tc, x1, x2, wT, y1, u1, w1, y2, u2, w2, ts, off
         w_d = keep.tile([P, S, PACK], BF16, name="w_d", align_bytes=64)
         w_flat = w_d[:].rearrange("p i j -> p (i j)")
         nc.vector.tensor_copy(w_d[:, :, 0], w_plane[0][:].indirect(offsets[:]))
+        deal_x(0, nc.vector.tensor_copy)
         quantise(qx_d[0], x_d[0], E4M3)
         for u in range(2):
             weave_x(0, u, turn_x(0, u, 2 + u))
@@ -144,28 +150,25 @@ def tile_attend_gheads_sm_kernel(tc, x1, x2, wT, y1, u1, w1, y2, u2, w2, ts, off
                                     lhsT_scale=qx_d[0][1][:, t * P : (t + 1) * P], rhs=qw[0][:, half * 256 : (half + 1) * 256].bitcast(E4M3),
                                     rhs_scale=qw[1][:, half * 256 : (half + 1) * 256], start=True, stop=True)
 
-        work = [keep.tile([P, PACK, S], F32, name="work%d" % h) for h in heads]
+        work = [keep.tile([P, PACK, S], F32, name="work%d" % h, align_bytes=64) for h in heads]
         neg_m = [keep.tile([P, PACK], F32, name="neg_m%d" % h) for h in heads]
-        total = [keep.tile([P, PACK], F32, name="total%d" % h) for h in heads]
+        total = [None, keep.tile([P, PACK], F32, name="total1")]
         inv = [keep.tile([P, PACK], F32, name="inv%d" % h) for h in heads]
         g = [keep.tile([P, S * PACK], BF16, name="g%d" % h, align_bytes=64) for h in heads]
         g_t = [keep.tile([P, R], BF16, name="g_t%d" % c, align_bytes=64) for c in range(4)]
-        cinv = keep.tile([P, PACK], F32, name="cinv")
         turned = keep.tile([P, 4, R], F32, name="turned")
 
         def expo(h, t):
             nc.scalar.activation(work[h][:, t, :], work[h][:, t, :], ACT.Exp, bias=neg_m[h][:, t : t + 1], scale=(1.0, -1.0)[h],
                                  accum_out=total[h][:, t : t + 1])
 
-        def scores_direct(h, acc):
-            for t in range(PACK):
-                nc.vector.scalar_tensor_tensor(work[h][:, t, 0:256], acc[t // 2][:, (t % 2) * 256 : (t % 2 + 1) * 256], u_col[h][:, t : t + 1], ts_all[:, 0:256], ALU.mult, ALU.mult)
-            for t in range(PACK + 1):
-                if t < PACK:
-                    nc.vector.scalar_tensor_tensor(work[h][:, t, 256:512], acc[2 + t // 2][:, (t % 2) * 256 : (t % 2 + 1) * 256], u_col[h][:, t : t + 1], ts_all[:, 256:512], ALU.mult, ALU.mult)
-                if t > 0:
-                    nc.vector.tensor_reduce(neg_m[h][:, t - 1 : t], work[h][:, t - 1, :], AX.X, ALU.max, negate=True)
-                    expo(h, t - 1)
+        def scale_direct(h, acc, half, t):
+            cols = slice(half * 256, (half + 1) * 256)
+            nc.vector.scalar_tensor_tensor(work[h][:, t, cols], acc[2 * half + t // 2][:, (t % 2) * 256 : (t % 2 + 1) * 256], u_col[h][:, t : t + 1],
+                                           ts_all[:, cols], ALU.mult, ALU.mult)
+
+        def max_direct(h, t):
+            nc.vector.tensor_reduce(neg_m[h][:, t : t + 1], work[h][:, t, :], AX.X, ALU.max, negate=True)
 
         def scores_turned(h, banks_a, banks_s):
             for c in range(4):
@@ -182,13 +185,9 @@ def tile_attend_gheads_sm_kernel(tc, x1, x2, wT, y1, u1, w1, y2, u2, w2, ts, off
             for t in range(PACK):
                 nc.vector.tensor_scalar(work[h][:, t, :], sb[t][:], neg_u[:, t : t + 1], None, ALU.mult, ALU.min,
                                         accum_out=neg_m[h][:, t : t + 1])
-                expo(h, t)
 
         def recip(h, lo, hi):
             nc.vector.reciprocal(inv[h][:, lo:hi], total[h][:, lo:hi])
-
-        def fold(lo, hi):
-            nc.vector.tensor_tensor(cinv[:, lo:hi], inv[0][:, lo:hi], wu[0][:, lo:hi], ALU.mult)
 
         def diff(h, t, col, op=ALU.subtract):
             nc.vector.scalar_tensor_tensor(work[h][:, t, :], work[h][:, t, :], col[:, t : t + 1], y_raw[h][:, t, :], ALU.mult, op)
@@ -199,14 +198,14 @@ def tile_attend_gheads_sm_kernel(tc, x1, x2, wT, y1, u1, w1, y2, u2, w2, ts, off
 
         def turn_g():
             for c in range(4):
-                nc.scalar.activation(g_t[c][:].rearrange("i (s t) -> i s t", t=PACK), hb[c][:].rearrange("i (t s) -> i s t", t=PACK),
+                nc.scalar.activation(g_t[c][:].rearrange("i (u s e) -> i u s e", u=2, e=2), hb[c][:].rearrange("i (u e s) -> i u s e", u=2, e=2),
                                      ACT.Copy, scale=ts_col[:, c : c + 1])
             for pair in range(2):
                 bk = bank(4 + pair, "gw%d" % pair)
                 for k in range(2):
                     words = g_t[2 * pair + k][:].bitcast(F32)
                     for u in range(2):
-                        nc.tensor.transpose(bk[:, (2 * k + u) * P : (2 * k + u + 1) * P], words[:, u:256:2], ident[:])
+                        nc.tensor.transpose(bk[:, (2 * k + u) * P : (2 * k + u + 1) * P], words[:, u * P : (u + 1) * P], ident[:])
                 nc.scalar.copy(g[0][:, pair * 1024 : (pair + 1) * 1024].bitcast(F32).rearrange("s (k i u) -> s k i u", k=2, u=2),
                                bk[:].rearrange("s (k u i) -> s k i u", k=2, u=2))
 
@@ -224,36 +223,39 @@ def tile_attend_gheads_sm_kernel(tc, x1, x2, wT, y1, u1, w1, y2, u2, w2, ts, off
                 nc.gpsimd.memset(win[:, k * 512 : (k + 1) * 512], 0.0)
             return win
 
-        window0 = zero("window0", "w_d")
-        for t in range(PACK - 1):
-            nc.gpsimd.tensor_scalar(y_raw[0][:, t, :], y_raw[0][:, t, :], wu[0][:, t : t + 1], 0.0, ALU.mult, ALU.add)
-        deal_x(1, nc.scalar.copy)
-        nc.scalar.activation(y_raw[0][:, 3, :], y_raw[0][:, 3, :], ACT.Copy, scale=wu[0][:, 3:4])
-        window1 = zero("window1", "x_raw1")
-        windows = [window0, window1, window2]
-        scores_direct(0, acc1)
-        recip(0, 0, 2)
+        deal_x(1, nc.scalar.copy, 2, 4)
+        deal_x(1, nc.vector.tensor_copy, 0, 2)
         quantise(qx_d[1], x_d[1], E4M3)
-        fold(0, 2)
-        sb = scores_turned(1, (4, 5, 6, 7), (4, 5, 6, 7))
-        xw = turn_x(1, 0, 0)
-        x_r[1][0] = keep.tile([P, 1024], BF16, name="x_r10", tag="ts_col2", align_bytes=64)
-        weave_x(1, 0, xw)
-        recip(0, 2, 3)
-        diff(0, 0, cinv)
-        fold(2, 3)
-        recip(0, 3, 4)
-        diff(0, 1, cinv)
-        fold(3, 4)
-        diff(0, 2, cinv)
-        diff(0, 3, cinv)
+        weave_x(1, 0, turn_x(1, 0, 4))
+        y_neg = keep.tile([P, PACK, S], F32, name="y_neg", tag="x_raw1", align_bytes=64)
+        for t in range(PACK):
+            nc.gpsimd.tensor_scalar(y_neg[:, t, :], y_raw[0][:, t, :], neg_wu[:, t : t + 1], 0.0, ALU.mult, ALU.add)
+        for half in range(2):
+            for t in range(PACK):
+                scale_direct(0, acc1, half, t)
+        sb = scores_turned(1, (5, 6, 7, 4), (5, 6, 7, 4))
+        total[0] = keep.tile([P, PACK], F32, name="total0", tag="ts_col2", align_bytes=64)
+        for t in range(PACK):
+            max_direct(0, t)
+        hb = [bank(c, "hT%d" % c) for c in range(4)]
+        for t in range(PACK):
+            turn_add(y_neg, t, t == 0, False)
+        for t in range(PACK):
+            expo(0, t)
+        recip(0, 0, 1)
+        recip(0, 1, 2)
+        max_turned(1, sb)
+        recip(0, 2, 4)
+        for t in range(PACK):
+            expo(1, t)
+        for t in range(PACK):
+            engine = nc.gpsimd if t < 2 else nc.vector
+            engine.tensor_scalar(work[0][:, t, :], work[0][:, t, :], inv[0][:, t : t + 1], wu[0][:, t : t + 1], ALU.mult, ALU.mult)
+            turn_add(work[0], t, False, t == PACK - 1)
+        windows = [window1, window2, zero("window0", "work0")]
         qx_r[0] = codes("qx_r0", "w_plane3")
         quantise_x(0, 0, 256)
         quantise_x(0, 256, 512)
-        hb = [bank(c, "hT%d" % c) for c in range(4)]
-        for t in range(PACK):
-            turn_add(work[0], t, True, True)
-        max_turned(1, sb)
         turn_g()
         weave_x(1, 1, turn_x(1, 1, 4))
         recip(1, 0, 2)
@@ -274,12 +276,12 @@ def tile_attend_gheads_sm_kernel(tc, x1, x2, wT, y1, u1, w1, y2, u2, w2, ts, off
         dw = [keep.tile([P, S], F32, name="dw%d" % j) for j in range(PACK)]
         out_view = out.rearrange("(p j) n -> j p n", j=PACK)
         for j in range(PACK):
-            acc = bank(j, "dw%d" % j)
+            acc = bank(0, "dw%d" % j)
             mm(acc[:], qx_r[1], j * P, E4M3, qg[1], E5M2, True, False)
             mm(acc[:], qx_r[0], j * P, E4M3, qg[0], E5M2, False, True)
-            nc.scalar.copy(dw[j][:], acc[:])
             if j == 0:
                 quantise_x(1, 256, 512)
             win = windows[j % WINDOWS]
+            nc.scalar.copy(dw[j][:], acc[:])
             nc.vector.tensor_copy(win[:].indirect(offsets[:]), dw[j][:])
             nc.sync.dma_start(out_view[j], win[:])

@@ -42,11 +42,10 @@ def tile_attend_gheads_sm_kernel(tc, x1, x2, wT, y1, u1, w1, y2, u2, w2, ts, off
         w_view = wT.rearrange("(p j) n -> j p n", j=PACK)
         ts_win = keep.tile([P, T], F32, name="ts_win")
         nc.vector.memset(ts_win[:].bitcast(U32), 0)
-        nc.sync.dma_start(w_plane[0][:], w_view[0])
+        nc.sync.dma_start(x_raw[0][:], xs[0].rearrange("(p j) r -> p j r", j=PACK))
         nc.sync.dma_start(offsets[:], offs)
         nc.sync.dma_start(ts_win[0:1, :], ts[0:1, :])
-        nc.sync.dma_start(x_raw[0][:], xs[0].rearrange("(p j) r -> p j r", j=PACK))
-        for j in range(1, PACK):
+        for j in range(PACK):
             nc.sync.dma_start(w_plane[j][:], w_view[j])
         u_col = [keep.tile([P, PACK], F32, name="u_col%d" % h) for h in heads]
         w_col = [keep.tile([P, PACK], F32, name="w_col%d" % h) for h in heads]
@@ -74,9 +73,9 @@ def tile_attend_gheads_sm_kernel(tc, x1, x2, wT, y1, u1, w1, y2, u2, w2, ts, off
         window1 = keep.tile([P, T], F32, name="window1")
         nc.vector.memset(window1[:].bitcast(U32), 0)
 
-        def codes(name, tag=None):
-            c = keep.tile([P, 512], U32, name=name + "_c", tag=tag or name + "_c", align_bytes=64)
-            s = keep.tile([P, 512], U8, name=name + "_s", align_bytes=64)
+        def codes(name, width=512, tag=None):
+            c = keep.tile([P, width], U32, name=name + "_c", tag=tag or name + "_c", align_bytes=64)
+            s = keep.tile([P, width], U8, name=name + "_s", align_bytes=64)
             return c, s
 
         def quantise(q, src, fmt, lo=0, hi=512):
@@ -89,7 +88,7 @@ def tile_attend_gheads_sm_kernel(tc, x1, x2, wT, y1, u1, w1, y2, u2, w2, ts, off
         x_d = [keep.tile([P, R * PACK], BF16, name="x_d%d" % h, align_bytes=64) for h in heads]
         x_r = [[keep.tile([P, 1024], BF16, name="x_r0%d" % u, align_bytes=64) for u in range(2)], [keep.tile([P, 1024], BF16, name="x_r1%d" % u, align_bytes=64) for u in range(2)]]
         qx_d = [codes("qx_d%d" % h) for h in heads]
-        qx_r = [None, codes("qx_r1")]
+        qx_r = [[None, None], [codes("qx_r1%d" % u, 256) for u in range(2)]]
         qg = [codes("qg%d" % h) for h in heads]
         qw = codes("qw")
 
@@ -107,13 +106,12 @@ def tile_attend_gheads_sm_kernel(tc, x1, x2, wT, y1, u1, w1, y2, u2, w2, ts, off
         def weave_x(h, u, bk):
             nc.scalar.copy(x_r[h][u][:].rearrange("s (e p t) -> s e p t", e=2, t=PACK), bk[:].bitcast(BF16).rearrange("s (t p e) -> s e p t", t=PACK, e=2))
 
-        def quantise_x(h, lo, hi):
-            u = lo // 256
-            nc.vector.quantize_mx(out=qx_r[h][0][:, lo:hi].bitcast(E4M3), scales=qx_r[h][1][:, lo:hi],
-                                  in_=x_r[h][u][:, PACK * (lo - 256 * u) : PACK * (hi - 256 * u)])
+        def quantise_x(h, u, lo=0, hi=256):
+            quantise(qx_r[h][u], x_r[h][u], E4M3, lo, hi)
 
         ts_row = keep.tile([P, S], F32, name="ts_row")
         nc.vector.tensor_copy(ts_row[:], ts_win[:].indirect(offsets[:]))
+        deal_x(0, nc.scalar.copy)
         bk = bank(0, "ts_turned")
         for c in range(4):
             nc.tensor.transpose(bk[:, c * P : (c + 1) * P], ts_row[:, c * P : (c + 1) * P], ident[:])
@@ -124,13 +122,12 @@ def tile_attend_gheads_sm_kernel(tc, x1, x2, wT, y1, u1, w1, y2, u2, w2, ts, off
         bk = bank(1, "ts_spread")
         for c in range(4):
             nc.tensor.transpose(bk[:, c * P : (c + 1) * P], ts_col[:, c : c + 1].to_broadcast([P, P]), ident[:])
-        ts_all = keep.tile([P, S], F32, name="ts_all")
+        ts_all = keep.tile([P, S], F32, name="ts_all", align_bytes=64)
         nc.scalar.copy(ts_all[:], bk[:])
 
         w_d = keep.tile([P, S, PACK], BF16, name="w_d", align_bytes=64)
         w_flat = w_d[:].rearrange("p i j -> p (i j)")
         nc.vector.tensor_copy(w_d[:, :, 0], w_plane[0][:].indirect(offsets[:]))
-        deal_x(0, nc.vector.tensor_copy)
         quantise(qx_d[0], x_d[0], E4M3)
         for u in range(2):
             weave_x(0, u, turn_x(0, u, 2 + u))
@@ -139,6 +136,8 @@ def tile_attend_gheads_sm_kernel(tc, x1, x2, wT, y1, u1, w1, y2, u2, w2, ts, off
             nc.scalar.activation(factor[:, t, :], ts_all[:], ACT.Copy, scale=wu[1][:, t : t + 1])
         nc.vector.tensor_copy(w_d[:, :, 1], w_plane[1][:].indirect(offsets[:]))
         nc.vector.tensor_copy(w_d[:, :, 2], w_plane[2][:].indirect(offsets[:]))
+        qx_r[0][0] = codes("qx_r00", 256, "w_plane2")
+        quantise_x(0, 0)
         acc1 = []
         for half in range(2):
             nc.vector.tensor_copy(w_d[:, half * 256 : (half + 1) * 256, 3], w_plane[3][:].indirect(offsets[:, half * 16 : (half + 1) * 16]))
@@ -227,12 +226,12 @@ def tile_attend_gheads_sm_kernel(tc, x1, x2, wT, y1, u1, w1, y2, u2, w2, ts, off
         deal_x(1, nc.vector.tensor_copy, 0, 2)
         quantise(qx_d[1], x_d[1], E4M3)
         weave_x(1, 0, turn_x(1, 0, 4))
-        y_neg = keep.tile([P, PACK, S], F32, name="y_neg", tag="x_raw1", align_bytes=64)
-        for t in range(PACK):
-            nc.gpsimd.tensor_scalar(y_neg[:, t, :], y_raw[0][:, t, :], neg_wu[:, t : t + 1], 0.0, ALU.mult, ALU.add)
         for half in range(2):
             for t in range(PACK):
                 scale_direct(0, acc1, half, t)
+        y_neg = keep.tile([P, PACK, S], F32, name="y_neg", tag="ts_all", align_bytes=64)
+        for t in range(PACK):
+            nc.gpsimd.tensor_scalar(y_neg[:, t, :], y_raw[0][:, t, :], neg_wu[:, t : t + 1], 0.0, ALU.mult, ALU.add)
         sb = scores_turned(1, (5, 6, 7, 4), (5, 6, 7, 4))
         total[0] = keep.tile([P, PACK], F32, name="total0", tag="ts_col2", align_bytes=64)
         for t in range(PACK):
@@ -242,20 +241,15 @@ def tile_attend_gheads_sm_kernel(tc, x1, x2, wT, y1, u1, w1, y2, u2, w2, ts, off
             turn_add(y_neg, t, t == 0, False)
         for t in range(PACK):
             expo(0, t)
-        recip(0, 0, 1)
-        recip(0, 1, 2)
         max_turned(1, sb)
+        recip(0, 0, 2)
         recip(0, 2, 4)
         for t in range(PACK):
             expo(1, t)
         for t in range(PACK):
-            engine = nc.gpsimd if t < 2 else nc.vector
-            engine.tensor_scalar(work[0][:, t, :], work[0][:, t, :], inv[0][:, t : t + 1], wu[0][:, t : t + 1], ALU.mult, ALU.mult)
+            nc.vector.tensor_scalar(work[0][:, t, :], work[0][:, t, :], inv[0][:, t : t + 1], wu[0][:, t : t + 1], ALU.mult, ALU.mult)
             turn_add(work[0], t, False, t == PACK - 1)
         windows = [window1, window2, zero("window0", "work0")]
-        qx_r[0] = codes("qx_r0", "w_plane3")
-        quantise_x(0, 0, 256)
-        quantise_x(0, 256, 512)
         turn_g()
         weave_x(1, 1, turn_x(1, 1, 4))
         recip(1, 0, 2)
@@ -265,22 +259,24 @@ def tile_attend_gheads_sm_kernel(tc, x1, x2, wT, y1, u1, w1, y2, u2, w2, ts, off
         recip(1, 3, 4)
         diff(1, 2, inv[1])
         diff(1, 3, inv[1])
-        quantise_x(1, 0, 128)
+        quantise_x(1, 0, 0, 128)
         weave(0, 256)
         weave(256, 512)
         quantise(qg[1], g[1], E5M2, 0, 256)
         quantise(qg[1], g[1], E5M2, 256, 512)
         quantise(qg[0], g[0], E5M2)
-        quantise_x(1, 128, 256)
+        quantise_x(1, 0, 128, 256)
+        qx_r[0][1] = codes("qx_r01", 256, "g0")
+        quantise_x(0, 1)
 
         dw = [keep.tile([P, S], F32, name="dw%d" % j) for j in range(PACK)]
         out_view = out.rearrange("(p j) n -> j p n", j=PACK)
         for j in range(PACK):
             acc = bank(0, "dw%d" % j)
-            mm(acc[:], qx_r[1], j * P, E4M3, qg[1], E5M2, True, False)
-            mm(acc[:], qx_r[0], j * P, E4M3, qg[0], E5M2, False, True)
+            mm(acc[:], qx_r[1][j // 2], j % 2 * P, E4M3, qg[1], E5M2, True, False)
+            mm(acc[:], qx_r[0][j // 2], j % 2 * P, E4M3, qg[0], E5M2, False, True)
             if j == 0:
-                quantise_x(1, 256, 512)
+                quantise_x(1, 1)
             win = windows[j % WINDOWS]
             nc.scalar.copy(dw[j][:], acc[:])
             nc.vector.tensor_copy(win[:].indirect(offsets[:]), dw[j][:])

@@ -66,8 +66,6 @@ def tile_attend_gheads_sm_kernel(tc, x1, x2, wT, y1, u1, w1, y2, u2, w2, ts, off
         neg_wu = keep.tile([P, PACK], F32, name="neg_wu")
         nc.gpsimd.tensor_scalar(neg_wu[:], wu[0][:], -1.0, 0.0, ALU.mult, ALU.add)
 
-        warm = keep.tile([P, 1], F32, name="warm")
-        nc.scalar.activation(warm[:], ident[:, 0:1], ACT.Exp)
         window2 = keep.tile([P, T], F32, name="window2")
         nc.vector.memset(window2[:].bitcast(U32), 0)
         window1 = keep.tile([P, T], F32, name="window1")
@@ -88,7 +86,7 @@ def tile_attend_gheads_sm_kernel(tc, x1, x2, wT, y1, u1, w1, y2, u2, w2, ts, off
         x_d = [keep.tile([P, R * PACK], BF16, name="x_d%d" % h, align_bytes=64) for h in heads]
         x_r = [[keep.tile([P, 1024], BF16, name="x_r0%d" % u, align_bytes=64) for u in range(2)], [keep.tile([P, 1024], BF16, name="x_r1%d" % u, align_bytes=64) for u in range(2)]]
         qx_d = [codes("qx_d%d" % h) for h in heads]
-        qx_r = [[None, None], [codes("qx_r1%d" % u, 256) for u in range(2)]]
+        qx_r = [[None, None], [None, codes("qx_r11", 256)]]
         qg = [codes("qg%d" % h) for h in heads]
         qw = codes("qw")
 
@@ -131,7 +129,7 @@ def tile_attend_gheads_sm_kernel(tc, x1, x2, wT, y1, u1, w1, y2, u2, w2, ts, off
         quantise(qx_d[0], x_d[0], E4M3)
         for u in range(2):
             weave_x(0, u, turn_x(0, u, 2 + u))
-        factor = keep.tile([P, PACK, S], F32, name="factor")
+        factor = keep.tile([P, PACK, S], F32, name="factor", align_bytes=64)
         for t in range(PACK):
             nc.scalar.activation(factor[:, t, :], ts_all[:], ACT.Copy, scale=wu[1][:, t : t + 1])
         nc.vector.tensor_copy(w_d[:, :, 1], w_plane[1][:].indirect(offsets[:]))
@@ -259,9 +257,10 @@ def tile_attend_gheads_sm_kernel(tc, x1, x2, wT, y1, u1, w1, y2, u2, w2, ts, off
         recip(1, 3, 4)
         diff(1, 2, inv[1])
         diff(1, 3, inv[1])
-        quantise_x(1, 0, 0, 128)
         weave(0, 256)
         weave(256, 512)
+        qx_r[1][0] = codes("qx_r10", 256, "factor")
+        quantise_x(1, 0, 0, 128)
         quantise(qg[1], g[1], E5M2, 0, 256)
         quantise(qg[1], g[1], E5M2, 256, 512)
         quantise(qg[0], g[0], E5M2)

@@ -86,9 +86,12 @@ def tile_attend_gheads_sm_kernel(tc, x1, x2, wT, y1, u1, w1, y2, u2, w2, ts, off
         x_d = [keep.tile([P, R * PACK], BF16, name="x_d%d" % h, align_bytes=64) for h in heads]
         x_r = [[keep.tile([P, 1024], BF16, name="x_r0%d" % u, align_bytes=64) for u in range(2)], [keep.tile([P, 1024], BF16, name="x_r1%d" % u, align_bytes=64) for u in range(2)]]
         qx_d = [codes("qx_d%d" % h) for h in heads]
-        qx_r = [[None, None], [None, codes("qx_r11", 256)]]
+        qx_r = [[None, None], [None, None]]
         qg = [codes("qg%d" % h) for h in heads]
         qw = codes("qw")
+        for h in heads:
+            nc.gpsimd.memset(qg[h][0][:, 256:S], 0)
+            nc.gpsimd.memset(qg[h][1][:, 256:S].bitcast(U32), 0)
 
         def deal_x(h, copy, lo=0, hi=PACK):
             copy(x_d[h][:].rearrange("p (t s j) -> p s t j", t=PACK, j=PACK)[:, :, lo:hi, :],
@@ -257,26 +260,36 @@ def tile_attend_gheads_sm_kernel(tc, x1, x2, wT, y1, u1, w1, y2, u2, w2, ts, off
         recip(1, 3, 4)
         diff(1, 2, inv[1])
         diff(1, 3, inv[1])
+        qx_r[1][0] = codes("qx_r10", 256, "y_raw1")
         weave(0, 256)
-        weave(256, 512)
-        qx_r[1][0] = codes("qx_r10", 256, "factor")
-        quantise_x(1, 0, 0, 128)
+        quantise_x(1, 0)
         quantise(qg[1], g[1], E5M2, 0, 256)
-        quantise(qg[1], g[1], E5M2, 256, 512)
-        quantise(qg[0], g[0], E5M2)
-        quantise_x(1, 0, 128, 256)
-        qx_r[0][1] = codes("qx_r01", 256, "g0")
-        quantise_x(0, 1)
+        quantise(qg[0], g[0], E5M2, 0, 256)
 
-        dw = [keep.tile([P, S], F32, name="dw%d" % j) for j in range(PACK)]
         out_view = out.rearrange("(p j) n -> j p n", j=PACK)
-        for j in range(PACK):
-            acc = bank(0, "dw%d" % j)
+
+        def result(j, lo, hi, b):
+            acc = bank(b, "dw%d_%d" % (j, lo))
             mm(acc[:], qx_r[1][j // 2], j % 2 * P, E4M3, qg[1], E5M2, True, False)
             mm(acc[:], qx_r[0][j // 2], j % 2 * P, E4M3, qg[0], E5M2, False, True)
-            if j == 0:
-                quantise_x(1, 1)
-            win = windows[j % WINDOWS]
-            nc.scalar.copy(dw[j][:], acc[:])
-            nc.vector.tensor_copy(win[:].indirect(offsets[:]), dw[j][:])
-            nc.sync.dma_start(out_view[j], win[:])
+            dw = keep.tile([P, hi - lo], F32, name="dw%d_%d" % (j, lo))
+            nc.scalar.copy(dw[:], acc[:, lo:hi])
+            return dw
+
+        def scatter(j, lo, hi, dw):
+            nc.vector.tensor_copy(windows[j % WINDOWS][:].indirect(offsets[:, lo // 16 : hi // 16]), dw[:])
+
+        early = [result(j, 0, 256, 6 + j) for j in range(2)]
+        weave(256, 512)
+        qx_r[0][1] = codes("qx_r01", 256, "factor")
+        quantise_x(0, 1)
+        scatter(0, 0, 256, early[0])
+        quantise(qg[1], g[1], E5M2, 256, S)
+        quantise(qg[0], g[0], E5M2, 256, S)
+        qx_r[1][1] = codes("qx_r11", 256, "g1")
+        quantise_x(1, 1)
+        scatter(1, 0, 256, early[1])
+        for j in range(PACK):
+            lo = 256 if j < 2 else 0
+            scatter(j, lo, S, result(j, lo, S, 6 + j % 2))
+            nc.sync.dma_start(out_view[j], windows[j % WINDOWS][:])

@@ -12,7 +12,6 @@ E4M3 = mybir.dt.float8_e4m3fn_x4
 E5M2 = mybir.dt.float8_e5m2_x4
 ALU = mybir.AluOpType
 ACT = mybir.ActivationFunctionType
-AX = mybir.AxisListType
 
 P = 128
 PACK = 4
@@ -36,7 +35,7 @@ def tile_attend_gheads_sm_kernel(tc, x1, x2, wT, y1, u1, w1, y2, u2, w2, ts, off
             return psum.tile([P, 512], F32, name=name, tag="bank%d" % b)
 
         offsets = keep.tile([P, S // 16], U16, name="offsets")
-        x_raw = [keep.tile([P, PACK, R], F32, name="x_raw%d" % h, align_bytes=64) for h in heads]
+        x_raw = [keep.tile([P, PACK, R], F32, name="x_raw%d" % h, tag="x_raw%d" % h, align_bytes=64) for h in heads]
         w_plane = [keep.tile([P, T], F32, name="w_plane%d" % j, align_bytes=64) for j in range(PACK)]
         y_raw = [keep.tile([P, PACK, S], F32, name="y_raw%d" % h, align_bytes=64) for h in heads]
         w_view = wT.rearrange("(p j) n -> j p n", j=PACK)
@@ -150,7 +149,7 @@ def tile_attend_gheads_sm_kernel(tc, x1, x2, wT, y1, u1, w1, y2, u2, w2, ts, off
                                     lhsT_scale=qx_d[0][1][:, t * P : (t + 1) * P], rhs=qw[0][:, half * 256 : (half + 1) * 256].bitcast(E4M3),
                                     rhs_scale=qw[1][:, half * 256 : (half + 1) * 256], start=True, stop=True)
 
-        work = [keep.tile([P, PACK, S], F32, name="work%d" % h, align_bytes=64) for h in heads]
+        work = [None, keep.tile([P, PACK, S], F32, name="work1", align_bytes=64)]
         neg_m = [keep.tile([P, PACK], F32, name="neg_m%d" % h) for h in heads]
         total = [None, keep.tile([P, PACK], F32, name="total1")]
         inv = [keep.tile([P, PACK], F32, name="inv%d" % h) for h in heads]
@@ -159,7 +158,7 @@ def tile_attend_gheads_sm_kernel(tc, x1, x2, wT, y1, u1, w1, y2, u2, w2, ts, off
         turned = keep.tile([P, 4, R], F32, name="turned")
 
         def expo(h, t):
-            nc.scalar.activation(work[h][:, t, :], work[h][:, t, :], ACT.Exp, bias=neg_m[h][:, t : t + 1], scale=(1.0, -1.0)[h],
+            nc.scalar.activation(work[h][:, t, :], work[h][:, t, :], ACT.Exp, bias=neg_m[h][:, t : t + 1], scale=-1.0,
                                  accum_out=total[h][:, t : t + 1])
 
         def scale_direct(h, acc, half, t):
@@ -168,7 +167,7 @@ def tile_attend_gheads_sm_kernel(tc, x1, x2, wT, y1, u1, w1, y2, u2, w2, ts, off
                                            ts_all[:, cols], ALU.mult, ALU.mult)
 
         def max_direct(h, t):
-            nc.vector.tensor_reduce(neg_m[h][:, t : t + 1], work[h][:, t, :], AX.X, ALU.max, negate=True)
+            nc.vector.tensor_scalar(work[h][:, t, :], work[h][:, t, :], -1.0, None, ALU.mult, ALU.min, accum_out=neg_m[h][:, t : t + 1])
 
         def scores_turned(h, banks_a, banks_s):
             for c in range(4):
@@ -223,10 +222,12 @@ def tile_attend_gheads_sm_kernel(tc, x1, x2, wT, y1, u1, w1, y2, u2, w2, ts, off
                 nc.gpsimd.memset(win[:, k * 512 : (k + 1) * 512], 0.0)
             return win
 
-        deal_x(1, nc.scalar.copy, 2, 4)
+        deal_x(1, nc.scalar.copy, 3, 4)
         deal_x(1, nc.vector.tensor_copy, 0, 2)
+        deal_x(1, nc.vector.tensor_copy, 2, 3)
         quantise(qx_d[1], x_d[1], E4M3)
         weave_x(1, 0, turn_x(1, 0, 4))
+        work[0] = keep.tile([P, PACK, S], F32, name="work0", tag="x_raw1", align_bytes=64)
         for half in range(2):
             for t in range(PACK):
                 scale_direct(0, acc1, half, t)
@@ -250,7 +251,7 @@ def tile_attend_gheads_sm_kernel(tc, x1, x2, wT, y1, u1, w1, y2, u2, w2, ts, off
         for t in range(PACK):
             nc.vector.tensor_scalar(work[0][:, t, :], work[0][:, t, :], inv[0][:, t : t + 1], wu[0][:, t : t + 1], ALU.mult, ALU.mult)
             turn_add(work[0], t, False, t == PACK - 1)
-        windows = [window1, window2, zero("window0", "work0")]
+        windows = [window1, window2, zero("window0", "x_raw1")]
         turn_g()
         weave_x(1, 1, turn_x(1, 1, 4))
         recip(1, 0, 2)

@@ -69,6 +69,8 @@ def tile_attend_gheads_sm_kernel(tc, x1, x2, wT, y1, u1, w1, y2, u2, w2, ts, off
         nc.vector.memset(window2[:].bitcast(U32), 0)
         window1 = keep.tile([P, T], F32, name="window1")
         nc.vector.memset(window1[:].bitcast(U32), 0)
+        window0 = keep.tile([P, T], F32, name="window0")
+        nc.vector.memset(window0[:].bitcast(U32), 0)
 
         def codes(name, width=512, tag=None):
             c = keep.tile([P, width], U32, name=name + "_c", tag=tag or name + "_c", align_bytes=64)
@@ -216,12 +218,6 @@ def tile_attend_gheads_sm_kernel(tc, x1, x2, wT, y1, u1, w1, y2, u2, w2, ts, off
                 ALU.mult,
             )
 
-        def zero(name, tag):
-            win = keep.tile([P, T], F32, name=name, tag=tag, align_bytes=64)
-            for k in range(4):
-                nc.gpsimd.memset(win[:, k * 512 : (k + 1) * 512], 0.0)
-            return win
-
         deal_x(1, nc.scalar.copy, 3, 4)
         deal_x(1, nc.vector.tensor_copy, 0, 2)
         deal_x(1, nc.vector.tensor_copy, 2, 3)
@@ -251,7 +247,7 @@ def tile_attend_gheads_sm_kernel(tc, x1, x2, wT, y1, u1, w1, y2, u2, w2, ts, off
         for t in range(PACK):
             nc.vector.tensor_scalar(work[0][:, t, :], work[0][:, t, :], inv[0][:, t : t + 1], wu[0][:, t : t + 1], ALU.mult, ALU.mult)
             turn_add(work[0], t, False, t == PACK - 1)
-        windows = [window1, window2, zero("window0", "x_raw1")]
+        windows = [window1, window2, window0]
         turn_g()
         weave_x(1, 1, turn_x(1, 1, 4))
         recip(1, 0, 2)

@@ -193,16 +193,16 @@ def tile_attend_gheads_sm_kernel(tc, x1, x2, wT, y1, u1, w1, y2, u2, w2, ts, off
         def diff(h, t, col, op=ALU.subtract):
             nc.vector.scalar_tensor_tensor(work[h][:, t, :], work[h][:, t, :], col[:, t : t + 1], y_raw[h][:, t, :], ALU.mult, op)
 
-        def turn_add(src, t, start, stop):
-            for c in range(4):
+        def turn_add(src, t, start, stop, blocks=range(4)):
+            for c in blocks:
                 nc.tensor.matmul(hb[c][:, t * P : (t + 1) * P], src[:, t, c * P : (c + 1) * P], ident[:], start=start, stop=stop, is_transpose=True)
 
         def turn_g():
-            for c in range(4):
-                nc.scalar.activation(g_t[c][:].rearrange("i (u s e) -> i u s e", u=2, e=2), hb[c][:].rearrange("i (u e s) -> i u s e", u=2, e=2),
-                                     ACT.Copy, scale=ts_col[:, c : c + 1])
             for pair in range(2):
-                bk = bank(4 + pair, "gw%d" % pair)
+                for c in (2 * pair, 2 * pair + 1):
+                    nc.scalar.activation(g_t[c][:].rearrange("i (u s e) -> i u s e", u=2, e=2), hb[c][:].rearrange("i (u e s) -> i u s e", u=2, e=2),
+                                         ACT.Copy, scale=ts_col[:, c : c + 1])
+                bk = bank(pair, "gw%d" % pair)
                 for k in range(2):
                     words = g_t[2 * pair + k][:].bitcast(F32)
                     for u in range(2):
@@ -230,26 +230,29 @@ def tile_attend_gheads_sm_kernel(tc, x1, x2, wT, y1, u1, w1, y2, u2, w2, ts, off
         y_neg = keep.tile([P, PACK, S], F32, name="y_neg", tag="ts_all", align_bytes=64)
         for t in range(PACK):
             nc.gpsimd.tensor_scalar(y_neg[:, t, :], y_raw[0][:, t, :], neg_wu[:, t : t + 1], 0.0, ALU.mult, ALU.add)
-        sb = scores_turned(1, (5, 6, 7, 4), (5, 6, 7, 4))
+        sb = scores_turned(1, (5, 6, 7, 4), (0, 1, 2, 3))
         total[0] = keep.tile([P, PACK], F32, name="total0", tag="ts_col2", align_bytes=64)
         for t in range(PACK):
             max_direct(0, t)
-        hb = [bank(c, "hT%d" % c) for c in range(4)]
+        hb = [bank((5, 6, 7, 4)[c], "hT%d" % c) for c in range(4)]
         for t in range(PACK):
             turn_add(y_neg, t, t == 0, False)
         for t in range(PACK):
             expo(0, t)
-        max_turned(1, sb)
         recip(0, 0, 2)
+        max_turned(1, sb)
         recip(0, 2, 4)
         for t in range(PACK):
             expo(1, t)
         for t in range(PACK):
-            nc.vector.tensor_scalar(work[0][:, t, :], work[0][:, t, :], inv[0][:, t : t + 1], wu[0][:, t : t + 1], ALU.mult, ALU.mult)
-            turn_add(work[0], t, False, t == PACK - 1)
+            engine = nc.gpsimd if t < 2 else nc.vector
+            engine.tensor_scalar(work[0][:, t, :], work[0][:, t, :], inv[0][:, t : t + 1], wu[0][:, t : t + 1], ALU.mult, ALU.mult)
+            turn_add(work[0], t, False, t == PACK - 1, range(2))
+        for t in range(PACK):
+            turn_add(work[0], t, False, t == PACK - 1, range(2, 4))
         windows = [window1, window2, window0]
         turn_g()
-        weave_x(1, 1, turn_x(1, 1, 4))
+        weave_x(1, 1, turn_x(1, 1, 0))
         recip(1, 0, 2)
         diff(1, 0, inv[1])
         recip(1, 2, 3)
@@ -276,7 +279,7 @@ def tile_attend_gheads_sm_kernel(tc, x1, x2, wT, y1, u1, w1, y2, u2, w2, ts, off
         def scatter(j, lo, hi, dw):
             nc.vector.tensor_copy(windows[j % WINDOWS][:].indirect(offsets[:, lo // 16 : hi // 16]), dw[:])
 
-        early = [result(j, 0, 256, 6 + j) for j in range(2)]
+        early = [result(j, 0, 256, 2 + j) for j in range(2)]
         weave(256, 512)
         qx_r[0][1] = codes("qx_r01", 256, "factor")
         quantise_x(0, 1)
@@ -288,5 +291,9 @@ def tile_attend_gheads_sm_kernel(tc, x1, x2, wT, y1, u1, w1, y2, u2, w2, ts, off
         scatter(1, 0, 256, early[1])
         for j in range(PACK):
             lo = 256 if j < 2 else 0
-            scatter(j, lo, S, result(j, lo, S, 6 + j % 2))
-            nc.sync.dma_start(out_view[j], windows[j % WINDOWS][:])
+            scatter(j, lo, S, result(j, lo, S, 2 + j % 2))
+            if j < PACK - 1:
+                nc.sync.dma_start(out_view[j], windows[j % WINDOWS][:])
+            else:
+                nc.sync.dma_start(out_view[j][:, 0 : T // 2], windows[j % WINDOWS][:, 0 : T // 2])
+                nc.scalar.dma_start(out_view[j][:, T // 2 : T], windows[j % WINDOWS][:, T // 2 : T])

@@ -84,8 +84,8 @@ def tile_attend_gheads_sm_kernel(tc, x1, x2, wT, y1, u1, w1, y2, u2, w2, ts, off
             nc.tensor.matmul_mx(out=acc, lhsT=lhs[0][:, lo : lo + P].bitcast(lfmt), lhsT_scale=lhs[1][:, lo : lo + P],
                                 rhs=rhs[0][:].bitcast(rfmt), rhs_scale=rhs[1][:], start=start, stop=stop)
 
-        x_d = [keep.tile([P, R * PACK], BF16, name="x_d%d" % h, align_bytes=64) for h in heads]
-        x_r = [[keep.tile([P, 1024], BF16, name="x_r0%d" % u, align_bytes=64) for u in range(2)], [keep.tile([P, 1024], BF16, name="x_r1%d" % u, align_bytes=64) for u in range(2)]]
+        x_d = [[keep.tile([P, R * 2], BF16, name="x_d%d%d" % (h, k), align_bytes=64) for k in range(2)] for h in heads]
+        x_r = [[keep.tile([P, 1024], BF16, name="x_r0%d" % u, align_bytes=64) for u in range(2)], [None, keep.tile([P, 1024], BF16, name="x_r11", align_bytes=64)]]
         qx_d = [codes("qx_d%d" % h) for h in heads]
         qx_r = [[None, None], [None, None]]
         qg = [codes("qg%d" % h) for h in heads]
@@ -94,16 +94,21 @@ def tile_attend_gheads_sm_kernel(tc, x1, x2, wT, y1, u1, w1, y2, u2, w2, ts, off
             nc.gpsimd.memset(qg[h][0][:, 256:S], 0)
             nc.gpsimd.memset(qg[h][1][:, 256:S].bitcast(U32), 0)
 
-        def deal_x(h, copy, lo=0, hi=PACK):
-            copy(x_d[h][:].rearrange("p (t s j) -> p s t j", t=PACK, j=PACK)[:, :, lo:hi, :],
+        def deal_x(h, copy, lo, hi):
+            copy(x_d[h][lo // 2][:].rearrange("p (t s j) -> p s t j", t=2, j=PACK)[:, :, lo % 2 : lo % 2 + hi - lo, :],
                  x_raw[h][:].rearrange("p j (s t) -> p s t j", t=PACK)[:, :, lo:hi, :])
 
         def turn_x(h, u, b):
-            words = x_d[h][:].bitcast(F32)
             bk = bank(b, "xw%d%d" % (h, u))
             for t in range(PACK):
-                nc.tensor.transpose(bk[:, t * P : (t + 1) * P], words[:, 256 * t + u : 256 * (t + 1) : 2], ident[:])
+                words = x_d[h][t // 2][:].bitcast(F32)
+                nc.tensor.transpose(bk[:, t * P : (t + 1) * P], words[:, 256 * (t % 2) + u : 256 * (t % 2 + 1) : 2], ident[:])
             return bk
+
+        def quantise_d(h):
+            for k in range(2):
+                cols = slice(256 * k, 256 * (k + 1))
+                nc.vector.quantize_mx(out=qx_d[h][0][:, cols].bitcast(E4M3), scales=qx_d[h][1][:, cols], in_=x_d[h][k][:])
 
         def weave_x(h, u, bk):
             nc.scalar.copy(x_r[h][u][:].rearrange("s (e p t) -> s e p t", e=2, t=PACK), bk[:].bitcast(BF16).rearrange("s (t p e) -> s e p t", t=PACK, e=2))
@@ -113,7 +118,8 @@ def tile_attend_gheads_sm_kernel(tc, x1, x2, wT, y1, u1, w1, y2, u2, w2, ts, off
 
         ts_row = keep.tile([P, S], F32, name="ts_row")
         nc.vector.tensor_copy(ts_row[:], ts_win[:].indirect(offsets[:]))
-        deal_x(0, nc.scalar.copy)
+        deal_x(0, nc.scalar.copy, 0, 2)
+        deal_x(0, nc.scalar.copy, 2, 4)
         bk = bank(0, "ts_turned")
         for c in range(4):
             nc.tensor.transpose(bk[:, c * P : (c + 1) * P], ts_row[:, c * P : (c + 1) * P], ident[:])
@@ -121,6 +127,8 @@ def tile_attend_gheads_sm_kernel(tc, x1, x2, wT, y1, u1, w1, y2, u2, w2, ts, off
         nc.scalar.copy(ts_col[:], bk[:, 0:512:P])
         ts_col2 = keep.tile([P, 4], F32, name="ts_col2", align_bytes=64)
         nc.scalar.copy(ts_col2[:], bk[:, 0:512:P])
+        ts_half = keep.tile([P, 2], F32, name="ts_half", align_bytes=64)
+        nc.scalar.copy(ts_half[:], bk[:, 0:256:P])
         bk = bank(1, "ts_spread")
         for c in range(4):
             nc.tensor.transpose(bk[:, c * P : (c + 1) * P], ts_col[:, c : c + 1].to_broadcast([P, P]), ident[:])
@@ -130,7 +138,7 @@ def tile_attend_gheads_sm_kernel(tc, x1, x2, wT, y1, u1, w1, y2, u2, w2, ts, off
         w_d = keep.tile([P, S, PACK], BF16, name="w_d", align_bytes=64)
         w_flat = w_d[:].rearrange("p i j -> p (i j)")
         nc.vector.tensor_copy(w_d[:, :, 0], w_plane[0][:].indirect(offsets[:]))
-        quantise(qx_d[0], x_d[0], E4M3)
+        quantise_d(0)
         for u in range(2):
             weave_x(0, u, turn_x(0, u, 2 + u))
         factor = keep.tile([P, PACK, S], F32, name="factor", align_bytes=64)
@@ -155,8 +163,8 @@ def tile_attend_gheads_sm_kernel(tc, x1, x2, wT, y1, u1, w1, y2, u2, w2, ts, off
         neg_m = [keep.tile([P, PACK], F32, name="neg_m%d" % h) for h in heads]
         total = [None, keep.tile([P, PACK], F32, name="total1")]
         inv = [keep.tile([P, PACK], F32, name="inv%d" % h) for h in heads]
-        g = [keep.tile([P, S * PACK], BF16, name="g%d" % h, align_bytes=64) for h in heads]
-        g_t = [keep.tile([P, R], BF16, name="g_t%d" % c, align_bytes=64) for c in range(4)]
+        g = [[keep.tile([P, 1024], BF16, name="g0%d" % pair, align_bytes=64) for pair in range(2)], [keep.tile([P, 1024], BF16, name="g10", align_bytes=64), None]]
+        g_t = [None] * 4
         turned = keep.tile([P, 4, R], F32, name="turned")
 
         def expo(h, t):
@@ -197,22 +205,29 @@ def tile_attend_gheads_sm_kernel(tc, x1, x2, wT, y1, u1, w1, y2, u2, w2, ts, off
             for c in blocks:
                 nc.tensor.matmul(hb[c][:, t * P : (t + 1) * P], src[:, t, c * P : (c + 1) * P], ident[:], start=start, stop=stop, is_transpose=True)
 
-        def turn_g():
-            for pair in range(2):
-                for c in (2 * pair, 2 * pair + 1):
-                    nc.scalar.activation(g_t[c][:].rearrange("i (u s e) -> i u s e", u=2, e=2), hb[c][:].rearrange("i (u e s) -> i u s e", u=2, e=2),
-                                         ACT.Copy, scale=ts_col[:, c : c + 1])
-                bk = bank(pair, "gw%d" % pair)
-                for k in range(2):
-                    words = g_t[2 * pair + k][:].bitcast(F32)
-                    for u in range(2):
-                        nc.tensor.transpose(bk[:, (2 * k + u) * P : (2 * k + u + 1) * P], words[:, u * P : (u + 1) * P], ident[:])
-                nc.scalar.copy(g[0][:, pair * 1024 : (pair + 1) * 1024].bitcast(F32).rearrange("s (k i u) -> s k i u", k=2, u=2),
-                               bk[:].rearrange("s (k u i) -> s k i u", k=2, u=2))
+        def turn_g(pair):
+            for c in (2 * pair, 2 * pair + 1):
+                g_t[c] = keep.tile([P, R], BF16, name="g_t%d" % c, tag="g_t%d" % (c % 2), align_bytes=64)
+                nc.scalar.activation(g_t[c][:].rearrange("i (u s e) -> i u s e", u=2, e=2), hb[c][:].rearrange("i (u e s) -> i u s e", u=2, e=2),
+                                     ACT.Copy, scale=(ts_col if pair else ts_half)[:, c : c + 1])
+            if pair == 0:
+                x_r[1][0] = keep.tile([P, 1024], BF16, name="x_r10", tag="ts_half", align_bytes=64)
+                weave_x(1, 0, turn_x(1, 0, 0))
+            bk = bank(1 + pair, "gw%d" % pair)
+            for k in range(2):
+                words = g_t[2 * pair + k][:].bitcast(F32)
+                for u in range(2):
+                    nc.tensor.transpose(bk[:, (2 * k + u) * P : (2 * k + u + 1) * P], words[:, u * P : (u + 1) * P], ident[:])
+            nc.scalar.copy(g[0][pair][:].bitcast(F32).rearrange("s (k i u) -> s k i u", k=2, u=2),
+                           bk[:].rearrange("s (k u i) -> s k i u", k=2, u=2))
+
+        def quantise_g(h, pair):
+            cols = slice(256 * pair, 256 * (pair + 1))
+            nc.vector.quantize_mx(out=qg[h][0][:, cols].bitcast(E5M2), scales=qg[h][1][:, cols], in_=g[h][pair][:])
 
         def weave(lo, hi):
             nc.vector.tensor_tensor(
-                g[1][:, PACK * lo : PACK * hi].rearrange("p (c i t) -> p c t i", i=2, t=PACK),
+                g[1][lo // 256][:].rearrange("p (c i t) -> p c t i", i=2, t=PACK),
                 work[1][:, :, lo:hi].rearrange("p t (c i) -> p c t i", i=2),
                 factor[:, :, lo:hi].rearrange("p t (c i) -> p c t i", i=2),
                 ALU.mult,
@@ -221,8 +236,7 @@ def tile_attend_gheads_sm_kernel(tc, x1, x2, wT, y1, u1, w1, y2, u2, w2, ts, off
         deal_x(1, nc.scalar.copy, 3, 4)
         deal_x(1, nc.vector.tensor_copy, 0, 2)
         deal_x(1, nc.vector.tensor_copy, 2, 3)
-        quantise(qx_d[1], x_d[1], E4M3)
-        weave_x(1, 0, turn_x(1, 0, 4))
+        quantise_d(1)
         work[0] = keep.tile([P, PACK, S], F32, name="work0", tag="x_raw1", align_bytes=64)
         for half in range(2):
             for t in range(PACK):
@@ -251,8 +265,7 @@ def tile_attend_gheads_sm_kernel(tc, x1, x2, wT, y1, u1, w1, y2, u2, w2, ts, off
         for t in range(PACK):
             turn_add(work[0], t, False, t == PACK - 1, range(2, 4))
         windows = [window1, window2, window0]
-        turn_g()
-        weave_x(1, 1, turn_x(1, 1, 0))
+        turn_g(0)
         recip(1, 0, 2)
         diff(1, 0, inv[1])
         recip(1, 2, 3)
@@ -263,8 +276,8 @@ def tile_attend_gheads_sm_kernel(tc, x1, x2, wT, y1, u1, w1, y2, u2, w2, ts, off
         qx_r[1][0] = codes("qx_r10", 256, "y_raw1")
         weave(0, 256)
         quantise_x(1, 0)
-        quantise(qg[1], g[1], E5M2, 0, 256)
-        quantise(qg[0], g[0], E5M2, 0, 256)
+        quantise_g(1, 0)
+        quantise_g(0, 0)
 
         out_view = out.rearrange("(p j) n -> j p n", j=PACK)
 
@@ -272,26 +285,33 @@ def tile_attend_gheads_sm_kernel(tc, x1, x2, wT, y1, u1, w1, y2, u2, w2, ts, off
             acc = bank(b, "dw%d_%d" % (j, lo))
             mm(acc[:], qx_r[1][j // 2], j % 2 * P, E4M3, qg[1], E5M2, True, False)
             mm(acc[:], qx_r[0][j // 2], j % 2 * P, E4M3, qg[0], E5M2, False, True)
-            dw = keep.tile([P, hi - lo], F32, name="dw%d_%d" % (j, lo))
+            return acc
+
+        def drain(j, lo, hi, acc, tag=None):
+            dw = keep.tile([P, hi - lo], F32, name="dw%d_%d" % (j, lo), tag=tag or "dw%d_%d" % (j, lo), align_bytes=64)
             nc.scalar.copy(dw[:], acc[:, lo:hi])
             return dw
 
         def scatter(j, lo, hi, dw):
             nc.vector.tensor_copy(windows[j % WINDOWS][:].indirect(offsets[:, lo // 16 : hi // 16]), dw[:])
 
-        early = [result(j, 0, 256, 2 + j) for j in range(2)]
+        early = [result(j, 0, 256, (3, 0)[j]) for j in range(2)]
+        first = drain(0, 0, 256, early[0])
+        turn_g(1)
+        weave_x(1, 1, turn_x(1, 1, 1))
+        g[1][1] = keep.tile([P, 1024], BF16, name="g11", tag="g00", align_bytes=64)
         weave(256, 512)
         qx_r[0][1] = codes("qx_r01", 256, "factor")
         quantise_x(0, 1)
-        scatter(0, 0, 256, early[0])
-        quantise(qg[1], g[1], E5M2, 256, S)
-        quantise(qg[0], g[0], E5M2, 256, S)
-        qx_r[1][1] = codes("qx_r11", 256, "g1")
+        scatter(0, 0, 256, first)
+        quantise_g(1, 1)
+        quantise_g(0, 1)
+        qx_r[1][1] = codes("qx_r11", 256, "g00")
         quantise_x(1, 1)
-        scatter(1, 0, 256, early[1])
+        scatter(1, 0, 256, drain(1, 0, 256, early[1], "g01"))
         for j in range(PACK):
             lo = 256 if j < 2 else 0
-            scatter(j, lo, S, result(j, lo, S, 2 + j % 2))
+            scatter(j, lo, S, drain(j, lo, S, result(j, lo, S, (3, 0)[j % 2])))
             if j < PACK - 1:
                 nc.sync.dma_start(out_view[j], windows[j % WINDOWS][:])
             else:

@@ -15,12 +15,17 @@ ACT = mybir.ActivationFunctionType
 
 P = 128
 PACK = 4
-D = 512
 R = 512
 S = 512
 T = 2048
-FLOPS = 4 * 2 * 512 * 512 * 512
+HALF = 256
+BAND = 16
+BANK = 512
+ALIGN = 64
 WINDOWS = 3
+EARLY_TILES = 2
+GPSIMD_TILES = 2
+FLOPS = 4 * 2 * 512 * 512 * 512
 
 
 def tile_attend_gheads_sm_kernel(tc, x1, x2, wT, y1, u1, w1, y2, u2, w2, ts, offs, out):
@@ -32,12 +37,15 @@ def tile_attend_gheads_sm_kernel(tc, x1, x2, wT, y1, u1, w1, y2, u2, w2, ts, off
         psum = ctx.enter_context(tc.psum_pool(name="psum", bufs=1))
 
         def bank(b, name):
-            return psum.tile([P, 512], F32, name=name, tag="bank%d" % b)
+            return psum.tile([P, BANK], F32, name=name, tag="bank%d" % b)
 
-        offsets = keep.tile([P, S // 16], U16, name="offsets")
-        x_raw = [keep.tile([P, PACK, R], F32, name="x_raw%d" % h, tag="x_raw%d" % h, align_bytes=64) for h in heads]
-        w_plane = [keep.tile([P, T], F32, name="w_plane%d" % j, align_bytes=64) for j in range(PACK)]
-        y_raw = [keep.tile([P, PACK, S], F32, name="y_raw%d" % h, align_bytes=64) for h in heads]
+        def half_cols(half):
+            return slice(half * HALF, (half + 1) * HALF)
+
+        offsets = keep.tile([P, S // BAND], U16, name="offsets")
+        x_raw = [keep.tile([P, PACK, R], F32, name="x_raw%d" % h, tag="x_raw%d" % h, align_bytes=ALIGN) for h in heads]
+        w_plane = [keep.tile([P, T], F32, name="w_plane%d" % j, align_bytes=ALIGN) for j in range(PACK)]
+        y_raw = [keep.tile([P, PACK, S], F32, name="y_raw%d" % h, align_bytes=ALIGN) for h in heads]
         w_view = wT.rearrange("(p j) n -> j p n", j=PACK)
         ts_win = keep.tile([P, T], F32, name="ts_win")
         nc.vector.memset(ts_win[:].bitcast(U32), 0)
@@ -48,7 +56,7 @@ def tile_attend_gheads_sm_kernel(tc, x1, x2, wT, y1, u1, w1, y2, u2, w2, ts, off
             nc.sync.dma_start(w_plane[j][:], w_view[j])
         u_col = [keep.tile([P, PACK], F32, name="u_col%d" % h) for h in heads]
         w_col = [keep.tile([P, PACK], F32, name="w_col%d" % h) for h in heads]
-        for h in (1, 0):
+        for h in reversed(heads):
             nc.scalar.dma_start(u_col[h][:], us[h].rearrange("(p t) o -> p (t o)", t=PACK))
             nc.scalar.dma_start(w_col[h][:], ws[h].rearrange("(p t) o -> p (t o)", t=PACK))
         nc.sync.dma_start(x_raw[1][:], xs[1].rearrange("(p j) r -> p j r", j=PACK))
@@ -57,261 +65,257 @@ def tile_attend_gheads_sm_kernel(tc, x1, x2, wT, y1, u1, w1, y2, u2, w2, ts, off
 
         ident = keep.tile([P, P], F32, name="ident")
         make_identity(nc, ident[:])
-        neg_u = keep.tile([P, PACK], F32, name="neg_u")
+        neg_u2 = keep.tile([P, PACK], F32, name="neg_u")
         wu = [keep.tile([P, PACK], F32, name="wu%d" % h) for h in heads]
-        nc.gpsimd.tensor_scalar(neg_u[:], u_col[1][:], -1.0, 0.0, ALU.mult, ALU.add)
-        nc.gpsimd.tensor_tensor(wu[1][:], u_col[1][:], w_col[1][:], ALU.mult)
-        nc.gpsimd.tensor_tensor(wu[0][:], u_col[0][:], w_col[0][:], ALU.mult)
-        neg_wu = keep.tile([P, PACK], F32, name="neg_wu")
-        nc.gpsimd.tensor_scalar(neg_wu[:], wu[0][:], -1.0, 0.0, ALU.mult, ALU.add)
+        nc.gpsimd.tensor_scalar(neg_u2[:], u_col[1][:], -1.0, 0.0, ALU.mult, ALU.add)
+        for h in reversed(heads):
+            nc.gpsimd.tensor_tensor(wu[h][:], u_col[h][:], w_col[h][:], ALU.mult)
+        neg_wu1 = keep.tile([P, PACK], F32, name="neg_wu")
+        nc.gpsimd.tensor_scalar(neg_wu1[:], wu[0][:], -1.0, 0.0, ALU.mult, ALU.add)
 
-        window2 = keep.tile([P, T], F32, name="window2")
-        nc.vector.memset(window2[:].bitcast(U32), 0)
-        window1 = keep.tile([P, T], F32, name="window1")
-        nc.vector.memset(window1[:].bitcast(U32), 0)
-        window0 = keep.tile([P, T], F32, name="window0")
-        nc.vector.memset(window0[:].bitcast(U32), 0)
+        windows = []
+        for n in range(WINDOWS):
+            windows.append(keep.tile([P, T], F32, name="window%d" % n))
+            nc.vector.memset(windows[n][:].bitcast(U32), 0)
 
-        def codes(name, width=512, tag=None):
-            c = keep.tile([P, width], U32, name=name + "_c", tag=tag or name + "_c", align_bytes=64)
-            s = keep.tile([P, width], U8, name=name + "_s", align_bytes=64)
-            return c, s
+        def codes(name, width, tag=None):
+            words = keep.tile([P, width], U32, name=name + "_c", tag=tag or name + "_c", align_bytes=ALIGN)
+            scales = keep.tile([P, width], U8, name=name + "_s", align_bytes=ALIGN)
+            return words, scales
 
-        def quantise(q, src, fmt, lo=0, hi=512):
-            nc.vector.quantize_mx(out=q[0][:, lo:hi].bitcast(fmt), scales=q[1][:, lo:hi], in_=src[:, PACK * lo : PACK * hi])
+        def quantise(q, cols, src, fmt):
+            nc.vector.quantize_mx(out=q[0][:, cols].bitcast(fmt), scales=q[1][:, cols], in_=src)
 
-        def mm(acc, lhs, lo, lfmt, rhs, rfmt, start, stop):
-            nc.tensor.matmul_mx(out=acc, lhsT=lhs[0][:, lo : lo + P].bitcast(lfmt), lhsT_scale=lhs[1][:, lo : lo + P],
-                                rhs=rhs[0][:].bitcast(rfmt), rhs_scale=rhs[1][:], start=start, stop=stop)
+        def mm(acc, lhs, lo, rhs, cols, rhs_fmt, start, stop):
+            nc.tensor.matmul_mx(out=acc, lhsT=lhs[0][:, lo : lo + P].bitcast(E4M3), lhsT_scale=lhs[1][:, lo : lo + P],
+                                rhs=rhs[0][:, cols].bitcast(rhs_fmt), rhs_scale=rhs[1][:, cols], start=start, stop=stop)
 
-        x_d = [[keep.tile([P, R * 2], BF16, name="x_d%d%d" % (h, k), align_bytes=64) for k in range(2)] for h in heads]
-        x_r = [[keep.tile([P, 1024], BF16, name="x_r0%d" % u, align_bytes=64) for u in range(2)], [None, keep.tile([P, 1024], BF16, name="x_r11", align_bytes=64)]]
-        qx_d = [codes("qx_d%d" % h) for h in heads]
+        x_d = [[keep.tile([P, HALF * PACK], BF16, name="x_d%d%d" % (h, k), align_bytes=ALIGN) for k in range(2)] for h in heads]
+        x_r = [[keep.tile([P, HALF * PACK], BF16, name="x_r0%d" % u, align_bytes=ALIGN) for u in range(2)],
+               [None, keep.tile([P, HALF * PACK], BF16, name="x_r11", align_bytes=ALIGN)]]
+        qx_d = [codes("qx_d%d" % h, R) for h in heads]
         qx_r = [[None, None], [None, None]]
-        qg = [codes("qg%d" % h) for h in heads]
-        qw = codes("qw")
+        qg = [codes("qg%d" % h, S) for h in heads]
+        qw = codes("qw", S)
         for h in heads:
-            nc.gpsimd.memset(qg[h][0][:, 256:S], 0)
-            nc.gpsimd.memset(qg[h][1][:, 256:S].bitcast(U32), 0)
+            nc.gpsimd.memset(qg[h][0][:, half_cols(1)], 0)
+            nc.gpsimd.memset(qg[h][1][:, half_cols(1)].bitcast(U32), 0)
 
-        def deal_x(h, copy, lo, hi):
-            copy(x_d[h][lo // 2][:].rearrange("p (t s j) -> p s t j", t=2, j=PACK)[:, :, lo % 2 : lo % 2 + hi - lo, :],
-                 x_raw[h][:].rearrange("p j (s t) -> p s t j", t=PACK)[:, :, lo:hi, :])
+        def deal_x(h, k, copy):
+            copy(x_d[h][k][:].rearrange("p (t s j) -> p s t j", t=2, j=PACK),
+                 x_raw[h][:].rearrange("p j (s t) -> p s t j", t=PACK)[:, :, 2 * k : 2 * k + 2, :])
+
+        def quantise_x_d(h):
+            for k in range(2):
+                quantise(qx_d[h], half_cols(k), x_d[h][k][:], E4M3)
 
         def turn_x(h, u, b):
-            bk = bank(b, "xw%d%d" % (h, u))
+            acc = bank(b, "xw%d%d" % (h, u))
             for t in range(PACK):
-                words = x_d[h][t // 2][:].bitcast(F32)
-                nc.tensor.transpose(bk[:, t * P : (t + 1) * P], words[:, 256 * (t % 2) + u : 256 * (t % 2 + 1) : 2], ident[:])
-            return bk
+                pairs = x_d[h][t // 2][:].bitcast(F32)
+                lo = 2 * P * (t % 2)
+                nc.tensor.transpose(acc[:, t * P : (t + 1) * P], pairs[:, lo + u : lo + 2 * P : 2], ident[:])
+            return acc
 
-        def quantise_d(h):
-            for k in range(2):
-                cols = slice(256 * k, 256 * (k + 1))
-                nc.vector.quantize_mx(out=qx_d[h][0][:, cols].bitcast(E4M3), scales=qx_d[h][1][:, cols], in_=x_d[h][k][:])
+        def weave_x(h, u, acc):
+            nc.scalar.copy(x_r[h][u][:].rearrange("s (e p t) -> s e p t", e=2, t=PACK),
+                           acc[:].bitcast(BF16).rearrange("s (t p e) -> s e p t", t=PACK, e=2))
 
-        def weave_x(h, u, bk):
-            nc.scalar.copy(x_r[h][u][:].rearrange("s (e p t) -> s e p t", e=2, t=PACK), bk[:].bitcast(BF16).rearrange("s (t p e) -> s e p t", t=PACK, e=2))
-
-        def quantise_x(h, u, lo=0, hi=256):
-            quantise(qx_r[h][u], x_r[h][u], E4M3, lo, hi)
+        def quantise_x_r(h, u, tag):
+            qx_r[h][u] = codes("qx_r%d%d" % (h, u), HALF, tag)
+            quantise(qx_r[h][u], half_cols(0), x_r[h][u][:], E4M3)
 
         ts_row = keep.tile([P, S], F32, name="ts_row")
         nc.vector.tensor_copy(ts_row[:], ts_win[:].indirect(offsets[:]))
-        deal_x(0, nc.scalar.copy, 0, 2)
-        deal_x(0, nc.scalar.copy, 2, 4)
-        bk = bank(0, "ts_turned")
-        for c in range(4):
-            nc.tensor.transpose(bk[:, c * P : (c + 1) * P], ts_row[:, c * P : (c + 1) * P], ident[:])
-        ts_col = keep.tile([P, 4], F32, name="ts_col")
-        nc.scalar.copy(ts_col[:], bk[:, 0:512:P])
-        ts_col2 = keep.tile([P, 4], F32, name="ts_col2", align_bytes=64)
-        nc.scalar.copy(ts_col2[:], bk[:, 0:512:P])
-        ts_half = keep.tile([P, 2], F32, name="ts_half", align_bytes=64)
-        nc.scalar.copy(ts_half[:], bk[:, 0:256:P])
-        bk = bank(1, "ts_spread")
-        for c in range(4):
-            nc.tensor.transpose(bk[:, c * P : (c + 1) * P], ts_col[:, c : c + 1].to_broadcast([P, P]), ident[:])
-        ts_all = keep.tile([P, S], F32, name="ts_all", align_bytes=64)
-        nc.scalar.copy(ts_all[:], bk[:])
+        for k in range(2):
+            deal_x(0, k, nc.scalar.copy)
+        ts_bank = bank(0, "ts_turned")
+        for c in range(PACK):
+            nc.tensor.transpose(ts_bank[:, c * P : (c + 1) * P], ts_row[:, c * P : (c + 1) * P], ident[:])
+        ts_col = keep.tile([P, PACK], F32, name="ts_col")
+        nc.scalar.copy(ts_col[:], ts_bank[:, 0:S:P])
+        ts_scores = keep.tile([P, PACK], F32, name="ts_scores", align_bytes=ALIGN)
+        nc.scalar.copy(ts_scores[:], ts_bank[:, 0:S:P])
+        ts_first = keep.tile([P, 2], F32, name="ts_first", align_bytes=ALIGN)
+        nc.scalar.copy(ts_first[:], ts_bank[:, 0:HALF:P])
+        spread_bank = bank(1, "ts_spread")
+        for c in range(PACK):
+            nc.tensor.transpose(spread_bank[:, c * P : (c + 1) * P], ts_col[:, c : c + 1].to_broadcast([P, P]), ident[:])
+        ts_all = keep.tile([P, S], F32, name="ts_all", align_bytes=ALIGN)
+        nc.scalar.copy(ts_all[:], spread_bank[:])
 
-        w_d = keep.tile([P, S, PACK], BF16, name="w_d", align_bytes=64)
+        w_d = keep.tile([P, S, PACK], BF16, name="w_d", align_bytes=ALIGN)
         w_flat = w_d[:].rearrange("p i j -> p (i j)")
         nc.vector.tensor_copy(w_d[:, :, 0], w_plane[0][:].indirect(offsets[:]))
-        quantise_d(0)
+        quantise_x_d(0)
         for u in range(2):
             weave_x(0, u, turn_x(0, u, 2 + u))
-        factor = keep.tile([P, PACK, S], F32, name="factor", align_bytes=64)
+        factor = keep.tile([P, PACK, S], F32, name="factor", align_bytes=ALIGN)
         for t in range(PACK):
             nc.scalar.activation(factor[:, t, :], ts_all[:], ACT.Copy, scale=wu[1][:, t : t + 1])
-        nc.vector.tensor_copy(w_d[:, :, 1], w_plane[1][:].indirect(offsets[:]))
-        nc.vector.tensor_copy(w_d[:, :, 2], w_plane[2][:].indirect(offsets[:]))
-        qx_r[0][0] = codes("qx_r00", 256, "w_plane2")
-        quantise_x(0, 0)
-        acc1 = []
+        for j in (1, 2):
+            nc.vector.tensor_copy(w_d[:, :, j], w_plane[j][:].indirect(offsets[:]))
+        quantise_x_r(0, 0, "w_plane2")
+
+        direct = []
         for half in range(2):
-            nc.vector.tensor_copy(w_d[:, half * 256 : (half + 1) * 256, 3], w_plane[3][:].indirect(offsets[:, half * 16 : (half + 1) * 16]))
-            quantise(qw, w_flat, E4M3, half * 256, (half + 1) * 256)
+            entries = offsets[:, half * HALF // BAND : (half + 1) * HALF // BAND]
+            nc.vector.tensor_copy(w_d[:, half_cols(half), 3], w_plane[3][:].indirect(entries))
+            quantise(qw, half_cols(half), w_flat[:, half * HALF * PACK : (half + 1) * HALF * PACK], E4M3)
             for t in range(PACK):
                 if t % 2 == 0:
-                    acc1.append(bank(2 * half + t // 2, "a1_%d%d" % (half, t)))
-                nc.tensor.matmul_mx(out=acc1[-1][:, (t % 2) * 256 : (t % 2 + 1) * 256], lhsT=qx_d[0][0][:, t * P : (t + 1) * P].bitcast(E4M3),
-                                    lhsT_scale=qx_d[0][1][:, t * P : (t + 1) * P], rhs=qw[0][:, half * 256 : (half + 1) * 256].bitcast(E4M3),
-                                    rhs_scale=qw[1][:, half * 256 : (half + 1) * 256], start=True, stop=True)
+                    direct.append(bank(2 * half + t // 2, "a1_%d%d" % (half, t)))
+                mm(direct[-1][:, half_cols(t % 2)], qx_d[0], t * P, qw, half_cols(half), E4M3, True, True)
 
-        work = [None, keep.tile([P, PACK, S], F32, name="work1", align_bytes=64)]
+        work = [None, keep.tile([P, PACK, S], F32, name="work1", align_bytes=ALIGN)]
         neg_m = [keep.tile([P, PACK], F32, name="neg_m%d" % h) for h in heads]
         total = [None, keep.tile([P, PACK], F32, name="total1")]
         inv = [keep.tile([P, PACK], F32, name="inv%d" % h) for h in heads]
-        g = [[keep.tile([P, 1024], BF16, name="g0%d" % pair, align_bytes=64) for pair in range(2)], [keep.tile([P, 1024], BF16, name="g10", align_bytes=64), None]]
-        g_t = [None] * 4
-        turned = keep.tile([P, 4, R], F32, name="turned")
+        g = [[keep.tile([P, HALF * PACK], BF16, name="g0%d" % half, align_bytes=ALIGN) for half in range(2)],
+             [keep.tile([P, HALF * PACK], BF16, name="g10", align_bytes=ALIGN), None]]
+        turned = keep.tile([P, PACK, R], F32, name="turned")
+
+        def negate_and_min(h, t, src, scalar):
+            nc.vector.tensor_scalar(work[h][:, t, :], src, scalar, None, ALU.mult, ALU.min, accum_out=neg_m[h][:, t : t + 1])
 
         def expo(h, t):
             nc.scalar.activation(work[h][:, t, :], work[h][:, t, :], ACT.Exp, bias=neg_m[h][:, t : t + 1], scale=-1.0,
                                  accum_out=total[h][:, t : t + 1])
 
-        def scale_direct(h, acc, half, t):
-            cols = slice(half * 256, (half + 1) * 256)
-            nc.vector.scalar_tensor_tensor(work[h][:, t, cols], acc[2 * half + t // 2][:, (t % 2) * 256 : (t % 2 + 1) * 256], u_col[h][:, t : t + 1],
-                                           ts_all[:, cols], ALU.mult, ALU.mult)
-
-        def max_direct(h, t):
-            nc.vector.tensor_scalar(work[h][:, t, :], work[h][:, t, :], -1.0, None, ALU.mult, ALU.min, accum_out=neg_m[h][:, t : t + 1])
-
-        def scores_turned(h, banks_a, banks_s):
-            for c in range(4):
-                bk = bank(banks_a[c], "aT%d%d" % (h, c))
-                mm(bk[:], qw, c * P, E4M3, qx_d[h], E4M3, True, True)
-                nc.scalar.activation(turned[:, c, :], bk[:], ACT.Copy, scale=ts_col2[:, c : c + 1])
-            sb = [bank(banks_s[t], "s%d%d" % (h, t)) for t in range(PACK)]
-            order = [(c, t) for c in range(4) for t in range(PACK)] if banks_a != banks_s else [(c, t) for t in range(PACK) for c in range(4)]
-            for c, t in order:
-                nc.tensor.transpose(sb[t][:, c * P : (c + 1) * P], turned[:, c, t * P : (t + 1) * P], ident[:])
-            return sb
-
-        def max_turned(h, sb):
-            for t in range(PACK):
-                nc.vector.tensor_scalar(work[h][:, t, :], sb[t][:], neg_u[:, t : t + 1], None, ALU.mult, ALU.min,
-                                        accum_out=neg_m[h][:, t : t + 1])
-
         def recip(h, lo, hi):
             nc.vector.reciprocal(inv[h][:, lo:hi], total[h][:, lo:hi])
 
-        def diff(h, t, col, op=ALU.subtract):
-            nc.vector.scalar_tensor_tensor(work[h][:, t, :], work[h][:, t, :], col[:, t : t + 1], y_raw[h][:, t, :], ALU.mult, op)
+        def diff(t):
+            nc.vector.scalar_tensor_tensor(work[1][:, t, :], work[1][:, t, :], inv[1][:, t : t + 1], y_raw[1][:, t, :],
+                                           ALU.mult, ALU.subtract)
 
-        def turn_add(src, t, start, stop, blocks=range(4)):
-            for c in blocks:
-                nc.tensor.matmul(hb[c][:, t * P : (t + 1) * P], src[:, t, c * P : (c + 1) * P], ident[:], start=start, stop=stop, is_transpose=True)
-
-        def turn_g(pair):
-            for c in (2 * pair, 2 * pair + 1):
-                g_t[c] = keep.tile([P, R], BF16, name="g_t%d" % c, tag="g_t%d" % (c % 2), align_bytes=64)
-                nc.scalar.activation(g_t[c][:].rearrange("i (u s e) -> i u s e", u=2, e=2), hb[c][:].rearrange("i (u e s) -> i u s e", u=2, e=2),
-                                     ACT.Copy, scale=(ts_col if pair else ts_half)[:, c : c + 1])
-            if pair == 0:
-                x_r[1][0] = keep.tile([P, 1024], BF16, name="x_r10", tag="ts_half", align_bytes=64)
-                weave_x(1, 0, turn_x(1, 0, 0))
-            bk = bank(1 + pair, "gw%d" % pair)
-            for k in range(2):
-                words = g_t[2 * pair + k][:].bitcast(F32)
-                for u in range(2):
-                    nc.tensor.transpose(bk[:, (2 * k + u) * P : (2 * k + u + 1) * P], words[:, u * P : (u + 1) * P], ident[:])
-            nc.scalar.copy(g[0][pair][:].bitcast(F32).rearrange("s (k i u) -> s k i u", k=2, u=2),
-                           bk[:].rearrange("s (k u i) -> s k i u", k=2, u=2))
-
-        def quantise_g(h, pair):
-            cols = slice(256 * pair, 256 * (pair + 1))
-            nc.vector.quantize_mx(out=qg[h][0][:, cols].bitcast(E5M2), scales=qg[h][1][:, cols], in_=g[h][pair][:])
-
-        def weave(lo, hi):
+        def weave_g2(half):
             nc.vector.tensor_tensor(
-                g[1][lo // 256][:].rearrange("p (c i t) -> p c t i", i=2, t=PACK),
-                work[1][:, :, lo:hi].rearrange("p t (c i) -> p c t i", i=2),
-                factor[:, :, lo:hi].rearrange("p t (c i) -> p c t i", i=2),
+                g[1][half][:].rearrange("p (c i t) -> p c t i", i=2, t=PACK),
+                work[1][:, :, half_cols(half)].rearrange("p t (c i) -> p c t i", i=2),
+                factor[:, :, half_cols(half)].rearrange("p t (c i) -> p c t i", i=2),
                 ALU.mult,
             )
 
-        deal_x(1, nc.scalar.copy, 3, 4)
-        deal_x(1, nc.vector.tensor_copy, 0, 2)
-        deal_x(1, nc.vector.tensor_copy, 2, 3)
-        quantise_d(1)
-        work[0] = keep.tile([P, PACK, S], F32, name="work0", tag="x_raw1", align_bytes=64)
+        def quantise_g(h, half):
+            quantise(qg[h], half_cols(half), g[h][half][:], E5M2)
+
+        quantise_x_r(0, 1, "w_d")
+        deal_x(1, 1, nc.scalar.copy)
+        deal_x(1, 0, nc.vector.tensor_copy)
+        quantise_x_d(1)
+
+        work[0] = keep.tile([P, PACK, S], F32, name="work0", tag="x_raw1", align_bytes=ALIGN)
         for half in range(2):
             for t in range(PACK):
-                scale_direct(0, acc1, half, t)
-        y_neg = keep.tile([P, PACK, S], F32, name="y_neg", tag="ts_all", align_bytes=64)
+                nc.vector.scalar_tensor_tensor(work[0][:, t, half_cols(half)], direct[2 * half + t // 2][:, half_cols(t % 2)],
+                                               u_col[0][:, t : t + 1], ts_all[:, half_cols(half)], ALU.mult, ALU.mult)
+        y_neg = keep.tile([P, PACK, S], F32, name="y_neg", tag="ts_all", align_bytes=ALIGN)
         for t in range(PACK):
-            nc.gpsimd.tensor_scalar(y_neg[:, t, :], y_raw[0][:, t, :], neg_wu[:, t : t + 1], 0.0, ALU.mult, ALU.add)
-        sb = scores_turned(1, (5, 6, 7, 4), (0, 1, 2, 3))
-        total[0] = keep.tile([P, PACK], F32, name="total0", tag="ts_col2", align_bytes=64)
+            nc.gpsimd.tensor_scalar(y_neg[:, t, :], y_raw[0][:, t, :], neg_wu1[:, t : t + 1], 0.0, ALU.mult, ALU.add)
+
+        upper_banks = (5, 6, 7, 4)
+        for c in range(PACK):
+            acc = bank(upper_banks[c], "aT1%d" % c)
+            mm(acc[:], qw, c * P, qx_d[1], slice(0, R), E4M3, True, True)
+            nc.scalar.activation(turned[:, c, :], acc[:], ACT.Copy, scale=ts_scores[:, c : c + 1])
+        back = [bank(t, "s1%d" % t) for t in range(PACK)]
+        for c in range(PACK):
+            for t in range(PACK):
+                nc.tensor.transpose(back[t][:, c * P : (c + 1) * P], turned[:, c, t * P : (t + 1) * P], ident[:])
+
+        total[0] = keep.tile([P, PACK], F32, name="total0", tag="ts_scores", align_bytes=ALIGN)
         for t in range(PACK):
-            max_direct(0, t)
-        hb = [bank((5, 6, 7, 4)[c], "hT%d" % c) for c in range(4)]
+            negate_and_min(0, t, work[0][:, t, :], -1.0)
+
+        sums = [bank(upper_banks[c], "hT%d" % c) for c in range(PACK)]
+
+        def turn_add(src, t, blocks, start, stop):
+            for c in blocks:
+                nc.tensor.matmul(sums[c][:, t * P : (t + 1) * P], src[:, t, c * P : (c + 1) * P], ident[:],
+                                 start=start, stop=stop, is_transpose=True)
+
         for t in range(PACK):
-            turn_add(y_neg, t, t == 0, False)
+            turn_add(y_neg, t, range(PACK), t == 0, False)
         for t in range(PACK):
             expo(0, t)
-        recip(0, 0, 2)
-        max_turned(1, sb)
-        recip(0, 2, 4)
+        recip(0, 0, GPSIMD_TILES)
+        for t in range(PACK):
+            negate_and_min(1, t, back[t][:], neg_u2[:, t : t + 1])
+        recip(0, GPSIMD_TILES, PACK)
         for t in range(PACK):
             expo(1, t)
         for t in range(PACK):
-            engine = nc.gpsimd if t < 2 else nc.vector
+            engine = nc.gpsimd if t < GPSIMD_TILES else nc.vector
             engine.tensor_scalar(work[0][:, t, :], work[0][:, t, :], inv[0][:, t : t + 1], wu[0][:, t : t + 1], ALU.mult, ALU.mult)
-            turn_add(work[0], t, False, t == PACK - 1, range(2))
+            turn_add(work[0], t, (0, 1), False, t == PACK - 1)
         for t in range(PACK):
-            turn_add(work[0], t, False, t == PACK - 1, range(2, 4))
-        windows = [window1, window2, window0]
-        turn_g(0)
+            turn_add(work[0], t, (2, 3), False, t == PACK - 1)
+
+        def scale_g1(half, ts_cols):
+            blocks = []
+            for k in range(2):
+                c = 2 * half + k
+                blocks.append(keep.tile([P, R], BF16, name="g_t%d" % c, tag="g_t%d" % k, align_bytes=ALIGN))
+                nc.scalar.activation(blocks[k][:].rearrange("i (u s e) -> i u s e", u=2, e=2),
+                                     sums[c][:].rearrange("i (u e s) -> i u s e", u=2, e=2), ACT.Copy, scale=ts_cols[:, c : c + 1])
+            return blocks
+
+        def turn_back_g1(half, blocks):
+            acc = bank(1 + half, "gw%d" % half)
+            for k in range(2):
+                pairs = blocks[k][:].bitcast(F32)
+                for u in range(2):
+                    nc.tensor.transpose(acc[:, (2 * k + u) * P : (2 * k + u + 1) * P], pairs[:, u * P : (u + 1) * P], ident[:])
+            nc.scalar.copy(g[0][half][:].bitcast(F32).rearrange("s (k i u) -> s k i u", k=2, u=2),
+                           acc[:].rearrange("s (k u i) -> s k i u", k=2, u=2))
+
+        first_blocks = scale_g1(0, ts_first)
+        x_r[1][0] = keep.tile([P, HALF * PACK], BF16, name="x_r10", tag="ts_first", align_bytes=ALIGN)
+        weave_x(1, 0, turn_x(1, 0, 0))
+        turn_back_g1(0, first_blocks)
+
         recip(1, 0, 2)
-        diff(1, 0, inv[1])
-        recip(1, 2, 3)
-        diff(1, 1, inv[1])
-        recip(1, 3, 4)
-        diff(1, 2, inv[1])
-        diff(1, 3, inv[1])
-        qx_r[1][0] = codes("qx_r10", 256, "y_raw1")
-        weave(0, 256)
-        quantise_x(1, 0)
+        for t in range(PACK):
+            diff(t)
+            if t + 2 < PACK:
+                recip(1, t + 2, t + 3)
+        weave_g2(0)
+        quantise_x_r(1, 0, "y_raw1")
         quantise_g(1, 0)
         quantise_g(0, 0)
 
         out_view = out.rearrange("(p j) n -> j p n", j=PACK)
+        result_banks = (3, 0)
 
-        def result(j, lo, hi, b):
-            acc = bank(b, "dw%d_%d" % (j, lo))
-            mm(acc[:], qx_r[1][j // 2], j % 2 * P, E4M3, qg[1], E5M2, True, False)
-            mm(acc[:], qx_r[0][j // 2], j % 2 * P, E4M3, qg[0], E5M2, False, True)
+        def multiply(j, lo):
+            acc = bank(result_banks[j % 2], "dw%d_%d" % (j, lo))
+            for h in reversed(heads):
+                mm(acc[:], qx_r[h][j // 2], j % 2 * P, qg[h], slice(0, S), E5M2, h == 1, h == 0)
             return acc
 
         def drain(j, lo, hi, acc, tag=None):
-            dw = keep.tile([P, hi - lo], F32, name="dw%d_%d" % (j, lo), tag=tag or "dw%d_%d" % (j, lo), align_bytes=64)
+            dw = keep.tile([P, hi - lo], F32, name="dw%d_%d" % (j, lo), tag=tag or "dw%d_%d" % (j, lo), align_bytes=ALIGN)
             nc.scalar.copy(dw[:], acc[:, lo:hi])
             return dw
 
         def scatter(j, lo, hi, dw):
-            nc.vector.tensor_copy(windows[j % WINDOWS][:].indirect(offsets[:, lo // 16 : hi // 16]), dw[:])
+            nc.vector.tensor_copy(windows[j % WINDOWS][:].indirect(offsets[:, lo // BAND : hi // BAND]), dw[:])
 
-        early = [result(j, 0, 256, (3, 0)[j]) for j in range(2)]
-        first = drain(0, 0, 256, early[0])
-        turn_g(1)
+        early0 = drain(0, 0, HALF, multiply(0, 0))
+        turn_back_g1(1, scale_g1(1, ts_col))
         weave_x(1, 1, turn_x(1, 1, 1))
-        g[1][1] = keep.tile([P, 1024], BF16, name="g11", tag="g00", align_bytes=64)
-        weave(256, 512)
-        qx_r[0][1] = codes("qx_r01", 256, "factor")
-        quantise_x(0, 1)
-        scatter(0, 0, 256, first)
+        early1 = multiply(1, 0)
+        g[1][1] = keep.tile([P, HALF * PACK], BF16, name="g11", tag="g00", align_bytes=ALIGN)
+        weave_g2(1)
+        scatter(0, 0, HALF, early0)
         quantise_g(1, 1)
         quantise_g(0, 1)
-        qx_r[1][1] = codes("qx_r11", 256, "g00")
-        quantise_x(1, 1)
-        scatter(1, 0, 256, drain(1, 0, 256, early[1], "g01"))
+        quantise_x_r(1, 1, "g00")
+        scatter(1, 0, HALF, drain(1, 0, HALF, early1, "g01"))
         for j in range(PACK):
-            lo = 256 if j < 2 else 0
-            scatter(j, lo, S, drain(j, lo, S, result(j, lo, S, (3, 0)[j % 2])))
+            lo = HALF if j < EARLY_TILES else 0
+            scatter(j, lo, S, drain(j, lo, S, multiply(j, lo)))
             if j < PACK - 1:
                 nc.sync.dma_start(out_view[j], windows[j % WINDOWS][:])
             else:

@@ -22,8 +22,6 @@ HALF = 256
 BAND = 16
 BANK = 512
 ALIGN = 64
-WINDOWS = 3
-EARLY_TILES = 2
 GPSIMD_TILES = 2
 FLOPS = 4 * 2 * 512 * 512 * 512
 
@@ -39,19 +37,30 @@ def tile_attend_gheads_sm_kernel(tc, x1, x2, wT, y1, u1, w1, y2, u2, w2, ts, off
         def bank(b, name):
             return psum.tile([P, BANK], F32, name=name, tag="bank%d" % b)
 
+        def sbuf(shape, dtype, name, tag=None):
+            return keep.tile(shape, dtype, name=name, tag=tag or name, align_bytes=ALIGN)
+
         def half_cols(half):
             return slice(half * HALF, (half + 1) * HALF)
 
+        def block(c):
+            return slice(c * P, (c + 1) * P)
+
         offsets = keep.tile([P, S // BAND], U16, name="offsets")
-        x_raw = [keep.tile([P, PACK, R], F32, name="x_raw%d" % h, tag="x_raw%d" % h, align_bytes=ALIGN) for h in heads]
-        w_plane = [keep.tile([P, T], F32, name="w_plane%d" % j, align_bytes=ALIGN) for j in range(PACK)]
-        y_raw = [keep.tile([P, PACK, S], F32, name="y_raw%d" % h, align_bytes=ALIGN) for h in heads]
+
+        def entries(half):
+            return offsets[:, half * HALF // BAND : (half + 1) * HALF // BAND]
+
+        x_raw = [sbuf([P, PACK, R], F32, "x_raw%d" % h) for h in heads]
+        w_plane = [sbuf([P, T], F32, "w_plane%d" % j) for j in range(PACK)]
+        y_raw = [sbuf([P, PACK, S], F32, "y_raw%d" % h) for h in heads]
         w_view = wT.rearrange("(p j) n -> j p n", j=PACK)
-        ts_win = keep.tile([P, T], F32, name="ts_win")
+        ts_win = sbuf([P, T], F32, "ts_win")
         nc.vector.memset(ts_win[:].bitcast(U32), 0)
         nc.sync.dma_start(x_raw[0][:], xs[0].rearrange("(p j) r -> p j r", j=PACK))
         nc.sync.dma_start(offsets[:], offs)
         nc.sync.dma_start(ts_win[0:1, :], ts[0:1, :])
+        nc.sync.dma_start(x_raw[1][:], xs[1].rearrange("(p j) r -> p j r", j=PACK))
         for j in range(PACK):
             nc.sync.dma_start(w_plane[j][:], w_view[j])
         u_col = [keep.tile([P, PACK], F32, name="u_col%d" % h) for h in heads]
@@ -59,29 +68,30 @@ def tile_attend_gheads_sm_kernel(tc, x1, x2, wT, y1, u1, w1, y2, u2, w2, ts, off
         for h in reversed(heads):
             nc.scalar.dma_start(u_col[h][:], us[h].rearrange("(p t) o -> p (t o)", t=PACK))
             nc.scalar.dma_start(w_col[h][:], ws[h].rearrange("(p t) o -> p (t o)", t=PACK))
-        nc.sync.dma_start(x_raw[1][:], xs[1].rearrange("(p j) r -> p j r", j=PACK))
         for h in heads:
             nc.sync.dma_start(y_raw[h][:], ys[h].rearrange("(p t) i -> p t i", t=PACK))
 
         ident = keep.tile([P, P], F32, name="ident")
         make_identity(nc, ident[:])
         neg_u2 = keep.tile([P, PACK], F32, name="neg_u")
-        wu = [keep.tile([P, PACK], F32, name="wu%d" % h) for h in heads]
+        wu = [sbuf([P, PACK], F32, "wu%d" % h) for h in heads]
         nc.gpsimd.tensor_scalar(neg_u2[:], u_col[1][:], -1.0, 0.0, ALU.mult, ALU.add)
         for h in reversed(heads):
             nc.gpsimd.tensor_tensor(wu[h][:], u_col[h][:], w_col[h][:], ALU.mult)
         neg_wu1 = keep.tile([P, PACK], F32, name="neg_wu")
         nc.gpsimd.tensor_scalar(neg_wu1[:], wu[0][:], -1.0, 0.0, ALU.mult, ALU.add)
 
-        windows = []
-        for n in range(WINDOWS):
-            windows.append(keep.tile([P, T], F32, name="window%d" % n))
-            nc.vector.memset(windows[n][:].bitcast(U32), 0)
+        windows = [None] * PACK
+
+        def zero_window(n, engine, tag=None):
+            windows[n] = sbuf([P, T], F32, "window%d" % n, tag)
+            engine.memset(windows[n][:].bitcast(U32), 0)
+
+        for n in range(PACK):
+            zero_window(n, nc.vector)
 
         def codes(name, width, tag=None):
-            words = keep.tile([P, width], U32, name=name + "_c", tag=tag or name + "_c", align_bytes=ALIGN)
-            scales = keep.tile([P, width], U8, name=name + "_s", align_bytes=ALIGN)
-            return words, scales
+            return sbuf([P, width], U32, name + "_c", tag), sbuf([P, width], U8, name + "_s")
 
         def quantise(q, cols, src, fmt):
             nc.vector.quantize_mx(out=q[0][:, cols].bitcast(fmt), scales=q[1][:, cols], in_=src)
@@ -90,16 +100,12 @@ def tile_attend_gheads_sm_kernel(tc, x1, x2, wT, y1, u1, w1, y2, u2, w2, ts, off
             nc.tensor.matmul_mx(out=acc, lhsT=lhs[0][:, lo : lo + P].bitcast(E4M3), lhsT_scale=lhs[1][:, lo : lo + P],
                                 rhs=rhs[0][:, cols].bitcast(rhs_fmt), rhs_scale=rhs[1][:, cols], start=start, stop=stop)
 
-        x_d = [[keep.tile([P, HALF * PACK], BF16, name="x_d%d%d" % (h, k), align_bytes=ALIGN) for k in range(2)] for h in heads]
-        x_r = [[keep.tile([P, HALF * PACK], BF16, name="x_r0%d" % u, align_bytes=ALIGN) for u in range(2)],
-               [None, keep.tile([P, HALF * PACK], BF16, name="x_r11", align_bytes=ALIGN)]]
+        x_d = [[sbuf([P, HALF * PACK], BF16, "x_d%d%d" % (h, k)) for k in range(2)] for h in heads]
+        x_r = [sbuf([P, 2 * HALF * PACK], BF16, "x_r%d" % u) for u in range(2)]
         qx_d = [codes("qx_d%d" % h, R) for h in heads]
-        qx_r = [[None, None], [None, None]]
-        qg = [codes("qg%d" % h, S) for h in heads]
+        qx_r = [None, None]
+        qg = [[None, None], [None, None]]
         qw = codes("qw", S)
-        for h in heads:
-            nc.gpsimd.memset(qg[h][0][:, half_cols(1)], 0)
-            nc.gpsimd.memset(qg[h][1][:, half_cols(1)].bitcast(U32), 0)
 
         def deal_x(h, k, copy):
             copy(x_d[h][k][:].rearrange("p (t s j) -> p s t j", t=2, j=PACK),
@@ -109,71 +115,80 @@ def tile_attend_gheads_sm_kernel(tc, x1, x2, wT, y1, u1, w1, y2, u2, w2, ts, off
             for k in range(2):
                 quantise(qx_d[h], half_cols(k), x_d[h][k][:], E4M3)
 
-        def turn_x(h, u, b):
-            acc = bank(b, "xw%d%d" % (h, u))
+        def turn_x(h, u):
+            acc = bank(2 + 2 * h + u, "xw%d%d" % (h, u))
             for t in range(PACK):
                 pairs = x_d[h][t // 2][:].bitcast(F32)
                 lo = 2 * P * (t % 2)
-                nc.tensor.transpose(acc[:, t * P : (t + 1) * P], pairs[:, lo + u : lo + 2 * P : 2], ident[:])
-            return acc
-
-        def weave_x(h, u, acc):
-            nc.scalar.copy(x_r[h][u][:].rearrange("s (e p t) -> s e p t", e=2, t=PACK),
+                nc.tensor.transpose(acc[:, block(t)], pairs[:, lo + u : lo + 2 * P : 2], ident[:])
+            nc.scalar.copy(x_r[u][:, h * HALF * PACK : (h + 1) * HALF * PACK].rearrange("s (e p t) -> s e p t", e=2, t=PACK),
                            acc[:].bitcast(BF16).rearrange("s (t p e) -> s e p t", t=PACK, e=2))
 
-        def quantise_x_r(h, u, tag):
-            qx_r[h][u] = codes("qx_r%d%d" % (h, u), HALF, tag)
-            quantise(qx_r[h][u], half_cols(0), x_r[h][u][:], E4M3)
+        def quantise_x_r(u, tag):
+            qx_r[u] = codes("qx_r%d" % u, 2 * HALF, tag)
+            quantise(qx_r[u], slice(0, 2 * HALF), x_r[u][:], E4M3)
 
-        ts_row = keep.tile([P, S], F32, name="ts_row")
-        nc.vector.tensor_copy(ts_row[:], ts_win[:].indirect(offsets[:]))
         for k in range(2):
             deal_x(0, k, nc.scalar.copy)
+        for k in range(2):
+            deal_x(1, k, nc.vector.tensor_copy)
+        for h in heads:
+            turn_x(h, 0)
+        ts_row = sbuf([P, S], F32, "ts_row", "x_raw1")
+        nc.scalar.activation(ts_row[:], ts_win[:].indirect(offsets[:]), ACT.Copy)
         ts_bank = bank(0, "ts_turned")
         for c in range(PACK):
-            nc.tensor.transpose(ts_bank[:, c * P : (c + 1) * P], ts_row[:, c * P : (c + 1) * P], ident[:])
+            nc.tensor.transpose(ts_bank[:, block(c)], ts_row[:, block(c)], ident[:])
+        turn_x(0, 1)
         ts_col = keep.tile([P, PACK], F32, name="ts_col")
         nc.scalar.copy(ts_col[:], ts_bank[:, 0:S:P])
-        ts_scores = keep.tile([P, PACK], F32, name="ts_scores", align_bytes=ALIGN)
-        nc.scalar.copy(ts_scores[:], ts_bank[:, 0:S:P])
-        ts_first = keep.tile([P, 2], F32, name="ts_first", align_bytes=ALIGN)
-        nc.scalar.copy(ts_first[:], ts_bank[:, 0:HALF:P])
         spread_bank = bank(1, "ts_spread")
         for c in range(PACK):
-            nc.tensor.transpose(spread_bank[:, c * P : (c + 1) * P], ts_col[:, c : c + 1].to_broadcast([P, P]), ident[:])
-        ts_all = keep.tile([P, S], F32, name="ts_all", align_bytes=ALIGN)
+            nc.tensor.transpose(spread_bank[:, block(c)], ts_col[:, c : c + 1].to_broadcast([P, P]), ident[:])
+        turn_x(1, 1)
+        ts_all = sbuf([P, S], F32, "ts_all")
         nc.scalar.copy(ts_all[:], spread_bank[:])
 
-        w_d = keep.tile([P, S, PACK], BF16, name="w_d", align_bytes=ALIGN)
-        w_flat = w_d[:].rearrange("p i j -> p (i j)")
-        nc.vector.tensor_copy(w_d[:, :, 0], w_plane[0][:].indirect(offsets[:]))
-        quantise_x_d(0)
-        for u in range(2):
-            weave_x(0, u, turn_x(0, u, 2 + u))
-        factor = keep.tile([P, PACK, S], F32, name="factor", align_bytes=ALIGN)
-        for t in range(PACK):
-            nc.scalar.activation(factor[:, t, :], ts_all[:], ACT.Copy, scale=wu[1][:, t : t + 1])
-        for j in (1, 2):
+        w_d = sbuf([P, S, PACK], BF16, "w_d")
+
+        def gather(j):
             nc.vector.tensor_copy(w_d[:, :, j], w_plane[j][:].indirect(offsets[:]))
-        quantise_x_r(0, 0, "w_plane2")
 
-        direct = []
+        quantise_x_d(0)
+        gather(0)
+        quantise_x_d(1)
+        gather(1)
+        quantise_x_r(0, "w_plane1")
+        gather(2)
         for half in range(2):
-            entries = offsets[:, half * HALF // BAND : (half + 1) * HALF // BAND]
-            nc.vector.tensor_copy(w_d[:, half_cols(half), 3], w_plane[3][:].indirect(entries))
-            quantise(qw, half_cols(half), w_flat[:, half * HALF * PACK : (half + 1) * HALF * PACK], E4M3)
-            for t in range(PACK):
-                if t % 2 == 0:
-                    direct.append(bank(2 * half + t // 2, "a1_%d%d" % (half, t)))
-                mm(direct[-1][:, half_cols(t % 2)], qx_d[0], t * P, qw, half_cols(half), E4M3, True, True)
+            nc.vector.tensor_copy(w_d[:, half_cols(half), 3], w_plane[3][:].indirect(entries(half)))
 
-        work = [None, keep.tile([P, PACK, S], F32, name="work1", align_bytes=ALIGN)]
+        direct = [bank(t, "a1_%d" % t) for t in range(PACK)]
+        turned = sbuf([P, PACK, R], F32, "turned")
+        upper_banks = (4, 7, 0, 1)
+
+        def turned_pass(c):
+            acc = bank(upper_banks[c], "aT1%d" % c)
+            mm(acc[:], qw, c * P, qx_d[1], slice(0, R), E4M3, True, True)
+            nc.scalar.activation(turned[:, c, :], acc[:], ACT.Copy, scale=ts_col[:, c : c + 1])
+
+        w_flat = w_d[:].rearrange("p i j -> p (i j)")
+        for half in range(2):
+            quantise(qw, half_cols(half), w_flat[:, half * HALF * PACK : (half + 1) * HALF * PACK], E4M3)
+        factor = sbuf([P, PACK, S], F32, "factor", "w_d")
+        for t in range(PACK):
+            nc.gpsimd.tensor_scalar(factor[:, t, :], ts_all[:], wu[1][:, t : t + 1], 0.0, ALU.mult, ALU.add)
+        work = [sbuf([P, PACK, S], F32, "work%d" % h) for h in heads]
+
+        def direct_pass(t, cols, acc):
+            mm(acc[:, cols], qx_d[0], t * P, qw, cols, E4M3, True, True)
+            nc.vector.scalar_tensor_tensor(work[0][:, t, cols], acc[:, cols], u_col[0][:, t : t + 1],
+                                           ts_all[:, cols], ALU.mult, ALU.mult)
+
         neg_m = [keep.tile([P, PACK], F32, name="neg_m%d" % h) for h in heads]
-        total = [None, keep.tile([P, PACK], F32, name="total1")]
+        total = [keep.tile([P, PACK], F32, name="total%d" % h) for h in heads]
         inv = [keep.tile([P, PACK], F32, name="inv%d" % h) for h in heads]
-        g = [[keep.tile([P, HALF * PACK], BF16, name="g0%d" % half, align_bytes=ALIGN) for half in range(2)],
-             [keep.tile([P, HALF * PACK], BF16, name="g10", align_bytes=ALIGN), None]]
-        turned = keep.tile([P, PACK, R], F32, name="turned")
+        g = [[sbuf([P, HALF * PACK], BF16, "g0%d" % half) for half in range(2)], [sbuf([P, HALF * PACK], BF16, "g10"), None]]
 
         def negate_and_min(h, t, src, scalar):
             nc.vector.tensor_scalar(work[h][:, t, :], src, scalar, None, ALU.mult, ALU.min, accum_out=neg_m[h][:, t : t + 1])
@@ -185,8 +200,8 @@ def tile_attend_gheads_sm_kernel(tc, x1, x2, wT, y1, u1, w1, y2, u2, w2, ts, off
         def recip(h, lo, hi):
             nc.vector.reciprocal(inv[h][:, lo:hi], total[h][:, lo:hi])
 
-        def diff(t):
-            nc.vector.scalar_tensor_tensor(work[1][:, t, :], work[1][:, t, :], inv[1][:, t : t + 1], y_raw[1][:, t, :],
+        def diff(t, cols):
+            nc.vector.scalar_tensor_tensor(work[1][:, t, cols], work[1][:, t, cols], inv[1][:, t : t + 1], y_raw[1][:, t, cols],
                                            ALU.mult, ALU.subtract)
 
         def weave_g2(half):
@@ -197,43 +212,33 @@ def tile_attend_gheads_sm_kernel(tc, x1, x2, wT, y1, u1, w1, y2, u2, w2, ts, off
                 ALU.mult,
             )
 
-        def quantise_g(h, half):
-            quantise(qg[h], half_cols(half), g[h][half][:], E5M2)
+        def quantise_g(h, half, tag=None):
+            qg[h][half] = codes("qg%d%d" % (h, half), HALF, tag)
+            quantise(qg[h][half], half_cols(0), g[h][half][:], E5M2)
 
-        quantise_x_r(0, 1, "w_d")
-        deal_x(1, 1, nc.scalar.copy)
-        deal_x(1, 0, nc.vector.tensor_copy)
-        quantise_x_d(1)
-
-        work[0] = keep.tile([P, PACK, S], F32, name="work0", tag="x_raw1", align_bytes=ALIGN)
-        for half in range(2):
-            for t in range(PACK):
-                nc.vector.scalar_tensor_tensor(work[0][:, t, half_cols(half)], direct[2 * half + t // 2][:, half_cols(t % 2)],
-                                               u_col[0][:, t : t + 1], ts_all[:, half_cols(half)], ALU.mult, ALU.mult)
-        y_neg = keep.tile([P, PACK, S], F32, name="y_neg", tag="ts_all", align_bytes=ALIGN)
+        for t in range(PACK):
+            if t == 0:
+                direct_pass(t, half_cols(0), bank(7, "a1_first"))
+                turned_pass(0)
+            direct_pass(t, half_cols(1) if t == 0 else slice(0, S), direct[t])
+            negate_and_min(0, t, work[0][:, t, :], -1.0)
+            if t + 1 < PACK:
+                turned_pass(t + 1)
+        y_neg = sbuf([P, PACK, S], F32, "y_neg", "wu1")
         for t in range(PACK):
             nc.gpsimd.tensor_scalar(y_neg[:, t, :], y_raw[0][:, t, :], neg_wu1[:, t : t + 1], 0.0, ALU.mult, ALU.add)
 
-        upper_banks = (5, 6, 7, 4)
-        for c in range(PACK):
-            acc = bank(upper_banks[c], "aT1%d" % c)
-            mm(acc[:], qw, c * P, qx_d[1], slice(0, R), E4M3, True, True)
-            nc.scalar.activation(turned[:, c, :], acc[:], ACT.Copy, scale=ts_scores[:, c : c + 1])
-        back = [bank(t, "s1%d" % t) for t in range(PACK)]
+        back_banks = (6, 5, 2, 3)
+        back = [bank(back_banks[t], "s1%d" % t) for t in range(PACK)]
         for c in range(PACK):
             for t in range(PACK):
-                nc.tensor.transpose(back[t][:, c * P : (c + 1) * P], turned[:, c, t * P : (t + 1) * P], ident[:])
-
-        total[0] = keep.tile([P, PACK], F32, name="total0", tag="ts_scores", align_bytes=ALIGN)
-        for t in range(PACK):
-            negate_and_min(0, t, work[0][:, t, :], -1.0)
+                nc.tensor.transpose(back[t][:, block(c)], turned[:, c, block(t)], ident[:])
 
         sums = [bank(upper_banks[c], "hT%d" % c) for c in range(PACK)]
 
         def turn_add(src, t, blocks, start, stop):
             for c in blocks:
-                nc.tensor.matmul(sums[c][:, t * P : (t + 1) * P], src[:, t, c * P : (c + 1) * P], ident[:],
-                                 start=start, stop=stop, is_transpose=True)
+                nc.tensor.matmul(sums[c][:, block(t)], src[:, t, block(c)], ident[:], start=start, stop=stop, is_transpose=True)
 
         for t in range(PACK):
             turn_add(y_neg, t, range(PACK), t == 0, False)
@@ -252,72 +257,87 @@ def tile_attend_gheads_sm_kernel(tc, x1, x2, wT, y1, u1, w1, y2, u2, w2, ts, off
         for t in range(PACK):
             turn_add(work[0], t, (2, 3), False, t == PACK - 1)
 
-        def scale_g1(half, ts_cols):
+        def scale_g1(half):
             blocks = []
             for k in range(2):
                 c = 2 * half + k
-                blocks.append(keep.tile([P, R], BF16, name="g_t%d" % c, tag="g_t%d" % k, align_bytes=ALIGN))
+                blocks.append(sbuf([P, R], BF16, "g_t%d" % c, "g_t%d" % (c % 3)))
                 nc.scalar.activation(blocks[k][:].rearrange("i (u s e) -> i u s e", u=2, e=2),
-                                     sums[c][:].rearrange("i (u e s) -> i u s e", u=2, e=2), ACT.Copy, scale=ts_cols[:, c : c + 1])
+                                     sums[c][:].rearrange("i (u e s) -> i u s e", u=2, e=2), ACT.Copy, scale=ts_col[:, c : c + 1])
             return blocks
 
         def turn_back_g1(half, blocks):
-            acc = bank(1 + half, "gw%d" % half)
+            acc = bank(back_banks[1 + half], "gw%d" % half)
             for k in range(2):
                 pairs = blocks[k][:].bitcast(F32)
                 for u in range(2):
-                    nc.tensor.transpose(acc[:, (2 * k + u) * P : (2 * k + u + 1) * P], pairs[:, u * P : (u + 1) * P], ident[:])
+                    nc.tensor.transpose(acc[:, block(2 * k + u)], pairs[:, block(u)], ident[:])
+            return acc
+
+        def copy_g1(half, acc):
             nc.scalar.copy(g[0][half][:].bitcast(F32).rearrange("s (k i u) -> s k i u", k=2, u=2),
                            acc[:].rearrange("s (k u i) -> s k i u", k=2, u=2))
 
-        first_blocks = scale_g1(0, ts_first)
-        x_r[1][0] = keep.tile([P, HALF * PACK], BF16, name="x_r10", tag="ts_first", align_bytes=ALIGN)
-        weave_x(1, 0, turn_x(1, 0, 0))
-        turn_back_g1(0, first_blocks)
+        copy_g1(0, turn_back_g1(0, scale_g1(0)))
 
         recip(1, 0, 2)
         for t in range(PACK):
-            diff(t)
+            diff(t, slice(0, S) if t < 3 else half_cols(0))
             if t + 2 < PACK:
                 recip(1, t + 2, t + 3)
         weave_g2(0)
-        quantise_x_r(1, 0, "y_raw1")
-        quantise_g(1, 0)
         quantise_g(0, 0)
+        quantise_g(1, 0, "g00")
+        diff(PACK - 1, half_cols(1))
 
         out_view = out.rearrange("(p j) n -> j p n", j=PACK)
-        result_banks = (3, 0)
 
-        def multiply(j, lo):
-            acc = bank(result_banks[j % 2], "dw%d_%d" % (j, lo))
-            for h in reversed(heads):
-                mm(acc[:], qx_r[h][j // 2], j % 2 * P, qg[h], slice(0, S), E5M2, h == 1, h == 0)
-            return acc
+        def multiply(j, half, acc):
+            for h in heads:
+                mm(acc, qx_r[j // 2], h * HALF + j % 2 * P, qg[h][half], half_cols(0), E5M2, h == 0, h == 1)
 
-        def drain(j, lo, hi, acc, tag=None):
-            dw = keep.tile([P, hi - lo], F32, name="dw%d_%d" % (j, lo), tag=tag or "dw%d_%d" % (j, lo), align_bytes=ALIGN)
-            nc.scalar.copy(dw[:], acc[:, lo:hi])
+        def drain(name, acc, width, copy, tag=None):
+            dw = sbuf([P, width], F32, name, tag)
+            copy(dw[:], acc[:, 0:width])
             return dw
 
-        def scatter(j, lo, hi, dw):
-            nc.vector.tensor_copy(windows[j % WINDOWS][:].indirect(offsets[:, lo // BAND : hi // BAND]), dw[:])
+        def scatter_half(j, half, src):
+            nc.scalar.activation(windows[j][:].indirect(entries(half)), src, ACT.Copy)
 
-        early0 = drain(0, 0, HALF, multiply(0, 0))
-        turn_back_g1(1, scale_g1(1, ts_col))
-        weave_x(1, 1, turn_x(1, 1, 1))
-        early1 = multiply(1, 0)
-        g[1][1] = keep.tile([P, HALF * PACK], BF16, name="g11", tag="g00", align_bytes=ALIGN)
+        def store(j):
+            nc.sync.dma_start(out_view[j], windows[j][:])
+
+        early = bank(3, "early")
+        multiply(0, 0, early[:, half_cols(0)])
+        copy_g1(1, turn_back_g1(1, scale_g1(1)))
+        late = bank(6, "late")
+        multiply(1, 0, late[:, half_cols(0)])
+        scatter_half(0, 0, drain("dw_early", early, HALF, nc.scalar.copy, "g_t0")[:])
+        g[1][1] = sbuf([P, HALF * PACK], BF16, "g11", "g10")
         weave_g2(1)
-        scatter(0, 0, HALF, early0)
-        quantise_g(1, 1)
         quantise_g(0, 1)
-        quantise_x_r(1, 1, "g00")
-        scatter(1, 0, HALF, drain(1, 0, HALF, early1, "g01"))
-        for j in range(PACK):
-            lo = HALF if j < EARLY_TILES else 0
-            scatter(j, lo, S, drain(j, lo, S, multiply(j, lo)))
-            if j < PACK - 1:
-                nc.sync.dma_start(out_view[j], windows[j % WINDOWS][:])
-            else:
-                nc.sync.dma_start(out_view[j][:, 0 : T // 2], windows[j % WINDOWS][:, 0 : T // 2])
-                nc.scalar.dma_start(out_view[j][:, T // 2 : T], windows[j % WINDOWS][:, T // 2 : T])
+        quantise_g(1, 1, "g01")
+        multiply(0, 1, late[:, half_cols(1)])
+        rest = bank(4, "rest")
+        multiply(1, 1, rest[:, half_cols(0)])
+        quantise_x_r(1, "g10")
+        dw_late = drain("dw_late", late, S, nc.vector.tensor_copy)
+        nc.vector.tensor_copy(windows[0][:].indirect(entries(1)), dw_late[:, half_cols(1)])
+        store(0)
+        dw_rest = drain("dw_rest", rest, HALF, nc.scalar.copy, "g_t0")
+        scatter_half(1, 0, dw_late[:, half_cols(0)])
+        scatter_half(1, 1, dw_rest[:])
+        store(1)
+        acc2 = bank(7, "acc2")
+        for half in range(2):
+            multiply(2, half, acc2[:, half_cols(half)])
+        last = [bank(half, "last%d" % half) for half in range(2)]
+        for half in range(2):
+            multiply(3, half, last[half][:, half_cols(0)])
+        dw2 = drain("dw2", acc2, S, nc.vector.tensor_copy, "dw_late")
+        dw3 = drain("dw30", last[0], HALF, nc.vector.tensor_copy, "qg00_c")
+        nc.vector.tensor_copy(windows[2][:].indirect(offsets[:]), dw2[:])
+        store(2)
+        scatter_half(3, 0, dw3[:])
+        scatter_half(3, 1, drain("dw31", last[1], HALF, nc.scalar.copy, "g_t0")[:])
+        store(3)

@@ -74,12 +74,13 @@ def tile_attend_gheads_sm_kernel(tc, x1, x2, wT, y1, u1, w1, y2, u2, w2, ts, off
         ident = keep.tile([P, P], F32, name="ident")
         make_identity(nc, ident[:])
         neg_u2 = keep.tile([P, PACK], F32, name="neg_u")
-        wu = [sbuf([P, PACK], F32, "wu%d" % h) for h in heads]
+        wu1 = keep.tile([P, PACK], F32, name="wu1")
+        wu2 = keep.tile([P, 1], F32, name="wu2")
         nc.gpsimd.tensor_scalar(neg_u2[:], u_col[1][:], -1.0, 0.0, ALU.mult, ALU.add)
-        for h in reversed(heads):
-            nc.gpsimd.tensor_tensor(wu[h][:], u_col[h][:], w_col[h][:], ALU.mult)
+        nc.gpsimd.tensor_tensor(wu2[:], u_col[1][:, 0:1], w_col[1][:, 0:1], ALU.mult)
+        nc.gpsimd.tensor_tensor(wu1[:], u_col[0][:], w_col[0][:], ALU.mult)
         neg_wu1 = keep.tile([P, PACK], F32, name="neg_wu")
-        nc.gpsimd.tensor_scalar(neg_wu1[:], wu[0][:], -1.0, 0.0, ALU.mult, ALU.add)
+        nc.gpsimd.tensor_scalar(neg_wu1[:], wu1[:], -1.0, 0.0, ALU.mult, ALU.add)
 
         windows = [None] * PACK
 
@@ -148,6 +149,8 @@ def tile_attend_gheads_sm_kernel(tc, x1, x2, wT, y1, u1, w1, y2, u2, w2, ts, off
         turn_x(1, 1)
         ts_all = sbuf([P, S], F32, "ts_all")
         nc.scalar.copy(ts_all[:], spread_bank[:])
+        factor = sbuf([P, PACK, S], F32, "factor")
+        nc.scalar.activation(factor[:, 0, :], ts_all[:], ACT.Copy, scale=wu2[:])
 
         w_d = sbuf([P, S, PACK], BF16, "w_d")
 
@@ -175,9 +178,11 @@ def tile_attend_gheads_sm_kernel(tc, x1, x2, wT, y1, u1, w1, y2, u2, w2, ts, off
         w_flat = w_d[:].rearrange("p i j -> p (i j)")
         for half in range(2):
             quantise(qw, half_cols(half), w_flat[:, half * HALF * PACK : (half + 1) * HALF * PACK], E4M3)
-        factor = sbuf([P, PACK, S], F32, "factor", "w_d")
-        for t in range(PACK):
-            nc.gpsimd.tensor_scalar(factor[:, t, :], ts_all[:], wu[1][:, t : t + 1], 0.0, ALU.mult, ALU.add)
+        quantise_x_r(1, "w_plane3")
+        wu_late = sbuf([P, PACK - 1], F32, "wu_late", "x_r1")
+        nc.vector.tensor_tensor(wu_late[:], u_col[1][:, 1:PACK], w_col[1][:, 1:PACK], ALU.mult)
+        for t in range(1, PACK):
+            nc.gpsimd.tensor_scalar(factor[:, t, :], ts_all[:], wu_late[:, t - 1 : t], 0.0, ALU.mult, ALU.add)
         work = [sbuf([P, PACK, S], F32, "work%d" % h) for h in heads]
 
         def direct_pass(t, cols, acc):
@@ -224,7 +229,7 @@ def tile_attend_gheads_sm_kernel(tc, x1, x2, wT, y1, u1, w1, y2, u2, w2, ts, off
             negate_and_min(0, t, work[0][:, t, :], -1.0)
             if t + 1 < PACK:
                 turned_pass(t + 1)
-        y_neg = sbuf([P, PACK, S], F32, "y_neg", "wu1")
+        y_neg = sbuf([P, PACK, S], F32, "y_neg", "x_r1")
         for t in range(PACK):
             nc.gpsimd.tensor_scalar(y_neg[:, t, :], y_raw[0][:, t, :], neg_wu1[:, t : t + 1], 0.0, ALU.mult, ALU.add)
 
@@ -252,7 +257,7 @@ def tile_attend_gheads_sm_kernel(tc, x1, x2, wT, y1, u1, w1, y2, u2, w2, ts, off
             expo(1, t)
         for t in range(PACK):
             engine = nc.gpsimd if t < GPSIMD_TILES else nc.vector
-            engine.tensor_scalar(work[0][:, t, :], work[0][:, t, :], inv[0][:, t : t + 1], wu[0][:, t : t + 1], ALU.mult, ALU.mult)
+            engine.tensor_scalar(work[0][:, t, :], work[0][:, t, :], inv[0][:, t : t + 1], wu1[:, t : t + 1], ALU.mult, ALU.mult)
             turn_add(work[0], t, (0, 1), False, t == PACK - 1)
         for t in range(PACK):
             turn_add(work[0], t, (2, 3), False, t == PACK - 1)
@@ -310,34 +315,34 @@ def tile_attend_gheads_sm_kernel(tc, x1, x2, wT, y1, u1, w1, y2, u2, w2, ts, off
         early = bank(3, "early")
         multiply(0, 0, early[:, half_cols(0)])
         copy_g1(1, turn_back_g1(1, scale_g1(1)))
-        late = bank(6, "late")
-        multiply(1, 0, late[:, half_cols(0)])
-        scatter_half(0, 0, drain("dw_early", early, HALF, nc.scalar.copy, "g_t0")[:])
+        second_tile = bank(6, "second_tile")
+        multiply(1, 0, second_tile[:, half_cols(0)])
+        last_first = bank(4, "last_first")
+        for j in range(2, PACK):
+            multiply(j, 0, last_first[:, half_cols(j - 2)])
+        scatter_half(0, 0, drain("dw00", early, HALF, nc.scalar.copy, "g_t0")[:])
         g[1][1] = sbuf([P, HALF * PACK], BF16, "g11", "g10")
         weave_g2(1)
         quantise_g(0, 1)
         quantise_g(1, 1, "g01")
-        multiply(0, 1, late[:, half_cols(1)])
-        rest = bank(4, "rest")
-        multiply(1, 1, rest[:, half_cols(0)])
-        quantise_x_r(1, "g10")
-        dw_late = drain("dw_late", late, S, nc.vector.tensor_copy)
-        nc.vector.tensor_copy(windows[0][:].indirect(entries(1)), dw_late[:, half_cols(1)])
-        store(0)
-        dw_rest = drain("dw_rest", rest, HALF, nc.scalar.copy, "g_t0")
-        scatter_half(1, 0, dw_late[:, half_cols(0)])
-        scatter_half(1, 1, dw_rest[:])
-        store(1)
-        acc2 = bank(7, "acc2")
-        for half in range(2):
-            multiply(2, half, acc2[:, half_cols(half)])
-        last = [bank(half, "last%d" % half) for half in range(2)]
-        for half in range(2):
-            multiply(3, half, last[half][:, half_cols(0)])
-        dw2 = drain("dw2", acc2, S, nc.vector.tensor_copy, "dw_late")
-        dw3 = drain("dw30", last[0], HALF, nc.vector.tensor_copy, "qg00_c")
-        nc.vector.tensor_copy(windows[2][:].indirect(offsets[:]), dw2[:])
-        store(2)
-        scatter_half(3, 0, dw3[:])
-        scatter_half(3, 1, drain("dw31", last[1], HALF, nc.scalar.copy, "g_t0")[:])
-        store(3)
+        late = [bank(b, "late%d" % b) for b in (7, 5)]
+        for j in range(2):
+            multiply(j, 1, late[j][:, half_cols(0)])
+        last_second = bank(0, "last_second")
+        for j in range(2, PACK):
+            multiply(j, 1, last_second[:, half_cols(j - 2)])
+
+        def finish(j, src):
+            nc.vector.tensor_copy(windows[j][:].indirect(entries(1)), src)
+            store(j)
+
+        dw10 = drain("dw10", second_tile, HALF, nc.vector.tensor_copy, "g10")
+        dw_late = [drain("dw%d1" % j, late[j], HALF, nc.vector.tensor_copy) for j in range(2)]
+        finish(0, dw_late[0][:])
+        scatter_half(1, 0, dw10[:])
+        finish(1, dw_late[1][:])
+        dw_first = drain("dw_first", last_first, S, nc.scalar.copy, "g10")
+        dw_second = drain("dw_second", last_second, S, nc.vector.tensor_copy, "dw11")
+        for j in range(2, PACK):
+            scatter_half(j, 0, dw_first[:, half_cols(j - 2)])
+            finish(j, dw_second[:, half_cols(j - 2)])

@@ -22,7 +22,6 @@ HALF = 256
 BAND = 16
 BANK = 512
 ALIGN = 64
-GPSIMD_TILES = 2
 FLOPS = 4 * 2 * 512 * 512 * 512
 
 
@@ -32,6 +31,7 @@ def tile_attend_gheads_sm_kernel(tc, x1, x2, wT, y1, u1, w1, y2, u2, w2, ts, off
     heads = (0, 1)
     with ExitStack() as ctx:
         keep = ctx.enter_context(tc.tile_pool(name="keep", bufs=1))
+        last = ctx.enter_context(tc.tile_pool(name="last", bufs=1))
         psum = ctx.enter_context(tc.psum_pool(name="psum", bufs=1))
 
         def bank(b, name):
@@ -52,11 +52,12 @@ def tile_attend_gheads_sm_kernel(tc, x1, x2, wT, y1, u1, w1, y2, u2, w2, ts, off
             return offsets[:, half * HALF // BAND : (half + 1) * HALF // BAND]
 
         x_raw = [sbuf([P, PACK, R], F32, "x_raw%d" % h) for h in heads]
-        w_plane = [sbuf([P, T], F32, "w_plane%d" % j) for j in range(PACK)]
+        w_plane = [sbuf([P, T], F32, "w_plane%d" % j) for j in range(PACK - 1)]
+        w_plane.append(last.tile([P, T], F32, name="w_plane3", align_bytes=ALIGN, offset=0))
         y_raw = [sbuf([P, PACK, S], F32, "y_raw%d" % h) for h in heads]
         w_view = wT.rearrange("(p j) n -> j p n", j=PACK)
         ts_win = sbuf([P, T], F32, "ts_win")
-        nc.vector.memset(ts_win[:].bitcast(U32), 0)
+        nc.gpsimd.memset(ts_win[:].bitcast(U32), 0)
         nc.sync.dma_start(x_raw[0][:], xs[0].rearrange("(p j) r -> p j r", j=PACK))
         nc.sync.dma_start(offsets[:], offs)
         nc.sync.dma_start(ts_win[0:1, :], ts[0:1, :])
@@ -73,23 +74,20 @@ def tile_attend_gheads_sm_kernel(tc, x1, x2, wT, y1, u1, w1, y2, u2, w2, ts, off
 
         ident = keep.tile([P, P], F32, name="ident")
         make_identity(nc, ident[:])
+        windows = [sbuf([P, T], F32, "window%d" % n) for n in range(PACK)]
+        nc.gpsimd.memset(windows[0][:].bitcast(U32), 0)
+        for n in (1, 2):
+            nc.vector.memset(windows[n][:, 0 : T // 2 - 1].bitcast(U32), 0)
+            nc.vector.memset(windows[n][:, T // 2 - 1 : T].bitcast(U32), 0)
+        nc.vector.memset(windows[3][:].bitcast(U32), 0)
+
         neg_u2 = keep.tile([P, PACK], F32, name="neg_u")
-        wu1 = keep.tile([P, PACK], F32, name="wu1")
-        wu2 = keep.tile([P, 1], F32, name="wu2")
+        wu = [keep.tile([P, PACK - 2 * h], F32, name="wu%d" % h) for h in heads]
         nc.gpsimd.tensor_scalar(neg_u2[:], u_col[1][:], -1.0, 0.0, ALU.mult, ALU.add)
-        nc.gpsimd.tensor_tensor(wu2[:], u_col[1][:, 0:1], w_col[1][:, 0:1], ALU.mult)
-        nc.gpsimd.tensor_tensor(wu1[:], u_col[0][:], w_col[0][:], ALU.mult)
+        for h in reversed(heads):
+            nc.gpsimd.tensor_tensor(wu[h][:], u_col[h][:, 0 : PACK - 2 * h], w_col[h][:, 0 : PACK - 2 * h], ALU.mult)
         neg_wu1 = keep.tile([P, PACK], F32, name="neg_wu")
-        nc.gpsimd.tensor_scalar(neg_wu1[:], wu1[:], -1.0, 0.0, ALU.mult, ALU.add)
-
-        windows = [None] * PACK
-
-        def zero_window(n, engine, tag=None):
-            windows[n] = sbuf([P, T], F32, "window%d" % n, tag)
-            engine.memset(windows[n][:].bitcast(U32), 0)
-
-        for n in range(PACK):
-            zero_window(n, nc.vector)
+        nc.gpsimd.tensor_scalar(neg_wu1[:], wu[0][:], -1.0, 0.0, ALU.mult, ALU.add)
 
         def codes(name, width, tag=None):
             return sbuf([P, width], U32, name + "_c", tag), sbuf([P, width], U8, name + "_s")
@@ -104,7 +102,8 @@ def tile_attend_gheads_sm_kernel(tc, x1, x2, wT, y1, u1, w1, y2, u2, w2, ts, off
         x_d = [[sbuf([P, HALF * PACK], BF16, "x_d%d%d" % (h, k)) for k in range(2)] for h in heads]
         x_r = [sbuf([P, 2 * HALF * PACK], BF16, "x_r%d" % u) for u in range(2)]
         qx_d = [codes("qx_d%d" % h, R) for h in heads]
-        qx_r = [None, None]
+        qx_r = [codes("qx_r0", 2 * HALF),
+                (last.tile([P, 2 * HALF], U32, name="qx_r1_c", align_bytes=ALIGN, offset=4096), sbuf([P, 2 * HALF], U8, "qx_r1_s"))]
         qg = [[None, None], [None, None]]
         qw = codes("qw", S)
 
@@ -125,75 +124,76 @@ def tile_attend_gheads_sm_kernel(tc, x1, x2, wT, y1, u1, w1, y2, u2, w2, ts, off
             nc.scalar.copy(x_r[u][:, h * HALF * PACK : (h + 1) * HALF * PACK].rearrange("s (e p t) -> s e p t", e=2, t=PACK),
                            acc[:].bitcast(BF16).rearrange("s (t p e) -> s e p t", t=PACK, e=2))
 
-        def quantise_x_r(u, tag):
-            qx_r[u] = codes("qx_r%d" % u, 2 * HALF, tag)
+        def quantise_x_r(u):
             quantise(qx_r[u], slice(0, 2 * HALF), x_r[u][:], E4M3)
 
-        for k in range(2):
-            deal_x(0, k, nc.scalar.copy)
+        deal_x(0, 0, nc.scalar.copy)
+        deal_x(0, 1, nc.vector.tensor_copy)
         for k in range(2):
             deal_x(1, k, nc.vector.tensor_copy)
-        for h in heads:
-            turn_x(h, 0)
-        ts_row = sbuf([P, S], F32, "ts_row", "x_raw1")
+        turn_x(0, 0)
+        ts_row = sbuf([P, S], F32, "ts_row")
         nc.scalar.activation(ts_row[:], ts_win[:].indirect(offsets[:]), ACT.Copy)
+        turn_x(0, 1)
         ts_bank = bank(0, "ts_turned")
         for c in range(PACK):
             nc.tensor.transpose(ts_bank[:, block(c)], ts_row[:, block(c)], ident[:])
-        turn_x(0, 1)
         ts_col = keep.tile([P, PACK], F32, name="ts_col")
         nc.scalar.copy(ts_col[:], ts_bank[:, 0:S:P])
+        turn_x(1, 0)
+        turn_x(1, 1)
         spread_bank = bank(1, "ts_spread")
         for c in range(PACK):
             nc.tensor.transpose(spread_bank[:, block(c)], ts_col[:, c : c + 1].to_broadcast([P, P]), ident[:])
-        turn_x(1, 1)
         ts_all = sbuf([P, S], F32, "ts_all")
         nc.scalar.copy(ts_all[:], spread_bank[:])
-        factor = sbuf([P, PACK, S], F32, "factor")
-        nc.scalar.activation(factor[:, 0, :], ts_all[:], ACT.Copy, scale=wu2[:])
 
         w_d = sbuf([P, S, PACK], BF16, "w_d")
 
         def gather(j):
             nc.vector.tensor_copy(w_d[:, :, j], w_plane[j][:].indirect(offsets[:]))
 
+        def gather_halves(j):
+            nc.vector.tensor_copy(w_d[:, half_cols(0), j], w_plane[j][:].indirect(entries(0)))
+            nc.scalar.activation(w_d[:, half_cols(1), j], w_plane[j][:].indirect(entries(1)), ACT.Copy)
+
         quantise_x_d(0)
-        gather(0)
         quantise_x_d(1)
+        gather(0)
         gather(1)
-        quantise_x_r(0, "w_plane1")
-        gather(2)
-        for half in range(2):
-            nc.vector.tensor_copy(w_d[:, half_cols(half), 3], w_plane[3][:].indirect(entries(half)))
-
-        direct = [bank(t, "a1_%d" % t) for t in range(PACK)]
-        turned = sbuf([P, PACK, R], F32, "turned")
-        upper_banks = (4, 7, 0, 1)
-
-        def turned_pass(c):
-            acc = bank(upper_banks[c], "aT1%d" % c)
-            mm(acc[:], qw, c * P, qx_d[1], slice(0, R), E4M3, True, True)
-            nc.scalar.activation(turned[:, c, :], acc[:], ACT.Copy, scale=ts_col[:, c : c + 1])
+        quantise_x_r(0)
+        gather_halves(2)
+        gather_halves(3)
+        factor = sbuf([P, PACK, S], F32, "factor")
+        wu_late = last.tile([P, 2], F32, name="wu_late", align_bytes=ALIGN, offset=0)
+        for t in range(2):
+            nc.scalar.activation(factor[:, t, :], ts_all[:], ACT.Copy, scale=wu[1][:, t : t + 1])
+        for t in range(2):
+            nc.scalar.activation(wu_late[:, t : t + 1], u_col[1][:, t + 2 : t + 3], ACT.Copy, scale=w_col[1][:, t + 2 : t + 3])
+        for t in range(2):
+            nc.scalar.activation(factor[:, t + 2, :], ts_all[:], ACT.Copy, scale=wu_late[:, t : t + 1])
 
         w_flat = w_d[:].rearrange("p i j -> p (i j)")
         for half in range(2):
             quantise(qw, half_cols(half), w_flat[:, half * HALF * PACK : (half + 1) * HALF * PACK], E4M3)
-        quantise_x_r(1, "w_plane3")
-        wu_late = sbuf([P, PACK - 1], F32, "wu_late", "x_r1")
-        nc.vector.tensor_tensor(wu_late[:], u_col[1][:, 1:PACK], w_col[1][:, 1:PACK], ALU.mult)
-        for t in range(1, PACK):
-            nc.gpsimd.tensor_scalar(factor[:, t, :], ts_all[:], wu_late[:, t - 1 : t], 0.0, ALU.mult, ALU.add)
+        quantise_x_r(1)
+
+        turned = sbuf([P, PACK, R], F32, "turned")
         work = [sbuf([P, PACK, S], F32, "work%d" % h) for h in heads]
+        neg_m = [keep.tile([P, PACK], F32, name="neg_m%d" % h) for h in heads]
+        total = [keep.tile([P, PACK], F32, name="total%d" % h) for h in heads]
+        inv = [sbuf([P, PACK], F32, "inv0"), None]
+        g = [[sbuf([P, HALF * PACK], BF16, "g0%d" % half) for half in range(2)], [sbuf([P, HALF * PACK], BF16, "g10"), None]]
+
+        def turned_pass(c):
+            acc = bank(2 + c % 2, "aT1%d" % c)
+            mm(acc[:], qw, c * P, qx_d[1], slice(0, R), E4M3, True, True)
+            nc.scalar.activation(turned[:, c, :], acc[:], ACT.Copy, scale=ts_col[:, c : c + 1])
 
         def direct_pass(t, cols, acc):
             mm(acc[:, cols], qx_d[0], t * P, qw, cols, E4M3, True, True)
             nc.vector.scalar_tensor_tensor(work[0][:, t, cols], acc[:, cols], u_col[0][:, t : t + 1],
                                            ts_all[:, cols], ALU.mult, ALU.mult)
-
-        neg_m = [keep.tile([P, PACK], F32, name="neg_m%d" % h) for h in heads]
-        total = [keep.tile([P, PACK], F32, name="total%d" % h) for h in heads]
-        inv = [keep.tile([P, PACK], F32, name="inv%d" % h) for h in heads]
-        g = [[sbuf([P, HALF * PACK], BF16, "g0%d" % half) for half in range(2)], [sbuf([P, HALF * PACK], BF16, "g10"), None]]
 
         def negate_and_min(h, t, src, scalar):
             nc.vector.tensor_scalar(work[h][:, t, :], src, scalar, None, ALU.mult, ALU.min, accum_out=neg_m[h][:, t : t + 1])
@@ -209,55 +209,45 @@ def tile_attend_gheads_sm_kernel(tc, x1, x2, wT, y1, u1, w1, y2, u2, w2, ts, off
             nc.vector.scalar_tensor_tensor(work[1][:, t, cols], work[1][:, t, cols], inv[1][:, t : t + 1], y_raw[1][:, t, cols],
                                            ALU.mult, ALU.subtract)
 
-        def weave_g2(half):
-            nc.vector.tensor_tensor(
-                g[1][half][:].rearrange("p (c i t) -> p c t i", i=2, t=PACK),
-                work[1][:, :, half_cols(half)].rearrange("p t (c i) -> p c t i", i=2),
-                factor[:, :, half_cols(half)].rearrange("p t (c i) -> p c t i", i=2),
-                ALU.mult,
-            )
-
         def quantise_g(h, half, tag=None):
             qg[h][half] = codes("qg%d%d" % (h, half), HALF, tag)
             quantise(qg[h][half], half_cols(0), g[h][half][:], E5M2)
 
+        direct_pass(0, half_cols(0), bank(7, "a1_first"))
         for t in range(PACK):
+            turned_pass(t)
             if t == 0:
-                direct_pass(t, half_cols(0), bank(7, "a1_first"))
-                turned_pass(0)
-            direct_pass(t, half_cols(1) if t == 0 else slice(0, S), direct[t])
-            negate_and_min(0, t, work[0][:, t, :], -1.0)
+                direct_pass(t, half_cols(1), bank(0, "a1_0"))
             if t + 1 < PACK:
-                turned_pass(t + 1)
-        y_neg = sbuf([P, PACK, S], F32, "y_neg", "x_r1")
+                direct_pass(t + 1, slice(0, S), bank((t + 1) % 2, "a1_%d" % (t + 1)))
+            negate_and_min(0, t, work[0][:, t, :], -1.0)
         for t in range(PACK):
-            nc.gpsimd.tensor_scalar(y_neg[:, t, :], y_raw[0][:, t, :], neg_wu1[:, t : t + 1], 0.0, ALU.mult, ALU.add)
+            expo(0, t)
 
-        back_banks = (6, 5, 2, 3)
+        back_banks = (2, 3, 0, 1)
         back = [bank(back_banks[t], "s1%d" % t) for t in range(PACK)]
-        for c in range(PACK):
-            for t in range(PACK):
+        for t in range(PACK):
+            for c in range(PACK):
                 nc.tensor.transpose(back[t][:, block(c)], turned[:, c, block(t)], ident[:])
 
-        sums = [bank(upper_banks[c], "hT%d" % c) for c in range(PACK)]
+        y_neg = sbuf([P, PACK, S], F32, "y_neg", "x_r1")
+        sums = [bank(PACK + c, "hT%d" % c) for c in range(PACK)]
 
         def turn_add(src, t, blocks, start, stop):
             for c in blocks:
                 nc.tensor.matmul(sums[c][:, block(t)], src[:, t, block(c)], ident[:], start=start, stop=stop, is_transpose=True)
 
         for t in range(PACK):
+            nc.gpsimd.tensor_scalar(y_neg[:, t, :], y_raw[0][:, t, :], neg_wu1[:, t : t + 1], 0.0, ALU.mult, ALU.add)
             turn_add(y_neg, t, range(PACK), t == 0, False)
+
         for t in range(PACK):
-            expo(0, t)
-        recip(0, 0, GPSIMD_TILES)
+            recip(0, t, t + 1)
         for t in range(PACK):
             negate_and_min(1, t, back[t][:], neg_u2[:, t : t + 1])
-        recip(0, GPSIMD_TILES, PACK)
-        for t in range(PACK):
             expo(1, t)
         for t in range(PACK):
-            engine = nc.gpsimd if t < GPSIMD_TILES else nc.vector
-            engine.tensor_scalar(work[0][:, t, :], work[0][:, t, :], inv[0][:, t : t + 1], wu1[:, t : t + 1], ALU.mult, ALU.mult)
+            nc.gpsimd.tensor_scalar(work[0][:, t, :], work[0][:, t, :], inv[0][:, t : t + 1], wu[0][:, t : t + 1], ALU.mult, ALU.mult)
             turn_add(work[0], t, (0, 1), False, t == PACK - 1)
         for t in range(PACK):
             turn_add(work[0], t, (2, 3), False, t == PACK - 1)
@@ -272,7 +262,7 @@ def tile_attend_gheads_sm_kernel(tc, x1, x2, wT, y1, u1, w1, y2, u2, w2, ts, off
             return blocks
 
         def turn_back_g1(half, blocks):
-            acc = bank(back_banks[1 + half], "gw%d" % half)
+            acc = bank(2 + half, "gw%d" % half)
             for k in range(2):
                 pairs = blocks[k][:].bitcast(F32)
                 for u in range(2):
@@ -285,15 +275,25 @@ def tile_attend_gheads_sm_kernel(tc, x1, x2, wT, y1, u1, w1, y2, u2, w2, ts, off
 
         copy_g1(0, turn_back_g1(0, scale_g1(0)))
 
+        def weave_g2(half):
+            nc.vector.tensor_tensor(
+                g[1][half][:].rearrange("p (c i t) -> p c t i", i=2, t=PACK),
+                work[1][:, :, half_cols(half)].rearrange("p t (c i) -> p c t i", i=2),
+                factor[:, :, half_cols(half)].rearrange("p t (c i) -> p c t i", i=2),
+                ALU.mult,
+            )
+
+        inv[1] = sbuf([P, PACK], F32, "inv1", "inv0")
         recip(1, 0, 2)
-        for t in range(PACK):
-            diff(t, slice(0, S) if t < 3 else half_cols(0))
-            if t + 2 < PACK:
-                recip(1, t + 2, t + 3)
+        diff(0, slice(0, S))
+        recip(1, 2, PACK)
+        for t in range(1, PACK - 1):
+            diff(t, slice(0, S))
+        for half in range(2):
+            diff(PACK - 1, half_cols(half))
         weave_g2(0)
         quantise_g(0, 0)
         quantise_g(1, 0, "g00")
-        diff(PACK - 1, half_cols(1))
 
         out_view = out.rearrange("(p j) n -> j p n", j=PACK)
 
@@ -312,10 +312,10 @@ def tile_attend_gheads_sm_kernel(tc, x1, x2, wT, y1, u1, w1, y2, u2, w2, ts, off
         def store(j):
             nc.sync.dma_start(out_view[j], windows[j][:])
 
-        early = bank(3, "early")
+        early = bank(0, "early")
         multiply(0, 0, early[:, half_cols(0)])
         copy_g1(1, turn_back_g1(1, scale_g1(1)))
-        second_tile = bank(6, "second_tile")
+        second_tile = bank(1, "second_tile")
         multiply(1, 0, second_tile[:, half_cols(0)])
         last_first = bank(4, "last_first")
         for j in range(2, PACK):
@@ -325,10 +325,10 @@ def tile_attend_gheads_sm_kernel(tc, x1, x2, wT, y1, u1, w1, y2, u2, w2, ts, off
         weave_g2(1)
         quantise_g(0, 1)
         quantise_g(1, 1, "g01")
-        late = [bank(b, "late%d" % b) for b in (7, 5)]
+        late = [bank(b, "late%d" % b) for b in (5, 6)]
         for j in range(2):
             multiply(j, 1, late[j][:, half_cols(0)])
-        last_second = bank(0, "last_second")
+        last_second = bank(7, "last_second")
         for j in range(2, PACK):
             multiply(j, 1, last_second[:, half_cols(j - 2)])
 

@@ -79,7 +79,6 @@ def tile_attend_gheads_sm_kernel(tc, x1, x2, wT, y1, u1, w1, y2, u2, w2, ts, off
         for n in (1, 2):
             nc.vector.memset(windows[n][:, 0 : T // 2 - 1].bitcast(U32), 0)
             nc.vector.memset(windows[n][:, T // 2 - 1 : T].bitcast(U32), 0)
-        nc.vector.memset(windows[3][:].bitcast(U32), 0)
 
         neg_u2 = keep.tile([P, PACK], F32, name="neg_u")
         wu = [keep.tile([P, PACK - 2 * h], F32, name="wu%d" % h) for h in heads]
@@ -129,24 +128,25 @@ def tile_attend_gheads_sm_kernel(tc, x1, x2, wT, y1, u1, w1, y2, u2, w2, ts, off
 
         deal_x(0, 0, nc.scalar.copy)
         deal_x(0, 1, nc.vector.tensor_copy)
+        nc.vector.memset(windows[3][:].bitcast(U32), 0)
         for k in range(2):
             deal_x(1, k, nc.vector.tensor_copy)
         turn_x(0, 0)
         ts_row = sbuf([P, S], F32, "ts_row")
         nc.scalar.activation(ts_row[:], ts_win[:].indirect(offsets[:]), ACT.Copy)
-        turn_x(0, 1)
         ts_bank = bank(0, "ts_turned")
         for c in range(PACK):
             nc.tensor.transpose(ts_bank[:, block(c)], ts_row[:, block(c)], ident[:])
         ts_col = keep.tile([P, PACK], F32, name="ts_col")
         nc.scalar.copy(ts_col[:], ts_bank[:, 0:S:P])
         turn_x(1, 0)
-        turn_x(1, 1)
         spread_bank = bank(1, "ts_spread")
         for c in range(PACK):
             nc.tensor.transpose(spread_bank[:, block(c)], ts_col[:, c : c + 1].to_broadcast([P, P]), ident[:])
         ts_all = sbuf([P, S], F32, "ts_all")
         nc.scalar.copy(ts_all[:], spread_bank[:])
+        turn_x(0, 1)
+        turn_x(1, 1)
 
         w_d = sbuf([P, S, PACK], BF16, "w_d")
 
@@ -162,12 +162,12 @@ def tile_attend_gheads_sm_kernel(tc, x1, x2, wT, y1, u1, w1, y2, u2, w2, ts, off
         gather(0)
         gather(1)
         quantise_x_r(0)
+        factor = sbuf([P, PACK, S], F32, "factor")
+        for t in range(2):
+            nc.vector.tensor_scalar(factor[:, t, :], ts_all[:], wu[1][:, t : t + 1], None, ALU.mult)
         gather_halves(2)
         gather_halves(3)
-        factor = sbuf([P, PACK, S], F32, "factor")
         wu_late = last.tile([P, 2], F32, name="wu_late", align_bytes=ALIGN, offset=0)
-        for t in range(2):
-            nc.scalar.activation(factor[:, t, :], ts_all[:], ACT.Copy, scale=wu[1][:, t : t + 1])
         for t in range(2):
             nc.scalar.activation(wu_late[:, t : t + 1], u_col[1][:, t + 2 : t + 3], ACT.Copy, scale=w_col[1][:, t + 2 : t + 3])
         for t in range(2):

@@ -101,8 +101,9 @@ def tile_attend_gheads_sm_kernel(tc, x1, x2, wT, y1, u1, w1, y2, u2, w2, ts, off
         x_d = [[sbuf([P, HALF * PACK], BF16, "x_d%d%d" % (h, k)) for k in range(2)] for h in heads]
         x_r = [sbuf([P, 2 * HALF * PACK], BF16, "x_r%d" % u) for u in range(2)]
         qx_d = [codes("qx_d%d" % h, R) for h in heads]
-        qx_r = [codes("qx_r0", 2 * HALF),
-                (last.tile([P, 2 * HALF], U32, name="qx_r1_c", align_bytes=ALIGN, offset=4096), sbuf([P, 2 * HALF], U8, "qx_r1_s"))]
+        qx_r0 = codes("qx_r0", 2 * HALF)
+        qx_r1 = [codes("qx_r10", HALF),
+                 (last.tile([P, HALF], U32, name="qx_r11_c", align_bytes=ALIGN, offset=4096), sbuf([P, HALF], U8, "qx_r11_s"))]
         qg = [[None, None], [None, None]]
         qw = codes("qw", S)
 
@@ -123,8 +124,8 @@ def tile_attend_gheads_sm_kernel(tc, x1, x2, wT, y1, u1, w1, y2, u2, w2, ts, off
             nc.scalar.copy(x_r[u][:, h * HALF * PACK : (h + 1) * HALF * PACK].rearrange("s (e p t) -> s e p t", e=2, t=PACK),
                            acc[:].bitcast(BF16).rearrange("s (t p e) -> s e p t", t=PACK, e=2))
 
-        def quantise_x_r(u):
-            quantise(qx_r[u], slice(0, 2 * HALF), x_r[u][:], E4M3)
+        def quantise_x_r1(h):
+            quantise(qx_r1[h], half_cols(0), x_r[1][:, h * HALF * PACK : (h + 1) * HALF * PACK], E4M3)
 
         deal_x(0, 0, nc.scalar.copy)
         deal_x(0, 1, nc.vector.tensor_copy)
@@ -161,11 +162,12 @@ def tile_attend_gheads_sm_kernel(tc, x1, x2, wT, y1, u1, w1, y2, u2, w2, ts, off
         quantise_x_d(1)
         gather(0)
         gather(1)
-        quantise_x_r(0)
+        quantise(qx_r0, slice(0, 2 * HALF), x_r[0][:], E4M3)
         factor = sbuf([P, PACK, S], F32, "factor")
         for t in range(2):
-            nc.vector.tensor_scalar(factor[:, t, :], ts_all[:], wu[1][:, t : t + 1], None, ALU.mult)
+            nc.scalar.activation(factor[:, t, :], ts_all[:], ACT.Copy, scale=wu[1][:, t : t + 1])
         gather_halves(2)
+        quantise_x_r1(0)
         gather_halves(3)
         wu_late = last.tile([P, 2], F32, name="wu_late", align_bytes=ALIGN, offset=0)
         for t in range(2):
@@ -176,7 +178,7 @@ def tile_attend_gheads_sm_kernel(tc, x1, x2, wT, y1, u1, w1, y2, u2, w2, ts, off
         w_flat = w_d[:].rearrange("p i j -> p (i j)")
         for half in range(2):
             quantise(qw, half_cols(half), w_flat[:, half * HALF * PACK : (half + 1) * HALF * PACK], E4M3)
-        quantise_x_r(1)
+        quantise_x_r1(1)
 
         turned = sbuf([P, PACK, R], F32, "turned")
         work = [sbuf([P, PACK, S], F32, "work%d" % h) for h in heads]
@@ -213,16 +215,26 @@ def tile_attend_gheads_sm_kernel(tc, x1, x2, wT, y1, u1, w1, y2, u2, w2, ts, off
             qg[h][half] = codes("qg%d%d" % (h, half), HALF, tag)
             quantise(qg[h][half], half_cols(0), g[h][half][:], E5M2)
 
-        direct_pass(0, half_cols(0), bank(7, "a1_first"))
-        for t in range(PACK):
-            turned_pass(t)
-            if t == 0:
-                direct_pass(t, half_cols(1), bank(0, "a1_0"))
-            if t + 1 < PACK:
-                direct_pass(t + 1, slice(0, S), bank((t + 1) % 2, "a1_%d" % (t + 1)))
+        def maximum(t):
             negate_and_min(0, t, work[0][:, t, :], -1.0)
-        for t in range(PACK):
+
+        def exp_and_recip(t):
             expo(0, t)
+            recip(0, t, t + 1)
+
+        direct_pass(0, half_cols(0), bank(7, "a1_first"))
+        turned_pass(0)
+        direct_pass(0, half_cols(1), bank(0, "a1_0"))
+        for t in range(1, PACK):
+            direct_pass(t, slice(0, S), bank(t % 2, "a1_%d" % t))
+            if t < PACK - 1:
+                maximum(t - 1)
+            turned_pass(t)
+            if t > 1:
+                exp_and_recip(t - 2)
+        for t in range(2, PACK):
+            maximum(t)
+            exp_and_recip(t)
 
         back_banks = (2, 3, 0, 1)
         back = [bank(back_banks[t], "s1%d" % t) for t in range(PACK)]
@@ -242,12 +254,11 @@ def tile_attend_gheads_sm_kernel(tc, x1, x2, wT, y1, u1, w1, y2, u2, w2, ts, off
             turn_add(y_neg, t, range(PACK), t == 0, False)
 
         for t in range(PACK):
-            recip(0, t, t + 1)
-        for t in range(PACK):
             negate_and_min(1, t, back[t][:], neg_u2[:, t : t + 1])
             expo(1, t)
         for t in range(PACK):
-            nc.gpsimd.tensor_scalar(work[0][:, t, :], work[0][:, t, :], inv[0][:, t : t + 1], wu[0][:, t : t + 1], ALU.mult, ALU.mult)
+            engine = nc.gpsimd if t + 1 < PACK else nc.vector
+            engine.tensor_scalar(work[0][:, t, :], work[0][:, t, :], inv[0][:, t : t + 1], wu[0][:, t : t + 1], ALU.mult, ALU.mult)
             turn_add(work[0], t, (0, 1), False, t == PACK - 1)
         for t in range(PACK):
             turn_add(work[0], t, (2, 3), False, t == PACK - 1)
@@ -299,7 +310,8 @@ def tile_attend_gheads_sm_kernel(tc, x1, x2, wT, y1, u1, w1, y2, u2, w2, ts, off
 
         def multiply(j, half, acc):
             for h in heads:
-                mm(acc, qx_r[j // 2], h * HALF + j % 2 * P, qg[h][half], half_cols(0), E5M2, h == 0, h == 1)
+                lhs, lo = (qx_r0, h * HALF) if j < 2 else (qx_r1[h], 0)
+                mm(acc, lhs, lo + j % 2 * P, qg[h][half], half_cols(0), E5M2, h == 0, h == 1)
 
         def drain(name, acc, width, copy, tag=None):
             dw = sbuf([P, width], F32, name, tag)

@@ -27,11 +27,12 @@ FLOPS = 4 * 2 * 512 * 512 * 512
 
 def tile_attend_gheads_sm_kernel(tc, x1, x2, wT, y1, u1, w1, y2, u2, w2, ts, offs, out):
     nc = tc.nc
-    xs, ys, us, ws = (x1, x2), (y1, y2), (u1, u2), (w1, w2)
+    xs, us, ws = (x1, x2), (u1, u2), (w1, w2)
     heads = (0, 1)
     with ExitStack() as ctx:
         keep = ctx.enter_context(tc.tile_pool(name="keep", bufs=1))
         last = ctx.enter_context(tc.tile_pool(name="last", bufs=1))
+        held = ctx.enter_context(tc.tile_pool(name="held", bufs=1))
         psum = ctx.enter_context(tc.psum_pool(name="psum", bufs=1))
 
         def bank(b, name):
@@ -54,7 +55,8 @@ def tile_attend_gheads_sm_kernel(tc, x1, x2, wT, y1, u1, w1, y2, u2, w2, ts, off
         x_raw = [sbuf([P, PACK, R], F32, "x_raw%d" % h) for h in heads]
         w_plane = [sbuf([P, T], F32, "w_plane%d" % j) for j in range(PACK - 1)]
         w_plane.append(last.tile([P, T], F32, name="w_plane3", align_bytes=ALIGN, offset=0))
-        y_raw = [sbuf([P, PACK, S], F32, "y_raw%d" % h) for h in heads]
+        y_pair = [sbuf([P, 2, S], F32, "y_pair%d" % k) for k in range(2)]
+        y2_raw = sbuf([P, PACK, S], F32, "y2_raw")
         w_view = wT.rearrange("(p j) n -> j p n", j=PACK)
         ts_win = sbuf([P, T], F32, "ts_win")
         nc.gpsimd.memset(ts_win[:].bitcast(U32), 0)
@@ -69,8 +71,9 @@ def tile_attend_gheads_sm_kernel(tc, x1, x2, wT, y1, u1, w1, y2, u2, w2, ts, off
         for h in reversed(heads):
             nc.scalar.dma_start(u_col[h][:], us[h].rearrange("(p t) o -> p (t o)", t=PACK))
             nc.scalar.dma_start(w_col[h][:], ws[h].rearrange("(p t) o -> p (t o)", t=PACK))
-        for h in heads:
-            nc.sync.dma_start(y_raw[h][:], ys[h].rearrange("(p t) i -> p t i", t=PACK))
+        for k in range(2):
+            nc.sync.dma_start(y_pair[k][:], y1.rearrange("(p t) i -> p t i", t=PACK)[:, 2 * k : 2 * k + 2, :])
+        nc.sync.dma_start(y2_raw[:], y2.rearrange("(p t) i -> p t i", t=PACK))
 
         ident = keep.tile([P, P], F32, name="ident")
         make_identity(nc, ident[:])
@@ -102,8 +105,7 @@ def tile_attend_gheads_sm_kernel(tc, x1, x2, wT, y1, u1, w1, y2, u2, w2, ts, off
         x_r = [sbuf([P, 2 * HALF * PACK], BF16, "x_r%d" % u) for u in range(2)]
         qx_d = [codes("qx_d%d" % h, R) for h in heads]
         qx_r0 = codes("qx_r0", 2 * HALF)
-        qx_r1 = [codes("qx_r10", HALF),
-                 (last.tile([P, HALF], U32, name="qx_r11_c", align_bytes=ALIGN, offset=4096), sbuf([P, HALF], U8, "qx_r11_s"))]
+        qx_r1 = [codes("qx_r1%d" % h, HALF) for h in heads]
         qg = [[None, None], [None, None]]
         qw = codes("qw", S)
 
@@ -167,7 +169,8 @@ def tile_attend_gheads_sm_kernel(tc, x1, x2, wT, y1, u1, w1, y2, u2, w2, ts, off
         for t in range(2):
             nc.scalar.activation(factor[:, t, :], ts_all[:], ACT.Copy, scale=wu[1][:, t : t + 1])
         gather_halves(2)
-        quantise_x_r1(0)
+        for h in heads:
+            quantise_x_r1(h)
         gather_halves(3)
         wu_late = last.tile([P, 2], F32, name="wu_late", align_bytes=ALIGN, offset=0)
         for t in range(2):
@@ -178,17 +181,16 @@ def tile_attend_gheads_sm_kernel(tc, x1, x2, wT, y1, u1, w1, y2, u2, w2, ts, off
         w_flat = w_d[:].rearrange("p i j -> p (i j)")
         for half in range(2):
             quantise(qw, half_cols(half), w_flat[:, half * HALF * PACK : (half + 1) * HALF * PACK], E4M3)
-        quantise_x_r1(1)
 
         turned = sbuf([P, PACK, R], F32, "turned")
         work = [sbuf([P, PACK, S], F32, "work%d" % h) for h in heads]
         neg_m = [keep.tile([P, PACK], F32, name="neg_m%d" % h) for h in heads]
         total = [keep.tile([P, PACK], F32, name="total%d" % h) for h in heads]
-        inv = [sbuf([P, PACK], F32, "inv0"), None]
+        inv = [held.tile([P, PACK], F32, name="inv0", offset=0), sbuf([P, PACK], F32, "inv1")]
         g = [[sbuf([P, HALF * PACK], BF16, "g0%d" % half) for half in range(2)], [sbuf([P, HALF * PACK], BF16, "g10"), None]]
 
         def turned_pass(c):
-            acc = bank(2 + c % 2, "aT1%d" % c)
+            acc = bank((4, 5, 2, 3)[c], "aT1%d" % c)
             mm(acc[:], qw, c * P, qx_d[1], slice(0, R), E4M3, True, True)
             nc.scalar.activation(turned[:, c, :], acc[:], ACT.Copy, scale=ts_col[:, c : c + 1])
 
@@ -201,14 +203,16 @@ def tile_attend_gheads_sm_kernel(tc, x1, x2, wT, y1, u1, w1, y2, u2, w2, ts, off
             nc.vector.tensor_scalar(work[h][:, t, :], src, scalar, None, ALU.mult, ALU.min, accum_out=neg_m[h][:, t : t + 1])
 
         def expo(h, t):
-            nc.scalar.activation(work[h][:, t, :], work[h][:, t, :], ACT.Exp, bias=neg_m[h][:, t : t + 1], scale=-1.0,
+            nc.scalar.activation(work[h][:, t, :], work[h][:, t, :], ACT.Exp, bias=neg_m[h][:, t : t + 1], scale=(1.0, -1.0)[h],
                                  accum_out=total[h][:, t : t + 1])
 
         def recip(h, lo, hi):
             nc.vector.reciprocal(inv[h][:, lo:hi], total[h][:, lo:hi])
 
+        h2 = held.tile([P, PACK, S], F32, name="h2", offset=0)
+
         def diff(t, cols):
-            nc.vector.scalar_tensor_tensor(work[1][:, t, cols], work[1][:, t, cols], inv[1][:, t : t + 1], y_raw[1][:, t, cols],
+            nc.vector.scalar_tensor_tensor(h2[:, t, cols], work[1][:, t, cols], inv[1][:, t : t + 1], y2_raw[:, t, cols],
                                            ALU.mult, ALU.subtract)
 
         def quantise_g(h, half, tag=None):
@@ -216,17 +220,17 @@ def tile_attend_gheads_sm_kernel(tc, x1, x2, wT, y1, u1, w1, y2, u2, w2, ts, off
             quantise(qg[h][half], half_cols(0), g[h][half][:], E5M2)
 
         def maximum(t):
-            negate_and_min(0, t, work[0][:, t, :], -1.0)
+            nc.vector.tensor_reduce(neg_m[0][:, t : t + 1], work[0][:, t, :], mybir.AxisListType.X, ALU.max, negate=True)
 
         def exp_and_recip(t):
             expo(0, t)
             recip(0, t, t + 1)
 
-        direct_pass(0, half_cols(0), bank(7, "a1_first"))
+        direct_pass(0, half_cols(0), bank(6, "a1_first"))
         turned_pass(0)
         direct_pass(0, half_cols(1), bank(0, "a1_0"))
         for t in range(1, PACK):
-            direct_pass(t, slice(0, S), bank(t % 2, "a1_%d" % t))
+            direct_pass(t, slice(0, S), bank((7, 1, 0)[t - 1], "a1_%d" % t))
             if t < PACK - 1:
                 maximum(t - 1)
             turned_pass(t)
@@ -236,13 +240,13 @@ def tile_attend_gheads_sm_kernel(tc, x1, x2, wT, y1, u1, w1, y2, u2, w2, ts, off
             maximum(t)
             exp_and_recip(t)
 
-        back_banks = (2, 3, 0, 1)
+        back_banks = (2, 3, 1, 0)
         back = [bank(back_banks[t], "s1%d" % t) for t in range(PACK)]
         for t in range(PACK):
             for c in range(PACK):
                 nc.tensor.transpose(back[t][:, block(c)], turned[:, c, block(t)], ident[:])
 
-        y_neg = sbuf([P, PACK, S], F32, "y_neg", "x_r1")
+        y_neg = sbuf([P, PACK, S], F32, "y_neg", "w_d")
         sums = [bank(PACK + c, "hT%d" % c) for c in range(PACK)]
 
         def turn_add(src, t, blocks, start, stop):
@@ -250,7 +254,7 @@ def tile_attend_gheads_sm_kernel(tc, x1, x2, wT, y1, u1, w1, y2, u2, w2, ts, off
                 nc.tensor.matmul(sums[c][:, block(t)], src[:, t, block(c)], ident[:], start=start, stop=stop, is_transpose=True)
 
         for t in range(PACK):
-            nc.gpsimd.tensor_scalar(y_neg[:, t, :], y_raw[0][:, t, :], neg_wu1[:, t : t + 1], 0.0, ALU.mult, ALU.add)
+            nc.gpsimd.tensor_scalar(y_neg[:, t, :], y_pair[t // 2][:, t % 2, :], neg_wu1[:, t : t + 1], 0.0, ALU.mult, ALU.add)
             turn_add(y_neg, t, range(PACK), t == 0, False)
 
         for t in range(PACK):
@@ -289,12 +293,11 @@ def tile_attend_gheads_sm_kernel(tc, x1, x2, wT, y1, u1, w1, y2, u2, w2, ts, off
         def weave_g2(half):
             nc.vector.tensor_tensor(
                 g[1][half][:].rearrange("p (c i t) -> p c t i", i=2, t=PACK),
-                work[1][:, :, half_cols(half)].rearrange("p t (c i) -> p c t i", i=2),
+                h2[:, :, half_cols(half)].rearrange("p t (c i) -> p c t i", i=2),
                 factor[:, :, half_cols(half)].rearrange("p t (c i) -> p c t i", i=2),
                 ALU.mult,
             )
 
-        inv[1] = sbuf([P, PACK], F32, "inv1", "inv0")
         recip(1, 0, 2)
         diff(0, slice(0, S))
         recip(1, 2, PACK)
@@ -309,9 +312,10 @@ def tile_attend_gheads_sm_kernel(tc, x1, x2, wT, y1, u1, w1, y2, u2, w2, ts, off
         out_view = out.rearrange("(p j) n -> j p n", j=PACK)
 
         def multiply(j, half, acc):
-            for h in heads:
+            order = heads if j < 2 else heads[::-1]
+            for h in order:
                 lhs, lo = (qx_r0, h * HALF) if j < 2 else (qx_r1[h], 0)
-                mm(acc, lhs, lo + j % 2 * P, qg[h][half], half_cols(0), E5M2, h == 0, h == 1)
+                mm(acc, lhs, lo + j % 2 * P, qg[h][half], half_cols(0), E5M2, h == order[0], h == order[1])
 
         def drain(name, acc, width, copy, tag=None):
             dw = sbuf([P, width], F32, name, tag)

@@ -179,8 +179,10 @@ def tile_attend_gheads_sm_kernel(tc, x1, x2, wT, y1, u1, w1, y2, u2, w2, ts, off
             nc.scalar.activation(factor[:, t + 2, :], ts_all[:], ACT.Copy, scale=wu_late[:, t : t + 1])
 
         w_flat = w_d[:].rearrange("p i j -> p (i j)")
-        for half in range(2):
-            quantise(qw, half_cols(half), w_flat[:, half * HALF * PACK : (half + 1) * HALF * PACK], E4M3)
+        y_first = sbuf([P, S], F32, "y_first")
+        quantise(qw, half_cols(0), w_flat[:, 0 : HALF * PACK], E4M3)
+        nc.vector.tensor_scalar(y_first[:], y_pair[0][:, 0, :], neg_wu1[:, 0:1], None, ALU.mult)
+        quantise(qw, half_cols(1), w_flat[:, HALF * PACK : S * PACK], E4M3)
 
         turned = sbuf([P, PACK, R], F32, "turned")
         work = [sbuf([P, PACK, S], F32, "work%d" % h) for h in heads]
@@ -226,8 +228,8 @@ def tile_attend_gheads_sm_kernel(tc, x1, x2, wT, y1, u1, w1, y2, u2, w2, ts, off
             expo(0, t)
             recip(0, t, t + 1)
 
-        direct_pass(0, half_cols(0), bank(6, "a1_first"))
         turned_pass(0)
+        direct_pass(0, half_cols(0), bank(6, "a1_first"))
         direct_pass(0, half_cols(1), bank(0, "a1_0"))
         for t in range(1, PACK):
             direct_pass(t, slice(0, S), bank((7, 1, 0)[t - 1], "a1_%d" % t))
@@ -246,16 +248,17 @@ def tile_attend_gheads_sm_kernel(tc, x1, x2, wT, y1, u1, w1, y2, u2, w2, ts, off
             for c in range(PACK):
                 nc.tensor.transpose(back[t][:, block(c)], turned[:, c, block(t)], ident[:])
 
-        y_neg = sbuf([P, PACK, S], F32, "y_neg", "w_d")
+        y_neg = sbuf([P, PACK - 1, S], F32, "y_neg", "w_d")
         sums = [bank(PACK + c, "hT%d" % c) for c in range(PACK)]
 
         def turn_add(src, t, blocks, start, stop):
             for c in blocks:
-                nc.tensor.matmul(sums[c][:, block(t)], src[:, t, block(c)], ident[:], start=start, stop=stop, is_transpose=True)
+                nc.tensor.matmul(sums[c][:, block(t)], src[:, block(c)], ident[:], start=start, stop=stop, is_transpose=True)
 
-        for t in range(PACK):
-            nc.gpsimd.tensor_scalar(y_neg[:, t, :], y_pair[t // 2][:, t % 2, :], neg_wu1[:, t : t + 1], 0.0, ALU.mult, ALU.add)
-            turn_add(y_neg, t, range(PACK), t == 0, False)
+        turn_add(y_first[:], 0, range(PACK), True, False)
+        for t in range(1, PACK):
+            nc.gpsimd.tensor_scalar(y_neg[:, t - 1, :], y_pair[t // 2][:, t % 2, :], neg_wu1[:, t : t + 1], 0.0, ALU.mult, ALU.add)
+            turn_add(y_neg[:, t - 1, :], t, range(PACK), False, False)
 
         for t in range(PACK):
             negate_and_min(1, t, back[t][:], neg_u2[:, t : t + 1])
@@ -263,9 +266,9 @@ def tile_attend_gheads_sm_kernel(tc, x1, x2, wT, y1, u1, w1, y2, u2, w2, ts, off
         for t in range(PACK):
             engine = nc.gpsimd if t + 1 < PACK else nc.vector
             engine.tensor_scalar(work[0][:, t, :], work[0][:, t, :], inv[0][:, t : t + 1], wu[0][:, t : t + 1], ALU.mult, ALU.mult)
-            turn_add(work[0], t, (0, 1), False, t == PACK - 1)
+            turn_add(work[0][:, t, :], t, (0, 1), False, t == PACK - 1)
         for t in range(PACK):
-            turn_add(work[0], t, (2, 3), False, t == PACK - 1)
+            turn_add(work[0][:, t, :], t, (2, 3), False, t == PACK - 1)
 
         def scale_g1(half):
             blocks = []

@@ -180,7 +180,8 @@ def tile_attend_gheads_sm_kernel(tc, x1, x2, wT, y1, u1, w1, y2, u2, w2, ts, off
 
         w_flat = w_d[:].rearrange("p i j -> p (i j)")
         y_first = sbuf([P, S], F32, "y_first")
-        quantise(qw, half_cols(0), w_flat[:, 0 : HALF * PACK], E4M3)
+        for c in range(2):
+            quantise(qw, block(c), w_flat[:, c * P * PACK : (c + 1) * P * PACK], E4M3)
         nc.vector.tensor_scalar(y_first[:], y_pair[0][:, 0, :], neg_wu1[:, 0:1], None, ALU.mult)
         quantise(qw, half_cols(1), w_flat[:, HALF * PACK : S * PACK], E4M3)
 
@@ -192,7 +193,7 @@ def tile_attend_gheads_sm_kernel(tc, x1, x2, wT, y1, u1, w1, y2, u2, w2, ts, off
         g = [[sbuf([P, HALF * PACK], BF16, "g0%d" % half) for half in range(2)], [sbuf([P, HALF * PACK], BF16, "g10"), None]]
 
         def turned_pass(c):
-            acc = bank((4, 5, 2, 3)[c], "aT1%d" % c)
+            acc = bank((4, 6, 2, 3)[c], "aT1%d" % c)
             mm(acc[:], qw, c * P, qx_d[1], slice(0, R), E4M3, True, True)
             nc.scalar.activation(turned[:, c, :], acc[:], ACT.Copy, scale=ts_col[:, c : c + 1])
 
@@ -232,7 +233,7 @@ def tile_attend_gheads_sm_kernel(tc, x1, x2, wT, y1, u1, w1, y2, u2, w2, ts, off
         direct_pass(0, half_cols(0), bank(6, "a1_first"))
         direct_pass(0, half_cols(1), bank(0, "a1_0"))
         for t in range(1, PACK):
-            direct_pass(t, slice(0, S), bank((7, 1, 0)[t - 1], "a1_%d" % t))
+            direct_pass(t, slice(0, S), bank((5, 7, 0)[t - 1], "a1_%d" % t))
             if t < PACK - 1:
                 maximum(t - 1)
             turned_pass(t)

@@ -104,8 +104,7 @@ def tile_attend_gheads_sm_kernel(tc, x1, x2, wT, y1, u1, w1, y2, u2, w2, ts, off
         x_d = [[sbuf([P, HALF * PACK], BF16, "x_d%d%d" % (h, k)) for k in range(2)] for h in heads]
         x_r = [sbuf([P, 2 * HALF * PACK], BF16, "x_r%d" % u) for u in range(2)]
         qx_d = [codes("qx_d%d" % h, R) for h in heads]
-        qx_r0 = codes("qx_r0", 2 * HALF)
-        qx_r1 = [codes("qx_r1%d" % h, HALF) for h in heads]
+        qx_r = [codes("qx_r%d" % u, 2 * HALF) for u in range(2)]
         qg = [[None, None], [None, None]]
         qw = codes("qw", S)
 
@@ -126,8 +125,8 @@ def tile_attend_gheads_sm_kernel(tc, x1, x2, wT, y1, u1, w1, y2, u2, w2, ts, off
             nc.scalar.copy(x_r[u][:, h * HALF * PACK : (h + 1) * HALF * PACK].rearrange("s (e p t) -> s e p t", e=2, t=PACK),
                            acc[:].bitcast(BF16).rearrange("s (t p e) -> s e p t", t=PACK, e=2))
 
-        def quantise_x_r1(h):
-            quantise(qx_r1[h], half_cols(0), x_r[1][:, h * HALF * PACK : (h + 1) * HALF * PACK], E4M3)
+        def quantise_x_r(u):
+            quantise(qx_r[u], slice(0, 2 * HALF), x_r[u][:], E4M3)
 
         deal_x(0, 0, nc.scalar.copy)
         deal_x(0, 1, nc.vector.tensor_copy)
@@ -164,13 +163,12 @@ def tile_attend_gheads_sm_kernel(tc, x1, x2, wT, y1, u1, w1, y2, u2, w2, ts, off
         quantise_x_d(1)
         gather(0)
         gather(1)
-        quantise(qx_r0, slice(0, 2 * HALF), x_r[0][:], E4M3)
+        quantise_x_r(0)
         factor = sbuf([P, PACK, S], F32, "factor")
         for t in range(2):
             nc.scalar.activation(factor[:, t, :], ts_all[:], ACT.Copy, scale=wu[1][:, t : t + 1])
         gather_halves(2)
-        for h in heads:
-            quantise_x_r1(h)
+        quantise_x_r(1)
         gather_halves(3)
         wu_late = last.tile([P, 2], F32, name="wu_late", align_bytes=ALIGN, offset=0)
         for t in range(2):
@@ -179,10 +177,8 @@ def tile_attend_gheads_sm_kernel(tc, x1, x2, wT, y1, u1, w1, y2, u2, w2, ts, off
             nc.scalar.activation(factor[:, t + 2, :], ts_all[:], ACT.Copy, scale=wu_late[:, t : t + 1])
 
         w_flat = w_d[:].rearrange("p i j -> p (i j)")
-        y_first = sbuf([P, S], F32, "y_first")
         for c in range(2):
             quantise(qw, block(c), w_flat[:, c * P * PACK : (c + 1) * P * PACK], E4M3)
-        nc.vector.tensor_scalar(y_first[:], y_pair[0][:, 0, :], neg_wu1[:, 0:1], None, ALU.mult)
         quantise(qw, half_cols(1), w_flat[:, HALF * PACK : S * PACK], E4M3)
 
         turned = sbuf([P, PACK, R], F32, "turned")
@@ -249,17 +245,16 @@ def tile_attend_gheads_sm_kernel(tc, x1, x2, wT, y1, u1, w1, y2, u2, w2, ts, off
             for c in range(PACK):
                 nc.tensor.transpose(back[t][:, block(c)], turned[:, c, block(t)], ident[:])
 
-        y_neg = sbuf([P, PACK - 1, S], F32, "y_neg", "w_d")
+        y_neg = sbuf([P, PACK, S], F32, "y_neg", "w_d")
         sums = [bank(PACK + c, "hT%d" % c) for c in range(PACK)]
 
         def turn_add(src, t, blocks, start, stop):
             for c in blocks:
                 nc.tensor.matmul(sums[c][:, block(t)], src[:, block(c)], ident[:], start=start, stop=stop, is_transpose=True)
 
-        turn_add(y_first[:], 0, range(PACK), True, False)
-        for t in range(1, PACK):
-            nc.gpsimd.tensor_scalar(y_neg[:, t - 1, :], y_pair[t // 2][:, t % 2, :], neg_wu1[:, t : t + 1], 0.0, ALU.mult, ALU.add)
-            turn_add(y_neg[:, t - 1, :], t, range(PACK), False, False)
+        for t in range(PACK):
+            nc.gpsimd.tensor_scalar(y_neg[:, t, :], y_pair[t // 2][:, t % 2, :], neg_wu1[:, t : t + 1], 0.0, ALU.mult, ALU.add)
+            turn_add(y_neg[:, t, :], t, range(PACK), t == 0, False)
 
         for t in range(PACK):
             negate_and_min(1, t, back[t][:], neg_u2[:, t : t + 1])
@@ -318,8 +313,7 @@ def tile_attend_gheads_sm_kernel(tc, x1, x2, wT, y1, u1, w1, y2, u2, w2, ts, off
         def multiply(j, half, acc):
             order = heads if j < 2 else heads[::-1]
             for h in order:
-                lhs, lo = (qx_r0, h * HALF) if j < 2 else (qx_r1[h], 0)
-                mm(acc, lhs, lo + j % 2 * P, qg[h][half], half_cols(0), E5M2, h == order[0], h == order[1])
+                mm(acc, qx_r[j // 2], h * HALF + j % 2 * P, qg[h][half], half_cols(0), E5M2, h == order[0], h == order[1])
 
         def drain(name, acc, width, copy, tag=None):
             dw = sbuf([P, width], F32, name, tag)

from contextlib import ExitStack

import concourse.mybir as mybir
from concourse.masks import make_identity

F32 = mybir.dt.float32
BF16 = mybir.dt.bfloat16
U32 = mybir.dt.uint32
U16 = mybir.dt.uint16
U8 = mybir.dt.uint8
E4M3 = mybir.dt.float8_e4m3fn_x4
E5M2 = mybir.dt.float8_e5m2_x4
ALU = mybir.AluOpType
ACT = mybir.ActivationFunctionType

P = 128
PACK = 4
R = 512
S = 512
T = 2048
HALF = 256
BAND = 16
BANK = 512
ALIGN = 64
FLOPS = 4 * 2 * 512 * 512 * 512


def tile_attend_gheads_sm_kernel(tc, x1, x2, wT, y1, u1, w1, y2, u2, w2, ts, offs, out):
    nc = tc.nc
    xs, us, ws = (x1, x2), (u1, u2), (w1, w2)
    heads = (0, 1)
    with ExitStack() as ctx:
        keep = ctx.enter_context(tc.tile_pool(name="keep", bufs=1))
        last = ctx.enter_context(tc.tile_pool(name="last", bufs=1))
        held = ctx.enter_context(tc.tile_pool(name="held", bufs=1))
        psum = ctx.enter_context(tc.psum_pool(name="psum", bufs=1))

        def bank(b, name):
            return psum.tile([P, BANK], F32, name=name, tag="bank%d" % b)

        def sbuf(shape, dtype, name, tag=None):
            return keep.tile(shape, dtype, name=name, tag=tag or name, align_bytes=ALIGN)

        def half_cols(half):
            return slice(half * HALF, (half + 1) * HALF)

        def block(c):
            return slice(c * P, (c + 1) * P)

        offsets = keep.tile([P, S // BAND], U16, name="offsets")

        def entries(half):
            return offsets[:, half * HALF // BAND : (half + 1) * HALF // BAND]

        x_raw = [sbuf([P, PACK, R], F32, "x_raw%d" % h) for h in heads]
        w_plane = [sbuf([P, T], F32, "w_plane%d" % j) for j in range(PACK - 1)]
        w_plane.append(last.tile([P, T], F32, name="w_plane3", align_bytes=ALIGN, offset=0))
        y_pair = [sbuf([P, 2, S], F32, "y_pair%d" % k) for k in range(2)]
        y2_raw = sbuf([P, PACK, S], F32, "y2_raw")
        w_view = wT.rearrange("(p j) n -> j p n", j=PACK)
        ts_win = sbuf([P, T], F32, "ts_win")
        nc.gpsimd.memset(ts_win[:].bitcast(U32), 0)
        nc.sync.dma_start(x_raw[0][:], xs[0].rearrange("(p j) r -> p j r", j=PACK))
        nc.sync.dma_start(offsets[:], offs)
        nc.sync.dma_start(ts_win[0:1, :], ts[0:1, :])
        nc.sync.dma_start(x_raw[1][:], xs[1].rearrange("(p j) r -> p j r", j=PACK))
        for j in range(PACK):
            nc.sync.dma_start(w_plane[j][:], w_view[j])
        u_col = [keep.tile([P, PACK], F32, name="u_col%d" % h) for h in heads]
        w_col = [keep.tile([P, PACK], F32, name="w_col%d" % h) for h in heads]
        for h in reversed(heads):
            nc.scalar.dma_start(u_col[h][:], us[h].rearrange("(p t) o -> p (t o)", t=PACK))
            nc.scalar.dma_start(w_col[h][:], ws[h].rearrange("(p t) o -> p (t o)", t=PACK))
        for k in range(2):
            nc.sync.dma_start(y_pair[k][:], y1.rearrange("(p t) i -> p t i", t=PACK)[:, 2 * k : 2 * k + 2, :])
        nc.sync.dma_start(y2_raw[:], y2.rearrange("(p t) i -> p t i", t=PACK))

        ident = keep.tile([P, P], F32, name="ident")
        make_identity(nc, ident[:])
        windows = [sbuf([P, T], F32, "window%d" % n) for n in range(PACK)]
        nc.gpsimd.memset(windows[0][:].bitcast(U32), 0)
        for n in (1, 2):
            nc.vector.memset(windows[n][:, 0 : T // 2 - 1].bitcast(U32), 0)
            nc.vector.memset(windows[n][:, T // 2 - 1 : T].bitcast(U32), 0)

        neg_u2 = keep.tile([P, PACK], F32, name="neg_u")
        wu = [keep.tile([P, PACK - 2 * h], F32, name="wu%d" % h) for h in heads]
        nc.gpsimd.tensor_scalar(neg_u2[:], u_col[1][:], -1.0, 0.0, ALU.mult, ALU.add)
        for h in reversed(heads):
            nc.gpsimd.tensor_tensor(wu[h][:], u_col[h][:, 0 : PACK - 2 * h], w_col[h][:, 0 : PACK - 2 * h], ALU.mult)
        neg_wu1 = keep.tile([P, PACK], F32, name="neg_wu")
        nc.gpsimd.tensor_scalar(neg_wu1[:], wu[0][:], -1.0, 0.0, ALU.mult, ALU.add)

        def codes(name, width, tag=None):
            return sbuf([P, width], U32, name + "_c", tag), sbuf([P, width], U8, name + "_s")

        def quantise(q, cols, src, fmt):
            nc.vector.quantize_mx(out=q[0][:, cols].bitcast(fmt), scales=q[1][:, cols], in_=src)

        def mm(acc, lhs, lo, rhs, cols, rhs_fmt, start, stop):
            nc.tensor.matmul_mx(out=acc, lhsT=lhs[0][:, lo : lo + P].bitcast(E4M3), lhsT_scale=lhs[1][:, lo : lo + P],
                                rhs=rhs[0][:, cols].bitcast(rhs_fmt), rhs_scale=rhs[1][:, cols], start=start, stop=stop)

        x_d = [[sbuf([P, HALF * PACK], BF16, "x_d%d%d" % (h, k)) for k in range(2)] for h in heads]
        x_r = [sbuf([P, 2 * HALF * PACK], BF16, "x_r%d" % u) for u in range(2)]
        qx_d = [codes("qx_d%d" % h, R) for h in heads]
        qx_r = [codes("qx_r%d" % u, 2 * HALF) for u in range(2)]
        qg = [[None, None], [None, None]]
        qw = codes("qw", S)

        def deal_x(h, k, copy):
            copy(x_d[h][k][:].rearrange("p (t s j) -> p s t j", t=2, j=PACK),
                 x_raw[h][:].rearrange("p j (s t) -> p s t j", t=PACK)[:, :, 2 * k : 2 * k + 2, :])

        def quantise_x_d(h):
            for k in range(2):
                quantise(qx_d[h], half_cols(k), x_d[h][k][:], E4M3)

        def turn_x(h, u):
            acc = bank(2 + 2 * h + u, "xw%d%d" % (h, u))
            for t in range(PACK):
                pairs = x_d[h][t // 2][:].bitcast(F32)
                lo = 2 * P * (t % 2)
                nc.tensor.transpose(acc[:, block(t)], pairs[:, lo + u : lo + 2 * P : 2], ident[:])
            nc.scalar.copy(x_r[u][:, h * HALF * PACK : (h + 1) * HALF * PACK].rearrange("s (e p t) -> s e p t", e=2, t=PACK),
                           acc[:].bitcast(BF16).rearrange("s (t p e) -> s e p t", t=PACK, e=2))

        def quantise_x_r(u):
            quantise(qx_r[u], slice(0, 2 * HALF), x_r[u][:], E4M3)

        deal_x(0, 0, nc.scalar.copy)
        deal_x(0, 1, nc.vector.tensor_copy)
        nc.vector.memset(windows[3][:].bitcast(U32), 0)
        for k in range(2):
            deal_x(1, k, nc.vector.tensor_copy)
        turn_x(0, 0)
        ts_row = sbuf([P, S], F32, "ts_row")
        nc.scalar.activation(ts_row[:], ts_win[:].indirect(offsets[:]), ACT.Copy)
        ts_bank = bank(0, "ts_turned")
        for c in range(PACK):
            nc.tensor.transpose(ts_bank[:, block(c)], ts_row[:, block(c)], ident[:])
        ts_col = keep.tile([P, PACK], F32, name="ts_col")
        nc.scalar.copy(ts_col[:], ts_bank[:, 0:S:P])
        turn_x(1, 0)
        spread_bank = bank(1, "ts_spread")
        for c in range(PACK):
            nc.tensor.transpose(spread_bank[:, block(c)], ts_col[:, c : c + 1].to_broadcast([P, P]), ident[:])
        ts_all = sbuf([P, S], F32, "ts_all")
        nc.scalar.copy(ts_all[:], spread_bank[:])
        turn_x(0, 1)
        turn_x(1, 1)

        w_d = sbuf([P, S, PACK], BF16, "w_d")

        def gather(j):
            nc.vector.tensor_copy(w_d[:, :, j], w_plane[j][:].indirect(offsets[:]))

        def gather_halves(j):
            nc.vector.tensor_copy(w_d[:, half_cols(0), j], w_plane[j][:].indirect(entries(0)))
            nc.scalar.activation(w_d[:, half_cols(1), j], w_plane[j][:].indirect(entries(1)), ACT.Copy)

        quantise_x_d(0)
        quantise_x_d(1)
        gather(0)
        gather(1)
        quantise_x_r(0)
        factor = sbuf([P, PACK, S], F32, "factor")
        for t in range(2):
            nc.scalar.activation(factor[:, t, :], ts_all[:], ACT.Copy, scale=wu[1][:, t : t + 1])
        gather_halves(2)
        quantise_x_r(1)
        gather_halves(3)
        wu_late = last.tile([P, 2], F32, name="wu_late", align_bytes=ALIGN, offset=0)
        for t in range(2):
            nc.scalar.activation(wu_late[:, t : t + 1], u_col[1][:, t + 2 : t + 3], ACT.Copy, scale=w_col[1][:, t + 2 : t + 3])
        for t in range(2):
            nc.scalar.activation(factor[:, t + 2, :], ts_all[:], ACT.Copy, scale=wu_late[:, t : t + 1])

        w_flat = w_d[:].rearrange("p i j -> p (i j)")
        for c in range(2):
            quantise(qw, block(c), w_flat[:, c * P * PACK : (c + 1) * P * PACK], E4M3)
        quantise(qw, half_cols(1), w_flat[:, HALF * PACK : S * PACK], E4M3)

        turned = sbuf([P, PACK, R], F32, "turned")
        work = [sbuf([P, PACK, S], F32, "work%d" % h) for h in heads]
        neg_m = [keep.tile([P, PACK], F32, name="neg_m%d" % h) for h in heads]
        total = [keep.tile([P, PACK], F32, name="total%d" % h) for h in heads]
        inv = [held.tile([P, PACK], F32, name="inv0", offset=0), sbuf([P, PACK], F32, "inv1")]
        g = [[sbuf([P, HALF * PACK], BF16, "g0%d" % half) for half in range(2)], [sbuf([P, HALF * PACK], BF16, "g10"), None]]

        def turned_pass(c):
            acc = bank((4, 6, 2, 3)[c], "aT1%d" % c)
            mm(acc[:], qw, c * P, qx_d[1], slice(0, R), E4M3, True, True)
            nc.scalar.activation(turned[:, c, :], acc[:], ACT.Copy, scale=ts_col[:, c : c + 1])

        def direct_pass(t, cols, acc):
            mm(acc[:, cols], qx_d[0], t * P, qw, cols, E4M3, True, True)
            nc.vector.scalar_tensor_tensor(work[0][:, t, cols], acc[:, cols], u_col[0][:, t : t + 1],
                                           ts_all[:, cols], ALU.mult, ALU.mult)

        def negate_and_min(h, t, src, scalar):
            nc.vector.tensor_scalar(work[h][:, t, :], src, scalar, None, ALU.mult, ALU.min, accum_out=neg_m[h][:, t : t + 1])

        def expo(h, t):
            nc.scalar.activation(work[h][:, t, :], work[h][:, t, :], ACT.Exp, bias=neg_m[h][:, t : t + 1], scale=(1.0, -1.0)[h],
                                 accum_out=total[h][:, t : t + 1])

        def recip(h, lo, hi):
            nc.vector.reciprocal(inv[h][:, lo:hi], total[h][:, lo:hi])

        h2 = held.tile([P, PACK, S], F32, name="h2", offset=0)

        def diff(t, cols):
            nc.vector.scalar_tensor_tensor(h2[:, t, cols], work[1][:, t, cols], inv[1][:, t : t + 1], y2_raw[:, t, cols],
                                           ALU.mult, ALU.subtract)

        def quantise_g(h, half, tag=None):
            qg[h][half] = codes("qg%d%d" % (h, half), HALF, tag)
            quantise(qg[h][half], half_cols(0), g[h][half][:], E5M2)

        def maximum(t):
            nc.vector.tensor_reduce(neg_m[0][:, t : t + 1], work[0][:, t, :], mybir.AxisListType.X, ALU.max, negate=True)

        def exp_and_recip(t):
            expo(0, t)
            recip(0, t, t + 1)

        turned_pass(0)
        direct_pass(0, half_cols(0), bank(6, "a1_first"))
        direct_pass(0, half_cols(1), bank(0, "a1_0"))
        for t in range(1, PACK):
            direct_pass(t, slice(0, S), bank((5, 7, 0)[t - 1], "a1_%d" % t))
            if t < PACK - 1:
                maximum(t - 1)
            turned_pass(t)
            if t > 1:
                exp_and_recip(t - 2)
        for t in range(2, PACK):
            maximum(t)
            exp_and_recip(t)

        back_banks = (2, 3, 1, 0)
        back = [bank(back_banks[t], "s1%d" % t) for t in range(PACK)]
        for t in range(PACK):
            for c in range(PACK):
                nc.tensor.transpose(back[t][:, block(c)], turned[:, c, block(t)], ident[:])

        y_neg = sbuf([P, PACK, S], F32, "y_neg", "w_d")
        sums = [bank(PACK + c, "hT%d" % c) for c in range(PACK)]

        def turn_add(src, t, blocks, start, stop):
            for c in blocks:
                nc.tensor.matmul(sums[c][:, block(t)], src[:, block(c)], ident[:], start=start, stop=stop, is_transpose=True)

        for t in range(PACK):
            nc.gpsimd.tensor_scalar(y_neg[:, t, :], y_pair[t // 2][:, t % 2, :], neg_wu1[:, t : t + 1], 0.0, ALU.mult, ALU.add)
            turn_add(y_neg[:, t, :], t, range(PACK), t == 0, False)

        for t in range(PACK):
            negate_and_min(1, t, back[t][:], neg_u2[:, t : t + 1])
            expo(1, t)
        for t in range(PACK):
            engine = nc.gpsimd if t + 1 < PACK else nc.vector
            engine.tensor_scalar(work[0][:, t, :], work[0][:, t, :], inv[0][:, t : t + 1], wu[0][:, t : t + 1], ALU.mult, ALU.mult)
            turn_add(work[0][:, t, :], t, (0, 1), False, t == PACK - 1)
        for t in range(PACK):
            turn_add(work[0][:, t, :], t, (2, 3), False, t == PACK - 1)

        def scale_g1(half):
            blocks = []
            for k in range(2):
                c = 2 * half + k
                blocks.append(sbuf([P, R], BF16, "g_t%d" % c, "g_t%d" % (c % 3)))
                nc.scalar.activation(blocks[k][:].rearrange("i (u s e) -> i u s e", u=2, e=2),
                                     sums[c][:].rearrange("i (u e s) -> i u s e", u=2, e=2), ACT.Copy, scale=ts_col[:, c : c + 1])
            return blocks

        def turn_back_g1(half, blocks):
            acc = bank(2 + half, "gw%d" % half)
            for k in range(2):
                pairs = blocks[k][:].bitcast(F32)
                for u in range(2):
                    nc.tensor.transpose(acc[:, block(2 * k + u)], pairs[:, block(u)], ident[:])
            return acc

        def copy_g1(half, acc):
            nc.scalar.copy(g[0][half][:].bitcast(F32).rearrange("s (k i u) -> s k i u", k=2, u=2),
                           acc[:].rearrange("s (k u i) -> s k i u", k=2, u=2))

        copy_g1(0, turn_back_g1(0, scale_g1(0)))

        def weave_g2(half):
            nc.vector.tensor_tensor(
                g[1][half][:].rearrange("p (c i t) -> p c t i", i=2, t=PACK),
                h2[:, :, half_cols(half)].rearrange("p t (c i) -> p c t i", i=2),
                factor[:, :, half_cols(half)].rearrange("p t (c i) -> p c t i", i=2),
                ALU.mult,
            )

        recip(1, 0, 2)
        diff(0, slice(0, S))
        recip(1, 2, PACK)
        for t in range(1, PACK - 1):
            diff(t, slice(0, S))
        for half in range(2):
            diff(PACK - 1, half_cols(half))
        weave_g2(0)
        quantise_g(0, 0)
        quantise_g(1, 0, "g00")

        out_view = out.rearrange("(p j) n -> j p n", j=PACK)

        def multiply(j, half, acc):
            order = heads if j < 2 else heads[::-1]
            for h in order:
                mm(acc, qx_r[j // 2], h * HALF + j % 2 * P, qg[h][half], half_cols(0), E5M2, h == order[0], h == order[1])

        def drain(name, acc, width, copy, tag=None):
            dw = sbuf([P, width], F32, name, tag)
            copy(dw[:], acc[:, 0:width])
            return dw

        def scatter_half(j, half, src):
            nc.scalar.activation(windows[j][:].indirect(entries(half)), src, ACT.Copy)

        def store(j):
            nc.sync.dma_start(out_view[j], windows[j][:])

        early = bank(0, "early")
        multiply(0, 0, early[:, half_cols(0)])
        copy_g1(1, turn_back_g1(1, scale_g1(1)))
        second_tile = bank(1, "second_tile")
        multiply(1, 0, second_tile[:, half_cols(0)])
        last_first = bank(4, "last_first")
        for j in range(2, PACK):
            multiply(j, 0, last_first[:, half_cols(j - 2)])
        scatter_half(0, 0, drain("dw00", early, HALF, nc.scalar.copy, "g_t0")[:])
        g[1][1] = sbuf([P, HALF * PACK], BF16, "g11", "g10")
        weave_g2(1)
        quantise_g(0, 1)
        quantise_g(1, 1, "g01")
        late = [bank(b, "late%d" % b) for b in (5, 6)]
        for j in range(2):
            multiply(j, 1, late[j][:, half_cols(0)])
        last_second = bank(7, "last_second")
        for j in range(2, PACK):
            multiply(j, 1, last_second[:, half_cols(j - 2)])

        def finish(j, src):
            nc.vector.tensor_copy(windows[j][:].indirect(entries(1)), src)
            store(j)

        dw10 = drain("dw10", second_tile, HALF, nc.vector.tensor_copy, "g10")
        dw_late = [drain("dw%d1" % j, late[j], HALF, nc.vector.tensor_copy) for j in range(2)]
        finish(0, dw_late[0][:])
        scatter_half(1, 0, dw10[:])
        finish(1, dw_late[1][:])
        dw_first = drain("dw_first", last_first, S, nc.scalar.copy, "g10")
        dw_second = drain("dw_second", last_second, S, nc.vector.tensor_copy, "dw11")
        for j in range(2, PACK):
            scatter_half(j, 0, dw_first[:, half_cols(j - 2)])
            finish(j, dw_second[:, half_cols(j - 2)])
